import numpy as np
import ml_dtypes


def mxq(x, axis, fmt="e4m3"):
    dtype, down = {"e4m3": (ml_dtypes.float8_e4m3fn, 7), "e5m2": (ml_dtypes.float8_e5m2, 14)}[fmt]
    v = np.moveaxis(np.asarray(x, np.float32).astype(ml_dtypes.bfloat16).astype(np.float64), axis, -1)
    blocks = v.reshape(v.shape[:-1] + (-1, 32))
    amax = np.abs(blocks).max(-1, keepdims=True)
    byte = np.maximum(np.where(amax > 0, np.frexp(amax)[1] - 1 + 127, 0) - down, 1)
    scale = np.exp2(byte - 127.0)
    codes = (blocks / scale).astype(np.float32).astype(dtype).astype(np.float64)
    return np.moveaxis((codes * scale).reshape(v.shape), -1, axis)


WIDE = False


def mx_kscale(k):
    if not WIDE:
        return np.ones(k)
    levels = np.array([18, -18])
    if k % 512:
        return np.exp2(np.random.permutation(np.resize(levels, k // 32))).repeat(32)
    a = np.empty((k // 512, 16))
    for p in range(k // 512):
        a[p, :8] = np.random.permutation(np.resize(levels, 8))
        for g in range(8):
            far = levels[np.abs(levels - a[p, g]) >= 10]
            a[p, g + 8] = far[np.random.randint(len(far))]
    return np.exp2(a.ravel()).repeat(32)


def f64(x):
    return np.asarray(x).astype(np.float64)


def striped(idx):
    return np.tile(np.asarray(idx).reshape(-1, 16).T, (8, 1)).astype(np.uint16)


def unstriped(offs):
    return offs[:16].T.reshape(-1).astype(np.int64)


B, N, T, D, R = 1, 512, 2048, 512, 1024
CLIP = 277.0


def setup_inputs():
    n = np.random.standard_normal
    idx = np.random.permutation(T)[:B * N]
    s = mx_kscale(D)[:, None]
    z = mx_kscale(R)[:, None]
    x = n((B, D, R))
    return {
        "xT": (x * s).astype(np.float32),
        "wT": (n((D, T)) * (1.00 / np.sqrt(D)) / s).astype(np.float32),
        "y": np.random.randint(0, 2, (B, R, N)).astype(np.float32),
        "wt": (np.random.uniform(0.5, 1.5, (B, R, 1)) * 1.0 / np.sqrt(R) * z).astype(np.float32),
        "xn": np.square(x).sum(1)[:, :, None].astype(np.float32),
        "xm": (x.transpose(0, 2, 1) / z).astype(np.float32),
        "offs": striped(idx),
    }


def reference(xT, wT, y, wt, xn, xm, offs):
    idx = unstriped(offs)
    pick = lambda x: x[:, idx].reshape(x.shape[0], B, N).transpose(1, 0, 2)
    a = mxq(f64(xT), 1, "e4m3").transpose(0, 2, 1) @ mxq(pick(f64(wT)), 1, "e4m3")
    g = (1.0 / (1.0 + np.exp(-a)) - f64(y))
    g = f64(wt) * np.minimum(1.0, CLIP / np.sqrt(f64(xn) * np.square(g).sum(-1, keepdims=True))) * g
    dw = mxq(f64(xm), 1, "e4m3").transpose(0, 2, 1) @ mxq(g, 1, "e5m2")
    gw = np.zeros((D, T))
    gw[:, idx] = dw.transpose(1, 0, 2).reshape(D, B * N)
    return gw

@@ -1,0 +1,190 @@
+from contextlib import ExitStack
+
+import concourse.mybir as mybir
+
+N, T, D, R = 512, 2048, 512, 1024
+CLIP = 277.0
+FLOPS = 2 * 2 * R * D * N
+
+F32 = mybir.dt.float32
+BF16 = mybir.dt.bfloat16
+U32 = mybir.dt.uint32
+U16 = mybir.dt.uint16
+U8 = mybir.dt.uint8
+E4M3 = mybir.dt.float8_e4m3fn_x4
+E5M2 = mybir.dt.float8_e5m2_x4
+ALU = mybir.AluOpType
+ACT = mybir.ActivationFunctionType
+
+P = 128
+PACK = 4
+PASS = P * PACK
+PASSES = R // PASS
+RUN = 4
+
+
+def tile_attend_gnce_w_clip_kernel(tc, xT, wT, y, wt, xn, xm, offs, out):
+    nc = tc.nc
+    with ExitStack() as ctx:
+        keep = ctx.enter_context(tc.tile_pool(name="keep", bufs=1))
+        psum = ctx.enter_context(tc.psum_pool(name="psum", bufs=1))
+
+        offsets = keep.tile([P, N // 16], U16, name="offsets")
+        nc.sync.dma_start(offsets[:], offs)
+
+        xT_planes = xT[0].rearrange("(p j) r -> p j r", j=PACK)
+        wT_planes = wT.rearrange("(p j) c -> p j c", j=PACK)
+        y_rows = y[0].rearrange("(g p t) n -> g p t n", p=P, t=PACK)
+        xm_rows = xm[0].rearrange("(g p t) d -> g p t d", p=P, t=PACK)
+
+        x_raw = [keep.tile([P, PACK, PASS], F32, name=f"x_raw{g}") for g in range(PASSES)]
+        w_raw = [keep.tile([P, T], F32, name=f"w_raw{j}") for j in range(PACK)]
+        y_raw = [keep.tile([P, PACK, N], F32, name=f"y_raw{g}") for g in range(PASSES)]
+        xm_raw = [keep.tile([P, PACK, D], F32, name=f"xm_raw{g}") for g in range(PASSES)]
+        weight = keep.tile([P, PASSES, PACK], F32, name="weight")
+        sq_len = keep.tile([P, PASSES, PACK], F32, name="sq_len")
+
+        for j in range(PACK):
+            nc.sync.dma_start(out=w_raw[j][:], in_=wT_planes[:, j, :])
+        for g in range(PASSES):
+            nc.sync.dma_start(out=x_raw[g][:], in_=xT_planes[:, :, g * PASS : (g + 1) * PASS])
+            for h in range(2):
+                nc.sync.dma_start(out=y_raw[g][:, 2 * h : 2 * h + 2, :], in_=y_rows[g][:, 2 * h : 2 * h + 2, :])
+        for g in range(PASSES):
+            nc.sync.dma_start(out=xm_raw[g][:], in_=xm_rows[g])
+        nc.scalar.dma_start(out=sq_len[:], in_=xn[0].rearrange("(g p t) o -> p g (t o)", p=P, t=PACK))
+        nc.scalar.dma_start(out=weight[:], in_=wt[0].rearrange("(g p t) o -> p g (t o)", p=P, t=PACK))
+
+        minus_half = keep.tile([P, PASSES * PACK], F32, name="minus_half")
+        plus_half = keep.tile([P, PASSES * PACK], F32, name="plus_half")
+        nc.gpsimd.memset(minus_half[:], -0.5)
+        nc.gpsimd.memset(plus_half[:], 0.5)
+        warm = keep.tile([P, 1], F32, name="warm")
+        nc.scalar.activation(warm[:], plus_half[:, 0:1], ACT.Sigmoid)
+
+        wide = [keep.tile([P, T], F32, name=f"wide{j}") for j in range(D // P)]
+        for j in range(D // P):
+            (nc.vector if j < 2 else nc.gpsimd).memset(wide[j][:], 0.0)
+
+        rel_sq = keep.tile([P, PASSES * PACK], F32, name="rel_sq")
+        rel_len = keep.tile([P, PASSES * PACK], F32, name="rel_len")
+        nc.gpsimd.tensor_scalar(rel_sq[:], sq_len[:].rearrange("p g t -> p (g t)"), 1.0 / (CLIP * CLIP), 0.0, ALU.mult, ALU.add)
+        nc.gpsimd.tensor_tensor(rel_len[:], rel_sq[:], plus_half[:], ALU.pow)
+
+        x_bf = [[keep.tile([P, 2, P, PACK], BF16, name=f"x_bf{g}{h}", align_bytes=64) for h in range(2)] for g in range(PASSES)]
+        x_codes = [[keep.tile([P, 2 * P], U32, name=f"x_codes{g}{h}", align_bytes=64) for h in range(2)] for g in range(PASSES)]
+        x_scales = [[keep.tile([P, 2 * P], U8, name=f"x_scales{g}{h}", align_bytes=64) for h in range(2)] for g in range(PASSES)]
+
+        def prepare_x(g):
+            for h in range(2):
+                copy = nc.vector.tensor_copy if h == 0 else nc.scalar.copy
+                copy(
+                    out=x_bf[g][h][:].rearrange("p t m j -> p m j t"),
+                    in_=x_raw[g][:].rearrange("p j (m t) -> p m j t", t=PACK)[:, :, :, 2 * h : 2 * h + 2],
+                )
+            for h in range(2):
+                nc.vector.quantize_mx(
+                    out=x_codes[g][h][:].bitcast(E4M3), scales=x_scales[g][h][:],
+                    in_=x_bf[g][h][:].rearrange("p t m j -> p (t m j)"),
+                )
+
+        w_bf = keep.tile([P, N, PACK], BF16, name="w_bf", align_bytes=64)
+        w_codes = keep.tile([P, N], U32, name="w_codes", align_bytes=64)
+        w_scales = keep.tile([P, N], U8, name="w_scales", align_bytes=64)
+        for j in range(PACK):
+            nc.vector.tensor_copy(out=w_bf[:, :, j], in_=w_raw[j][:].indirect(offsets[:]))
+        nc.vector.quantize_mx(out=w_codes[:].bitcast(E4M3), scales=w_scales[:], in_=w_bf[:].rearrange("p n j -> p (n j)"))
+
+        prob = [keep.tile([P, N], F32, name=f"prob{u}") for u in range(PASSES * PACK)]
+        q = [keep.tile([P, PACK, N], F32, name=f"q{g}") for g in range(PASSES)]
+        squares = [keep.tile([P, N], BF16, name=f"squares{h}") for h in range(2)]
+        ratio_sq = [keep.tile([P, PACK], F32, name=f"ratio_sq{g}") for g in range(PASSES)]
+        floored = [keep.tile([P, PACK], F32, name=f"floored{g}") for g in range(PASSES)]
+        cut = [keep.tile([P, PACK], F32, name=f"cut{g}") for g in range(PASSES)]
+        factor = [keep.tile([P, PACK], F32, name=f"factor{g}") for g in range(PASSES)]
+        g_bf = [keep.tile([P, N, PACK], BF16, name=f"g_bf{g}", align_bytes=64) for g in range(PASSES)]
+        g_codes = [keep.tile([P, N], U32, name=f"g_codes{g}", align_bytes=64) for g in range(PASSES)]
+        g_scales = [keep.tile([P, N], U8, name=f"g_scales{g}", align_bytes=64) for g in range(PASSES)]
+
+        def scores(g, t):
+            u = g * PACK + t
+            a = psum.tile([P, N], F32, name=f"bank{u}")
+            cols = slice(t % 2 * P, (t % 2 + 1) * P)
+            nc.tensor.matmul_mx(
+                out=a[:], lhsT=x_codes[g][t // 2][:, cols].bitcast(E4M3), lhsT_scale=x_scales[g][t // 2][:, cols],
+                rhs=w_codes[:].bitcast(E4M3), rhs_scale=w_scales[:], start=True, stop=True,
+            )
+            nc.scalar.activation(prob[u][:], a[:], ACT.Sigmoid)
+
+        def residual(g, t):
+            u = g * PACK + t
+            nc.vector.tensor_tensor(q[g][:, t, :], prob[u][:], y_raw[g][:, t, :], ALU.subtract)
+            nc.scalar.activation(
+                squares[t % 2][:], q[g][:, t, :], ACT.Square, scale=rel_len[:, u : u + 1], accum_out=ratio_sq[g][:, t : t + 1]
+            )
+
+        def row_cut(g, t0, t1):
+            nc.gpsimd.tensor_scalar(floored[g][:, t0:t1], ratio_sq[g][:, t0:t1], 1.0, 1.0, ALU.mult, ALU.max)
+            nc.gpsimd.tensor_tensor(cut[g][:, t0:t1], floored[g][:, t0:t1], minus_half[:, t0:t1], ALU.pow)
+
+        def gradient(g, t1):
+            nc.gpsimd.tensor_tensor(factor[g][:, 0:t1], cut[g][:, 0:t1], weight[:, g, 0:t1], ALU.mult)
+            nc.vector.tensor_tensor(
+                g_bf[g][:, :, 0:t1].rearrange("p (c i) t -> p c t i", i=RUN),
+                q[g][:, 0:t1, :].rearrange("p t (c i) -> p c t i", i=RUN),
+                factor[g][:, 0:t1].unsqueeze(1).unsqueeze(3).to_broadcast([P, N // RUN, t1, RUN]),
+                ALU.mult,
+            )
+
+        def quantize_g(g):
+            nc.vector.quantize_mx(
+                out=g_codes[g][:].bitcast(E5M2), scales=g_scales[g][:], in_=g_bf[g][:].rearrange("p n t -> p (n t)")
+            )
+
+        prepare_x(0)
+        for t in range(PACK):
+            scores(0, t)
+            residual(0, t)
+        row_cut(0, 0, PACK)
+        prepare_x(1)
+        for t in range(PACK - 1):
+            scores(1, t)
+            residual(1, t)
+        row_cut(1, 0, PACK - 1)
+        t = PACK - 1
+        scores(1, t)
+        residual(1, t)
+        row_cut(1, t, PACK)
+        gradient(0, PACK)
+        quantize_g(0)
+        gradient(1, t)
+        nc.vector.tensor_scalar(
+            g_bf[1][:, :, t], q[1][:, t, :], cut[1][:, t : t + 1], weight[:, 1, t : t + 1], ALU.mult, ALU.mult
+        )
+        quantize_g(1)
+
+        xm_bf = [keep.tile([P, PASSES, P, PACK], BF16, name=f"xm_bf{j}", align_bytes=64) for j in range(D // P)]
+        xm_codes = [keep.tile([P, PASSES, P], U32, name=f"xm_codes{j}", align_bytes=64) for j in range(D // P)]
+        xm_scales = [keep.tile([P, PASSES, P], U8, name=f"xm_scales{j}", align_bytes=64) for j in range(D // P)]
+        dense = [keep.tile([P, N], F32, name=f"dense{j}") for j in range(D // P)]
+        for j in range(D // P):
+            feats = slice(j * P, (j + 1) * P)
+            for g in range(PASSES):
+                nc.scalar.copy(
+                    out=xm_bf[j][:, g, :, :].rearrange("p (c i) t -> p c t i", i=RUN),
+                    in_=xm_raw[g][:, :, feats].rearrange("p t (c i) -> p c t i", i=RUN),
+                )
+            nc.vector.quantize_mx(
+                out=xm_codes[j][:].rearrange("p g d -> p (g d)").bitcast(E4M3),
+                scales=xm_scales[j][:].rearrange("p g d -> p (g d)"),
+                in_=xm_bf[j][:].rearrange("p g d t -> p (g d t)"),
+            )
+            dw = psum.tile([P, N], F32, name=f"bank{j}")
+            for g in range(PASSES):
+                nc.tensor.matmul_mx(
+                    out=dw[:], lhsT=xm_codes[j][:, g, :].bitcast(E4M3), lhsT_scale=xm_scales[j][:, g, :],
+                    rhs=g_codes[g][:].bitcast(E5M2), rhs_scale=g_scales[g][:], start=(g == 0), stop=(g == PASSES - 1),
+                )
+            nc.scalar.copy(out=dense[j][:], in_=dw[:])
+            nc.vector.tensor_copy(out=wide[j][:].indirect(offsets[:]), in_=dense[j][:])
+            nc.sync.dma_start(out=out[feats, :], in_=wide[j][:])

@@ -21,6 +21,8 @@ PACK = 4
 PASS = P * PACK
 PASSES = R // PASS
 RUN = 4
+ON_VECTOR = 3
+TINY = 2.0**-60
 
 
 def tile_attend_gnce_w_clip_kernel(tc, xT, wT, y, wt, xn, xm, offs, out):
@@ -48,6 +50,7 @@ def tile_attend_gnce_w_clip_kernel(tc, xT, wT, y, wt, xn, xm, offs, out):
             nc.sync.dma_start(out=w_raw[j][:], in_=wT_planes[:, j, :])
         for g in range(PASSES):
             nc.sync.dma_start(out=x_raw[g][:], in_=xT_planes[:, :, g * PASS : (g + 1) * PASS])
+        for g in range(PASSES):
             for h in range(2):
                 nc.sync.dma_start(out=y_raw[g][:, 2 * h : 2 * h + 2, :], in_=y_rows[g][:, 2 * h : 2 * h + 2, :])
         for g in range(PASSES):
@@ -55,84 +58,112 @@ def tile_attend_gnce_w_clip_kernel(tc, xT, wT, y, wt, xn, xm, offs, out):
         nc.scalar.dma_start(out=sq_len[:], in_=xn[0].rearrange("(g p t) o -> p g (t o)", p=P, t=PACK))
         nc.scalar.dma_start(out=weight[:], in_=wt[0].rearrange("(g p t) o -> p g (t o)", p=P, t=PACK))
 
-        minus_half = keep.tile([P, PASSES * PACK], F32, name="minus_half")
-        plus_half = keep.tile([P, PASSES * PACK], F32, name="plus_half")
-        nc.gpsimd.memset(minus_half[:], -0.5)
-        nc.gpsimd.memset(plus_half[:], 0.5)
+        zero = keep.tile([P, 1], F32, name="zero", tag="column")
+        tiny = keep.tile([P, 1], F32, name="tiny")
+        nc.gpsimd.memset(zero[:], 0.0)
+        nc.gpsimd.memset(tiny[:], TINY)
         warm = keep.tile([P, 1], F32, name="warm")
-        nc.scalar.activation(warm[:], plus_half[:, 0:1], ACT.Sigmoid)
+        nc.scalar.activation(warm[:], tiny[:], ACT.Sigmoid)
 
-        wide = [keep.tile([P, T], F32, name=f"wide{j}") for j in range(D // P)]
-        for j in range(D // P):
-            (nc.vector if j < 2 else nc.gpsimd).memset(wide[j][:], 0.0)
+        wide = [keep.tile([P, T], F32, name=f"wide{j}") for j in range(2)]
+        for j in range(2):
+            nc.vector.memset(wide[j][:], 0.0)
 
-        rel_sq = keep.tile([P, PASSES * PACK], F32, name="rel_sq")
-        rel_len = keep.tile([P, PASSES * PACK], F32, name="rel_len")
-        nc.gpsimd.tensor_scalar(rel_sq[:], sq_len[:].rearrange("p g t -> p (g t)"), 1.0 / (CLIP * CLIP), 0.0, ALU.mult, ALU.add)
-        nc.gpsimd.tensor_tensor(rel_len[:], rel_sq[:], plus_half[:], ALU.pow)
+        rel_sq = keep.tile([P, PASSES, PACK], F32, name="rel_sq")
+        nc.gpsimd.tensor_scalar(rel_sq[:], sq_len[:], 1.0 / (CLIP * CLIP), 0.0, ALU.mult, ALU.add)
 
-        x_bf = [[keep.tile([P, 2, P, PACK], BF16, name=f"x_bf{g}{h}", align_bytes=64) for h in range(2)] for g in range(PASSES)]
-        x_codes = [[keep.tile([P, 2 * P], U32, name=f"x_codes{g}{h}", align_bytes=64) for h in range(2)] for g in range(PASSES)]
-        x_scales = [[keep.tile([P, 2 * P], U8, name=f"x_scales{g}{h}", align_bytes=64) for h in range(2)] for g in range(PASSES)]
-
-        def prepare_x(g):
-            for h in range(2):
-                copy = nc.vector.tensor_copy if h == 0 else nc.scalar.copy
-                copy(
-                    out=x_bf[g][h][:].rearrange("p t m j -> p m j t"),
-                    in_=x_raw[g][:].rearrange("p j (m t) -> p m j t", t=PACK)[:, :, :, 2 * h : 2 * h + 2],
-                )
-            for h in range(2):
-                nc.vector.quantize_mx(
-                    out=x_codes[g][h][:].bitcast(E4M3), scales=x_scales[g][h][:],
-                    in_=x_bf[g][h][:].rearrange("p t m j -> p (t m j)"),
-                )
-
-        w_bf = keep.tile([P, N, PACK], BF16, name="w_bf", align_bytes=64)
+        w_bf = keep.tile([P, N, PACK], BF16, name="w_bf", tag="stage", align_bytes=64)
         w_codes = keep.tile([P, N], U32, name="w_codes", align_bytes=64)
         w_scales = keep.tile([P, N], U8, name="w_scales", align_bytes=64)
         for j in range(PACK):
             nc.vector.tensor_copy(out=w_bf[:, :, j], in_=w_raw[j][:].indirect(offsets[:]))
         nc.vector.quantize_mx(out=w_codes[:].bitcast(E4M3), scales=w_scales[:], in_=w_bf[:].rearrange("p n j -> p (n j)"))
 
-        prob = [keep.tile([P, N], F32, name=f"prob{u}") for u in range(PASSES * PACK)]
+        x_codes = [keep.tile([P, PASS], U32, name=f"x_codes{g}", align_bytes=64) for g in range(PASSES)]
+        x_scales = [keep.tile([P, PASS], U8, name=f"x_scales{g}", align_bytes=64) for g in range(PASSES)]
+
+        def group_x(copy, dst, g, t0, t1):
+            copy(
+                out=dst[:].rearrange("p t m j -> p m j t"),
+                in_=x_raw[g][:].rearrange("p j (m t) -> p m j t", t=PACK)[:, :, :, t0:t1],
+            )
+
+        def quantize_x(src, g, t0, t1):
+            cols = slice(t0 * P, t1 * P)
+            nc.vector.quantize_mx(
+                out=x_codes[g][:, cols].bitcast(E4M3), scales=x_scales[g][:, cols],
+                in_=src[:].rearrange("p t m j -> p (t m j)"),
+            )
+
+        x_lo = keep.tile([P, 2, P, PACK], BF16, name="x_lo", align_bytes=64)
+        x_hi = keep.tile([P, 2, P, PACK], BF16, name="x_hi", tag="stage", align_bytes=64)
+        group_x(nc.scalar.copy, x_lo, 0, 0, 2)
+        group_x(nc.vector.tensor_copy, x_hi, 0, 2, 4)
+        quantize_x(x_lo, 0, 0, 2)
+        quantize_x(x_hi, 0, 2, 4)
+        x_second = keep.tile([P, PACK, P, PACK], BF16, name="x_second", tag="stage", align_bytes=64)
+        group_x(nc.vector.tensor_copy, x_second, 1, 0, 4)
+        quantize_x(x_second, 1, 0, 4)
+
+        TILES = PASSES * PACK
+        prob = [keep.tile([P, N], F32, name=f"prob{u}") for u in range(TILES)]
         q = [keep.tile([P, PACK, N], F32, name=f"q{g}") for g in range(PASSES)]
-        squares = [keep.tile([P, N], BF16, name=f"squares{h}") for h in range(2)]
-        ratio_sq = [keep.tile([P, PACK], F32, name=f"ratio_sq{g}") for g in range(PASSES)]
-        floored = [keep.tile([P, PACK], F32, name=f"floored{g}") for g in range(PASSES)]
-        cut = [keep.tile([P, PACK], F32, name=f"cut{g}") for g in range(PASSES)]
+        squares_v = [keep.tile([P, N], BF16, name=f"squares_v{h}") for h in range(2)]
+        squares_s = [keep.tile([P, N], BF16, name=f"squares_s{h}") for h in range(2)]
+        sum_sq = keep.tile([P, TILES], F32, name="sum_sq")
         factor = [keep.tile([P, PACK], F32, name=f"factor{g}") for g in range(PASSES)]
         g_bf = [keep.tile([P, N, PACK], BF16, name=f"g_bf{g}", align_bytes=64) for g in range(PASSES)]
         g_codes = [keep.tile([P, N], U32, name=f"g_codes{g}", align_bytes=64) for g in range(PASSES)]
         g_scales = [keep.tile([P, N], U8, name=f"g_scales{g}", align_bytes=64) for g in range(PASSES)]
+        xm_bf = keep.tile([P, D // P, PASSES, P, PACK], BF16, name="xm_bf", align_bytes=64)
 
-        def scores(g, t):
-            u = g * PACK + t
+        for u in range(TILES):
+            g, t = divmod(u, PACK)
             a = psum.tile([P, N], F32, name=f"bank{u}")
-            cols = slice(t % 2 * P, (t % 2 + 1) * P)
+            cols = slice(t * P, (t + 1) * P)
             nc.tensor.matmul_mx(
-                out=a[:], lhsT=x_codes[g][t // 2][:, cols].bitcast(E4M3), lhsT_scale=x_scales[g][t // 2][:, cols],
+                out=a[:], lhsT=x_codes[g][:, cols].bitcast(E4M3), lhsT_scale=x_scales[g][:, cols],
                 rhs=w_codes[:].bitcast(E4M3), rhs_scale=w_scales[:], start=True, stop=True,
             )
-            nc.scalar.activation(prob[u][:], a[:], ACT.Sigmoid)
+            nc.scalar.activation(prob[u][:], a[:], ACT.Sigmoid, bias=zero[:])
 
-        def residual(g, t):
-            u = g * PACK + t
+        ratio = keep.tile([P, TILES], F32, name="ratio", tag="column")
+
+        def residual(u):
+            g, t = divmod(u, PACK)
             nc.vector.tensor_tensor(q[g][:, t, :], prob[u][:], y_raw[g][:, t, :], ALU.subtract)
-            nc.scalar.activation(
-                squares[t % 2][:], q[g][:, t, :], ACT.Square, scale=rel_len[:, u : u + 1], accum_out=ratio_sq[g][:, t : t + 1]
+
+        def square_on_vector(u):
+            g, t = divmod(u, PACK)
+            nc.vector.scalar_tensor_tensor(
+                squares_v[u % 2][:], q[g][:, t, :], 1.0, q[g][:, t, :], ALU.mult, ALU.mult, accum_out=sum_sq[:, u : u + 1]
             )
 
-        def row_cut(g, t0, t1):
-            nc.gpsimd.tensor_scalar(floored[g][:, t0:t1], ratio_sq[g][:, t0:t1], 1.0, 1.0, ALU.mult, ALU.max)
-            nc.gpsimd.tensor_tensor(cut[g][:, t0:t1], floored[g][:, t0:t1], minus_half[:, t0:t1], ALU.pow)
+        def square_on_scalar(u):
+            g, t = divmod(u, PACK)
+            if u == TILES - 1:
+                dst = xm_bf[:].rearrange("p j g d t -> p (j g) (d t)")[:, :, 0 : N // TILES]
+                src = q[g][:, t, :].rearrange("p (a b) -> p a b", a=TILES)
+            else:
+                dst, src = squares_s[u % 2][:], q[g][:, t, :]
+            nc.scalar.activation(dst, src, ACT.Square, accum_out=sum_sq[:, u : u + 1])
 
-        def gradient(g, t1):
-            nc.gpsimd.tensor_tensor(factor[g][:, 0:t1], cut[g][:, 0:t1], weight[:, g, 0:t1], ALU.mult)
+        def row_ratio(u):
+            g, t = divmod(u, PACK)
+            nc.scalar.activation(
+                ratio[:, u : u + 1], sum_sq[:, u : u + 1], ACT.Abs_reciprocal_sqrt, bias=tiny[:], scale=rel_sq[:, g, t : t + 1]
+            )
+
+        def row_factor(g):
+            nc.vector.scalar_tensor_tensor(
+                factor[g][:], ratio[:, g * PACK : (g + 1) * PACK], 1.0, weight[:, g, :], ALU.min, ALU.mult
+            )
+
+        def gradient(g):
             nc.vector.tensor_tensor(
-                g_bf[g][:, :, 0:t1].rearrange("p (c i) t -> p c t i", i=RUN),
-                q[g][:, 0:t1, :].rearrange("p t (c i) -> p c t i", i=RUN),
-                factor[g][:, 0:t1].unsqueeze(1).unsqueeze(3).to_broadcast([P, N // RUN, t1, RUN]),
+                g_bf[g][:].rearrange("p (c i) t -> p c t i", i=RUN),
+                q[g][:].rearrange("p t (c i) -> p c t i", i=RUN),
+                factor[g][:].unsqueeze(1).unsqueeze(3).to_broadcast([P, N // RUN, PACK, RUN]),
                 ALU.mult,
             )
 
@@ -141,29 +172,29 @@ def tile_attend_gnce_w_clip_kernel(tc, xT, wT, y, wt, xn, xm, offs, out):
                 out=g_codes[g][:].bitcast(E5M2), scales=g_scales[g][:], in_=g_bf[g][:].rearrange("p n t -> p (n t)")
             )
 
-        prepare_x(0)
-        for t in range(PACK):
-            scores(0, t)
-            residual(0, t)
-        row_cut(0, 0, PACK)
-        prepare_x(1)
-        for t in range(PACK - 1):
-            scores(1, t)
-            residual(1, t)
-        row_cut(1, 0, PACK - 1)
-        t = PACK - 1
-        scores(1, t)
-        residual(1, t)
-        row_cut(1, t, PACK)
-        gradient(0, PACK)
+        residual(0)
+        residual(1)
+        for u in range(ON_VECTOR):
+            residual(u + 2)
+            square_on_vector(u)
+            row_ratio(u)
+        for u in range(ON_VECTOR + 2, TILES):
+            residual(u)
+        for g in range(PASSES):
+            late = keep.tile([P, T], F32, name=f"wide{2 + g}", tag=f"y_raw{g}")
+            nc.gpsimd.memset(late[:], 0.0)
+            wide.append(late)
+        for u in range(ON_VECTOR, TILES):
+            square_on_scalar(u)
+            if u > ON_VECTOR:
+                row_ratio(u - 1)
+        row_ratio(TILES - 1)
+        row_factor(0)
+        gradient(0)
+        row_factor(1)
         quantize_g(0)
-        gradient(1, t)
-        nc.vector.tensor_scalar(
-            g_bf[1][:, :, t], q[1][:, t, :], cut[1][:, t : t + 1], weight[:, 1, t : t + 1], ALU.mult, ALU.mult
-        )
-        quantize_g(1)
+        gradient(1)
 
-        xm_bf = [keep.tile([P, PASSES, P, PACK], BF16, name=f"xm_bf{j}", align_bytes=64) for j in range(D // P)]
         xm_codes = [keep.tile([P, PASSES, P], U32, name=f"xm_codes{j}", align_bytes=64) for j in range(D // P)]
         xm_scales = [keep.tile([P, PASSES, P], U8, name=f"xm_scales{j}", align_bytes=64) for j in range(D // P)]
         dense = [keep.tile([P, N], F32, name=f"dense{j}") for j in range(D // P)]
@@ -171,14 +202,18 @@ def tile_attend_gnce_w_clip_kernel(tc, xT, wT, y, wt, xn, xm, offs, out):
             feats = slice(j * P, (j + 1) * P)
             for g in range(PASSES):
                 nc.scalar.copy(
-                    out=xm_bf[j][:, g, :, :].rearrange("p (c i) t -> p c t i", i=RUN),
+                    out=xm_bf[:, j, g, :, :].rearrange("p (c i) t -> p c t i", i=RUN),
                     in_=xm_raw[g][:, :, feats].rearrange("p t (c i) -> p c t i", i=RUN),
                 )
             nc.vector.quantize_mx(
                 out=xm_codes[j][:].rearrange("p g d -> p (g d)").bitcast(E4M3),
                 scales=xm_scales[j][:].rearrange("p g d -> p (g d)"),
-                in_=xm_bf[j][:].rearrange("p g d t -> p (g d t)"),
+                in_=xm_bf[:, j, :, :, :].rearrange("p g d t -> p (g d t)"),
             )
+            if j == 0:
+                quantize_g(1)
+        for j in range(D // P):
+            feats = slice(j * P, (j + 1) * P)
             dw = psum.tile([P, N], F32, name=f"bank{j}")
             for g in range(PASSES):
                 nc.tensor.matmul_mx(

@@ -22,6 +22,7 @@ PASS = P * PACK
 PASSES = R // PASS
 RUN = 4
 ON_VECTOR = 3
+ON_SCALAR = 128
 TINY = 2.0**-60
 
 
@@ -32,7 +33,6 @@ def tile_attend_gnce_w_clip_kernel(tc, xT, wT, y, wt, xn, xm, offs, out):
         psum = ctx.enter_context(tc.psum_pool(name="psum", bufs=1))
 
         offsets = keep.tile([P, N // 16], U16, name="offsets")
-        nc.sync.dma_start(offsets[:], offs)
 
         xT_planes = xT[0].rearrange("(p j) r -> p j r", j=PACK)
         wT_planes = wT.rearrange("(p j) c -> p j c", j=PACK)
@@ -48,15 +48,17 @@ def tile_attend_gnce_w_clip_kernel(tc, xT, wT, y, wt, xn, xm, offs, out):
 
         for j in range(PACK):
             nc.sync.dma_start(out=w_raw[j][:], in_=wT_planes[:, j, :])
+            if j == 0:
+                nc.sync.dma_start(offsets[:], offs)
         for g in range(PASSES):
             nc.sync.dma_start(out=x_raw[g][:], in_=xT_planes[:, :, g * PASS : (g + 1) * PASS])
+        nc.sync.dma_start(out=sq_len[:], in_=xn[0].rearrange("(g p t) o -> p g (t o)", p=P, t=PACK))
+        nc.sync.dma_start(out=weight[:], in_=wt[0].rearrange("(g p t) o -> p g (t o)", p=P, t=PACK))
         for g in range(PASSES):
             for h in range(2):
                 nc.sync.dma_start(out=y_raw[g][:, 2 * h : 2 * h + 2, :], in_=y_rows[g][:, 2 * h : 2 * h + 2, :])
         for g in range(PASSES):
             nc.sync.dma_start(out=xm_raw[g][:], in_=xm_rows[g])
-        nc.scalar.dma_start(out=sq_len[:], in_=xn[0].rearrange("(g p t) o -> p g (t o)", p=P, t=PACK))
-        nc.scalar.dma_start(out=weight[:], in_=wt[0].rearrange("(g p t) o -> p g (t o)", p=P, t=PACK))
 
         zero = keep.tile([P, 1], F32, name="zero", tag="column")
         tiny = keep.tile([P, 1], F32, name="tiny")
@@ -65,9 +67,9 @@ def tile_attend_gnce_w_clip_kernel(tc, xT, wT, y, wt, xn, xm, offs, out):
         warm = keep.tile([P, 1], F32, name="warm")
         nc.scalar.activation(warm[:], tiny[:], ACT.Sigmoid)
 
-        wide = [keep.tile([P, T], F32, name=f"wide{j}") for j in range(2)]
-        for j in range(2):
-            nc.vector.memset(wide[j][:], 0.0)
+        wide = [keep.tile([P, T], F32, name=f"wide{j}") for j in range(D // P)]
+        for j in range(D // P):
+            (nc.vector if j < 2 else nc.gpsimd).memset(wide[j][:], 0.0)
 
         rel_sq = keep.tile([P, PASSES, PACK], F32, name="rel_sq")
         nc.gpsimd.tensor_scalar(rel_sq[:], sq_len[:], 1.0 / (CLIP * CLIP), 0.0, ALU.mult, ALU.add)
@@ -101,13 +103,16 @@ def tile_attend_gnce_w_clip_kernel(tc, xT, wT, y, wt, xn, xm, offs, out):
         group_x(nc.vector.tensor_copy, x_hi, 0, 2, 4)
         quantize_x(x_lo, 0, 0, 2)
         quantize_x(x_hi, 0, 2, 4)
-        x_second = keep.tile([P, PACK, P, PACK], BF16, name="x_second", tag="stage", align_bytes=64)
-        group_x(nc.vector.tensor_copy, x_second, 1, 0, 4)
-        quantize_x(x_second, 1, 0, 4)
+        x_lo2 = keep.tile([P, 2, P, PACK], BF16, name="x_lo2", tag="stage", align_bytes=64)
+        group_x(nc.vector.tensor_copy, x_lo2, 1, 0, 2)
+        x_hi2 = keep.tile([P, 2, P, PACK], BF16, name="x_hi2", tag="x_lo", align_bytes=64)
+        group_x(nc.vector.tensor_copy, x_hi2, 1, 2, 4)
+        quantize_x(x_lo2, 1, 0, 2)
+        quantize_x(x_hi2, 1, 2, 4)
 
         TILES = PASSES * PACK
         prob = [keep.tile([P, N], F32, name=f"prob{u}") for u in range(TILES)]
-        q = [keep.tile([P, PACK, N], F32, name=f"q{g}") for g in range(PASSES)]
+        q = [keep.tile([P, PACK, N], F32, name=f"q{g}", align_bytes=64) for g in range(PASSES)]
         squares_v = [keep.tile([P, N], BF16, name=f"squares_v{h}") for h in range(2)]
         squares_s = [keep.tile([P, N], BF16, name=f"squares_s{h}") for h in range(2)]
         sum_sq = keep.tile([P, TILES], F32, name="sum_sq")
@@ -115,7 +120,7 @@ def tile_attend_gnce_w_clip_kernel(tc, xT, wT, y, wt, xn, xm, offs, out):
         g_bf = [keep.tile([P, N, PACK], BF16, name=f"g_bf{g}", align_bytes=64) for g in range(PASSES)]
         g_codes = [keep.tile([P, N], U32, name=f"g_codes{g}", align_bytes=64) for g in range(PASSES)]
         g_scales = [keep.tile([P, N], U8, name=f"g_scales{g}", align_bytes=64) for g in range(PASSES)]
-        xm_bf = keep.tile([P, D // P, PASSES, P, PACK], BF16, name="xm_bf", align_bytes=64)
+        xm_first = keep.tile([P, PASSES, P, PACK], BF16, name="xm_first", align_bytes=64)
 
         for u in range(TILES):
             g, t = divmod(u, PACK)
@@ -142,8 +147,8 @@ def tile_attend_gnce_w_clip_kernel(tc, xT, wT, y, wt, xn, xm, offs, out):
         def square_on_scalar(u):
             g, t = divmod(u, PACK)
             if u == TILES - 1:
-                dst = xm_bf[:].rearrange("p j g d t -> p (j g) (d t)")[:, :, 0 : N // TILES]
-                src = q[g][:, t, :].rearrange("p (a b) -> p a b", a=TILES)
+                dst = xm_first[:].rearrange("p g d t -> p g (d t)")[:, :, 0 : N // PASSES]
+                src = q[g][:, t, :].rearrange("p (a b) -> p a b", a=PASSES)
             else:
                 dst, src = squares_s[u % 2][:], q[g][:, t, :]
             nc.scalar.activation(dst, src, ACT.Square, accum_out=sum_sq[:, u : u + 1])
@@ -159,13 +164,16 @@ def tile_attend_gnce_w_clip_kernel(tc, xT, wT, y, wt, xn, xm, offs, out):
                 factor[g][:], ratio[:, g * PACK : (g + 1) * PACK], 1.0, weight[:, g, :], ALU.min, ALU.mult
             )
 
-        def gradient(g):
+        def gradient(g, width):
             nc.vector.tensor_tensor(
-                g_bf[g][:].rearrange("p (c i) t -> p c t i", i=RUN),
-                q[g][:].rearrange("p t (c i) -> p c t i", i=RUN),
-                factor[g][:].unsqueeze(1).unsqueeze(3).to_broadcast([P, N // RUN, PACK, RUN]),
+                g_bf[g][:, 0:width, :].rearrange("p (c i) t -> p c t i", i=RUN),
+                q[g][:, :, 0:width].rearrange("p t (c i) -> p c t i", i=RUN),
+                factor[g][:].unsqueeze(1).unsqueeze(3).to_broadcast([P, width // RUN, PACK, RUN]),
                 ALU.mult,
             )
+            if width < N:
+                for t in range(PACK):
+                    nc.scalar.activation(g_bf[g][:, width:N, t], q[g][:, t, width:N], ACT.Copy, scale=factor[g][:, t : t + 1])
 
         def quantize_g(g):
             nc.vector.quantize_mx(
@@ -180,40 +188,33 @@ def tile_attend_gnce_w_clip_kernel(tc, xT, wT, y, wt, xn, xm, offs, out):
             row_ratio(u)
         for u in range(ON_VECTOR + 2, TILES):
             residual(u)
-        for g in range(PASSES):
-            late = keep.tile([P, T], F32, name=f"wide{2 + g}", tag=f"y_raw{g}")
-            nc.gpsimd.memset(late[:], 0.0)
-            wide.append(late)
-        for u in range(ON_VECTOR, TILES):
+        square_on_scalar(ON_VECTOR)
+        row_ratio(ON_VECTOR)
+        square_on_scalar(ON_VECTOR + 1)
+        for u in range(ON_VECTOR + 2, TILES):
             square_on_scalar(u)
-            if u > ON_VECTOR:
-                row_ratio(u - 1)
+            row_ratio(u - 1)
         row_ratio(TILES - 1)
-        row_factor(0)
-        gradient(0)
-        row_factor(1)
-        quantize_g(0)
-        gradient(1)
 
         xm_codes = [keep.tile([P, PASSES, P], U32, name=f"xm_codes{j}", align_bytes=64) for j in range(D // P)]
         xm_scales = [keep.tile([P, PASSES, P], U8, name=f"xm_scales{j}", align_bytes=64) for j in range(D // P)]
         dense = [keep.tile([P, N], F32, name=f"dense{j}") for j in range(D // P)]
-        for j in range(D // P):
-            feats = slice(j * P, (j + 1) * P)
+
+        def group_xm(dst, j):
             for g in range(PASSES):
                 nc.scalar.copy(
-                    out=xm_bf[:, j, g, :, :].rearrange("p (c i) t -> p c t i", i=RUN),
-                    in_=xm_raw[g][:, :, feats].rearrange("p t (c i) -> p c t i", i=RUN),
+                    out=dst[:, g, :, :].rearrange("p (c i) t -> p c t i", i=RUN),
+                    in_=xm_raw[g][:, :, j * P : (j + 1) * P].rearrange("p t (c i) -> p c t i", i=RUN),
                 )
+
+        def quantize_xm(src, j):
             nc.vector.quantize_mx(
                 out=xm_codes[j][:].rearrange("p g d -> p (g d)").bitcast(E4M3),
                 scales=xm_scales[j][:].rearrange("p g d -> p (g d)"),
-                in_=xm_bf[:, j, :, :, :].rearrange("p g d t -> p (g d t)"),
+                in_=src[:].rearrange("p g d t -> p (g d t)"),
             )
-            if j == 0:
-                quantize_g(1)
-        for j in range(D // P):
-            feats = slice(j * P, (j + 1) * P)
+
+        def product(j):
             dw = psum.tile([P, N], F32, name=f"bank{j}")
             for g in range(PASSES):
                 nc.tensor.matmul_mx(
@@ -221,5 +222,24 @@ def tile_attend_gnce_w_clip_kernel(tc, xT, wT, y, wt, xn, xm, offs, out):
                     rhs=g_codes[g][:].bitcast(E5M2), rhs_scale=g_scales[g][:], start=(g == 0), stop=(g == PASSES - 1),
                 )
             nc.scalar.copy(out=dense[j][:], in_=dw[:])
+
+        def place(j):
             nc.vector.tensor_copy(out=wide[j][:].indirect(offsets[:]), in_=dense[j][:])
-            nc.sync.dma_start(out=out[feats, :], in_=wide[j][:])
+            nc.sync.dma_start(out=out[j * P : (j + 1) * P, :], in_=wide[j][:])
+
+        row_factor(0)
+        gradient(0, N)
+        group_xm(xm_first, 0)
+        row_factor(1)
+        quantize_g(0)
+        gradient(1, N - ON_SCALAR)
+        quantize_xm(xm_first, 0)
+        quantize_g(1)
+        for j in range(D // P):
+            product(j)
+            if j + 1 < D // P:
+                tag = "q1" if j == 0 else f"xm_codes{j - 1}"
+                staged = keep.tile([P, PASSES, P, PACK], BF16, name=f"xm_bf{j + 1}", tag=tag, align_bytes=64)
+                group_xm(staged, j + 1)
+                quantize_xm(staged, j + 1)
+            place(j)

@@ -22,7 +22,7 @@ PASS = P * PACK
 PASSES = R // PASS
 RUN = 4
 ON_VECTOR = 3
-ON_SCALAR = 128
+ON_SCALAR = 96
 TINY = 2.0**-60
 
 
@@ -67,9 +67,9 @@ def tile_attend_gnce_w_clip_kernel(tc, xT, wT, y, wt, xn, xm, offs, out):
         warm = keep.tile([P, 1], F32, name="warm")
         nc.scalar.activation(warm[:], tiny[:], ACT.Sigmoid)
 
-        wide = [keep.tile([P, T], F32, name=f"wide{j}") for j in range(D // P)]
-        for j in range(D // P):
-            (nc.vector if j < 2 else nc.gpsimd).memset(wide[j][:], 0.0)
+        wide = [keep.tile([P, T], F32, name=f"wide{j}") for j in range(2)]
+        for j in range(2):
+            nc.vector.memset(wide[j][:], 0.0)
 
         rel_sq = keep.tile([P, PASSES, PACK], F32, name="rel_sq")
         nc.gpsimd.tensor_scalar(rel_sq[:], sq_len[:], 1.0 / (CLIP * CLIP), 0.0, ALU.mult, ALU.add)
@@ -97,15 +97,15 @@ def tile_attend_gnce_w_clip_kernel(tc, xT, wT, y, wt, xn, xm, offs, out):
                 in_=src[:].rearrange("p t m j -> p (t m j)"),
             )
 
-        x_lo = keep.tile([P, 2, P, PACK], BF16, name="x_lo", align_bytes=64)
-        x_hi = keep.tile([P, 2, P, PACK], BF16, name="x_hi", tag="stage", align_bytes=64)
-        group_x(nc.scalar.copy, x_lo, 0, 0, 2)
-        group_x(nc.vector.tensor_copy, x_hi, 0, 2, 4)
+        x_lo = keep.tile([P, 2, P, PACK], BF16, name="x_lo", tag="stage", align_bytes=64)
+        x_hi = keep.tile([P, 2, P, PACK], BF16, name="x_hi", align_bytes=64)
+        group_x(nc.vector.tensor_copy, x_lo, 0, 0, 2)
+        group_x(nc.scalar.copy, x_hi, 0, 2, 4)
         quantize_x(x_lo, 0, 0, 2)
         quantize_x(x_hi, 0, 2, 4)
         x_lo2 = keep.tile([P, 2, P, PACK], BF16, name="x_lo2", tag="stage", align_bytes=64)
         group_x(nc.vector.tensor_copy, x_lo2, 1, 0, 2)
-        x_hi2 = keep.tile([P, 2, P, PACK], BF16, name="x_hi2", tag="x_lo", align_bytes=64)
+        x_hi2 = keep.tile([P, 2, P, PACK], BF16, name="x_hi2", tag="x_hi", align_bytes=64)
         group_x(nc.vector.tensor_copy, x_hi2, 1, 2, 4)
         quantize_x(x_lo2, 1, 0, 2)
         quantize_x(x_hi2, 1, 2, 4)
@@ -120,7 +120,7 @@ def tile_attend_gnce_w_clip_kernel(tc, xT, wT, y, wt, xn, xm, offs, out):
         g_bf = [keep.tile([P, N, PACK], BF16, name=f"g_bf{g}", align_bytes=64) for g in range(PASSES)]
         g_codes = [keep.tile([P, N], U32, name=f"g_codes{g}", align_bytes=64) for g in range(PASSES)]
         g_scales = [keep.tile([P, N], U8, name=f"g_scales{g}", align_bytes=64) for g in range(PASSES)]
-        xm_first = keep.tile([P, PASSES, P, PACK], BF16, name="xm_first", align_bytes=64)
+        xm_first = keep.tile([P, 1, PASSES, P, PACK], BF16, name="xm_first", align_bytes=64)
 
         for u in range(TILES):
             g, t = divmod(u, PACK)
@@ -147,7 +147,7 @@ def tile_attend_gnce_w_clip_kernel(tc, xT, wT, y, wt, xn, xm, offs, out):
         def square_on_scalar(u):
             g, t = divmod(u, PACK)
             if u == TILES - 1:
-                dst = xm_first[:].rearrange("p g d t -> p g (d t)")[:, :, 0 : N // PASSES]
+                dst = xm_first[:].rearrange("p j g d t -> p (j g) (d t)")[:, :, 0 : N // PASSES]
                 src = q[g][:, t, :].rearrange("p (a b) -> p a b", a=PASSES)
             else:
                 dst, src = squares_s[u % 2][:], q[g][:, t, :]
@@ -188,6 +188,10 @@ def tile_attend_gnce_w_clip_kernel(tc, xT, wT, y, wt, xn, xm, offs, out):
             row_ratio(u)
         for u in range(ON_VECTOR + 2, TILES):
             residual(u)
+        for g in range(PASSES):
+            late = keep.tile([P, T], F32, name=f"wide{2 + g}", tag=f"y_raw{g}")
+            nc.gpsimd.memset(late[:], 0.0)
+            wide.append(late)
         square_on_scalar(ON_VECTOR)
         row_ratio(ON_VECTOR)
         square_on_scalar(ON_VECTOR + 1)
@@ -196,29 +200,29 @@ def tile_attend_gnce_w_clip_kernel(tc, xT, wT, y, wt, xn, xm, offs, out):
             row_ratio(u - 1)
         row_ratio(TILES - 1)
 
-        xm_codes = [keep.tile([P, PASSES, P], U32, name=f"xm_codes{j}", align_bytes=64) for j in range(D // P)]
-        xm_scales = [keep.tile([P, PASSES, P], U8, name=f"xm_scales{j}", align_bytes=64) for j in range(D // P)]
+        xm_codes = keep.tile([P, D // P, PASSES, P], U32, name="xm_codes", align_bytes=64)
+        xm_scales = keep.tile([P, D // P, PASSES, P], U8, name="xm_scales", align_bytes=64)
         dense = [keep.tile([P, N], F32, name=f"dense{j}") for j in range(D // P)]
 
-        def group_xm(dst, j):
+        def group_xm(copy, dst, j0, j1):
             for g in range(PASSES):
-                nc.scalar.copy(
-                    out=dst[:, g, :, :].rearrange("p (c i) t -> p c t i", i=RUN),
-                    in_=xm_raw[g][:, :, j * P : (j + 1) * P].rearrange("p t (c i) -> p c t i", i=RUN),
+                copy(
+                    out=dst[:, :, g, :, :].rearrange("p j (c i) t -> p j c t i", i=RUN),
+                    in_=xm_raw[g][:, :, j0 * P : j1 * P].rearrange("p t (j c i) -> p j c t i", j=j1 - j0, i=RUN),
                 )
 
-        def quantize_xm(src, j):
+        def quantize_xm(src, j0, j1):
             nc.vector.quantize_mx(
-                out=xm_codes[j][:].rearrange("p g d -> p (g d)").bitcast(E4M3),
-                scales=xm_scales[j][:].rearrange("p g d -> p (g d)"),
-                in_=src[:].rearrange("p g d t -> p (g d t)"),
+                out=xm_codes[:, j0:j1, :, :].rearrange("p j g d -> p (j g d)").bitcast(E4M3),
+                scales=xm_scales[:, j0:j1, :, :].rearrange("p j g d -> p (j g d)"),
+                in_=src[:].rearrange("p j g d t -> p (j g d t)"),
             )
 
         def product(j):
             dw = psum.tile([P, N], F32, name=f"bank{j}")
             for g in range(PASSES):
                 nc.tensor.matmul_mx(
-                    out=dw[:], lhsT=xm_codes[j][:, g, :].bitcast(E4M3), lhsT_scale=xm_scales[j][:, g, :],
+                    out=dw[:], lhsT=xm_codes[:, j, g, :].bitcast(E4M3), lhsT_scale=xm_scales[:, j, g, :],
                     rhs=g_codes[g][:].bitcast(E5M2), rhs_scale=g_scales[g][:], start=(g == 0), stop=(g == PASSES - 1),
                 )
             nc.scalar.copy(out=dense[j][:], in_=dw[:])
@@ -229,17 +233,20 @@ def tile_attend_gnce_w_clip_kernel(tc, xT, wT, y, wt, xn, xm, offs, out):
 
         row_factor(0)
         gradient(0, N)
-        group_xm(xm_first, 0)
+        group_xm(nc.scalar.copy, xm_first, 0, 1)
         row_factor(1)
         quantize_g(0)
         gradient(1, N - ON_SCALAR)
-        quantize_xm(xm_first, 0)
+        quantize_xm(xm_first, 0, 1)
         quantize_g(1)
-        for j in range(D // P):
+        product(0)
+        xm_second = keep.tile([P, 1, PASSES, P, PACK], BF16, name="xm_second", tag="q1", align_bytes=64)
+        group_xm(nc.scalar.copy, xm_second, 1, 2)
+        xm_rest = keep.tile([P, 2, PASSES, P, PACK], BF16, name="xm_rest", tag="g_bf1", align_bytes=64)
+        group_xm(nc.vector.tensor_copy, xm_rest, 2, 4)
+        quantize_xm(xm_second, 1, 2)
+        quantize_xm(xm_rest, 2, 4)
+        place(0)
+        for j in range(1, D // P):
             product(j)
-            if j + 1 < D // P:
-                tag = "q1" if j == 0 else f"xm_codes{j - 1}"
-                staged = keep.tile([P, PASSES, P, PACK], BF16, name=f"xm_bf{j + 1}", tag=tag, align_bytes=64)
-                group_xm(staged, j + 1)
-                quantize_xm(staged, j + 1)
             place(j)

@@ -72,7 +72,8 @@ def tile_attend_gnce_w_clip_kernel(tc, xT, wT, y, wt, xn, xm, offs, out):
             nc.vector.memset(wide[j][:], 0.0)
 
         rel_sq = keep.tile([P, PASSES, PACK], F32, name="rel_sq")
-        nc.gpsimd.tensor_scalar(rel_sq[:], sq_len[:], 1.0 / (CLIP * CLIP), 0.0, ALU.mult, ALU.add)
+        nc.gpsimd.tensor_scalar(rel_sq[:], sq_len[:], 1.0 / (CLIP * CLIP), TINY, ALU.mult, ALU.add)
+        inv_sq = keep.tile([P, PASSES, PACK], F32, name="inv_sq")
 
         w_bf = keep.tile([P, N, PACK], BF16, name="w_bf", tag="stage", align_bytes=64)
         w_codes = keep.tile([P, N], U32, name="w_codes", align_bytes=64)
@@ -132,7 +133,10 @@ def tile_attend_gnce_w_clip_kernel(tc, xT, wT, y, wt, xn, xm, offs, out):
             )
             nc.scalar.activation(prob[u][:], a[:], ACT.Sigmoid, bias=zero[:])
 
-        ratio = keep.tile([P, TILES], F32, name="ratio", tag="column")
+        nc.vector.reciprocal(inv_sq[:], rel_sq[:])
+        rel_len = keep.tile([P, TILES], F32, name="rel_len", tag="column")
+        nc.scalar.activation(rel_len[:], inv_sq[:].rearrange("p g t -> p (g t)"), ACT.Abs_reciprocal_sqrt)
+        ratio = keep.tile([P, TILES], F32, name="ratio")
 
         def residual(u):
             g, t = divmod(u, PACK)
@@ -141,7 +145,7 @@ def tile_attend_gnce_w_clip_kernel(tc, xT, wT, y, wt, xn, xm, offs, out):
         def square_on_vector(u):
             g, t = divmod(u, PACK)
             nc.vector.scalar_tensor_tensor(
-                squares_v[u % 2][:], q[g][:, t, :], 1.0, q[g][:, t, :], ALU.mult, ALU.mult, accum_out=sum_sq[:, u : u + 1]
+                squares_v[u % 2][:], q[g][:, t, :], rel_sq[:, g, t : t + 1], q[g][:, t, :], ALU.mult, ALU.mult, accum_out=sum_sq[:, u : u + 1]
             )
 
         def square_on_scalar(u):
@@ -151,13 +155,11 @@ def tile_attend_gnce_w_clip_kernel(tc, xT, wT, y, wt, xn, xm, offs, out):
                 src = q[g][:, t, :].rearrange("p (a b) -> p a b", a=PASSES)
             else:
                 dst, src = squares_s[u % 2][:], q[g][:, t, :]
-            nc.scalar.activation(dst, src, ACT.Square, accum_out=sum_sq[:, u : u + 1])
+            nc.scalar.activation(dst, src, ACT.Square, scale=rel_len[:, u : u + 1], accum_out=sum_sq[:, u : u + 1])
 
-        def row_ratio(u):
-            g, t = divmod(u, PACK)
-            nc.scalar.activation(
-                ratio[:, u : u + 1], sum_sq[:, u : u + 1], ACT.Abs_reciprocal_sqrt, bias=tiny[:], scale=rel_sq[:, g, t : t + 1]
-            )
+        def row_ratio(g):
+            cols = slice(g * PACK, (g + 1) * PACK)
+            nc.scalar.activation(ratio[:, cols], sum_sq[:, cols], ACT.Abs_reciprocal_sqrt, bias=tiny[:])
 
         def row_factor(g):
             nc.vector.scalar_tensor_tensor(
@@ -185,31 +187,26 @@ def tile_attend_gnce_w_clip_kernel(tc, xT, wT, y, wt, xn, xm, offs, out):
         for u in range(ON_VECTOR):
             residual(u + 2)
             square_on_vector(u)
-            row_ratio(u)
         for u in range(ON_VECTOR + 2, TILES):
             residual(u)
         for g in range(PASSES):
             late = keep.tile([P, T], F32, name=f"wide{2 + g}", tag=f"y_raw{g}")
             nc.gpsimd.memset(late[:], 0.0)
             wide.append(late)
-        square_on_scalar(ON_VECTOR)
-        row_ratio(ON_VECTOR)
-        square_on_scalar(ON_VECTOR + 1)
-        for u in range(ON_VECTOR + 2, TILES):
+        for u in range(ON_VECTOR, TILES):
             square_on_scalar(u)
-            row_ratio(u - 1)
-        row_ratio(TILES - 1)
+            if u % PACK == PACK - 1:
+                row_ratio(u // PACK)
 
         xm_codes = keep.tile([P, D // P, PASSES, P], U32, name="xm_codes", align_bytes=64)
         xm_scales = keep.tile([P, D // P, PASSES, P], U8, name="xm_scales", align_bytes=64)
         dense = [keep.tile([P, N], F32, name=f"dense{j}") for j in range(D // P)]
 
-        def group_xm(copy, dst, j0, j1):
-            for g in range(PASSES):
-                copy(
-                    out=dst[:, :, g, :, :].rearrange("p j (c i) t -> p j c t i", i=RUN),
-                    in_=xm_raw[g][:, :, j0 * P : j1 * P].rearrange("p t (j c i) -> p j c t i", j=j1 - j0, i=RUN),
-                )
+        def group_xm(copy, dst, g, j0, j1):
+            copy(
+                out=dst[:, :, g, :, :].rearrange("p j (c i) t -> p j c t i", i=RUN),
+                in_=xm_raw[g][:, :, j0 * P : j1 * P].rearrange("p t (j c i) -> p j c t i", j=j1 - j0, i=RUN),
+            )
 
         def quantize_xm(src, j0, j1):
             nc.vector.quantize_mx(
@@ -233,7 +230,8 @@ def tile_attend_gnce_w_clip_kernel(tc, xT, wT, y, wt, xn, xm, offs, out):
 
         row_factor(0)
         gradient(0, N)
-        group_xm(nc.scalar.copy, xm_first, 0, 1)
+        for g in range(PASSES):
+            group_xm(nc.scalar.copy, xm_first[:], g, 0, 1)
         row_factor(1)
         quantize_g(0)
         gradient(1, N - ON_SCALAR)
@@ -241,9 +239,12 @@ def tile_attend_gnce_w_clip_kernel(tc, xT, wT, y, wt, xn, xm, offs, out):
         quantize_g(1)
         product(0)
         xm_second = keep.tile([P, 1, PASSES, P, PACK], BF16, name="xm_second", tag="q1", align_bytes=64)
-        group_xm(nc.scalar.copy, xm_second, 1, 2)
+        for g in range(PASSES):
+            group_xm(nc.scalar.copy, xm_second[:], g, 1, 2)
         xm_rest = keep.tile([P, 2, PASSES, P, PACK], BF16, name="xm_rest", tag="g_bf1", align_bytes=64)
-        group_xm(nc.vector.tensor_copy, xm_rest, 2, 4)
+        group_xm(nc.scalar.copy, xm_rest[:, 1:2], 0, 3, 4)
+        group_xm(nc.vector.tensor_copy, xm_rest[:, 0:1], 0, 2, 3)
+        group_xm(nc.vector.tensor_copy, xm_rest[:], 1, 2, 4)
         quantize_xm(xm_second, 1, 2)
         quantize_xm(xm_rest, 2, 4)
         place(0)

@@ -22,7 +22,7 @@ PASS = P * PACK
 PASSES = R // PASS
 RUN = 4
 ON_VECTOR = 3
-ON_SCALAR = 96
+HALF = N // 2
 TINY = 2.0**-60
 
 
@@ -42,7 +42,7 @@ def tile_attend_gnce_w_clip_kernel(tc, xT, wT, y, wt, xn, xm, offs, out):
         x_raw = [keep.tile([P, PACK, PASS], F32, name=f"x_raw{g}") for g in range(PASSES)]
         w_raw = [keep.tile([P, T], F32, name=f"w_raw{j}") for j in range(PACK)]
         y_raw = [keep.tile([P, PACK, N], F32, name=f"y_raw{g}") for g in range(PASSES)]
-        xm_raw = [keep.tile([P, PACK, D], F32, name=f"xm_raw{g}") for g in range(PASSES)]
+        xm_raw = [keep.tile([P, PASSES, PACK, D // 2], F32, name=f"xm_raw{h}") for h in range(2)]
         weight = keep.tile([P, PASSES, PACK], F32, name="weight")
         sq_len = keep.tile([P, PASSES, PACK], F32, name="sq_len")
 
@@ -57,8 +57,9 @@ def tile_attend_gnce_w_clip_kernel(tc, xT, wT, y, wt, xn, xm, offs, out):
         for g in range(PASSES):
             for h in range(2):
                 nc.sync.dma_start(out=y_raw[g][:, 2 * h : 2 * h + 2, :], in_=y_rows[g][:, 2 * h : 2 * h + 2, :])
-        for g in range(PASSES):
-            nc.sync.dma_start(out=xm_raw[g][:], in_=xm_rows[g])
+        for h in range(2):
+            for g in range(PASSES):
+                nc.sync.dma_start(out=xm_raw[h][:, g], in_=xm_rows[g][:, :, h * D // 2 : (h + 1) * D // 2])
 
         zero = keep.tile([P, 1], F32, name="zero", tag="column")
         tiny = keep.tile([P, 1], F32, name="tiny")
@@ -116,12 +117,13 @@ def tile_attend_gnce_w_clip_kernel(tc, xT, wT, y, wt, xn, xm, offs, out):
         q = [keep.tile([P, PACK, N], F32, name=f"q{g}", align_bytes=64) for g in range(PASSES)]
         squares_v = [keep.tile([P, N], BF16, name=f"squares_v{h}") for h in range(2)]
         squares_s = [keep.tile([P, N], BF16, name=f"squares_s{h}") for h in range(2)]
-        sum_sq = keep.tile([P, TILES], F32, name="sum_sq")
+        sum_sq = keep.tile([P, TILES], F32, name="sum_sq", tag="after_ratio", align_bytes=64)
         factor = [keep.tile([P, PACK], F32, name=f"factor{g}") for g in range(PASSES)]
-        g_bf = [keep.tile([P, N, PACK], BF16, name=f"g_bf{g}", align_bytes=64) for g in range(PASSES)]
-        g_codes = [keep.tile([P, N], U32, name=f"g_codes{g}", align_bytes=64) for g in range(PASSES)]
-        g_scales = [keep.tile([P, N], U8, name=f"g_scales{g}", align_bytes=64) for g in range(PASSES)]
-        xm_first = keep.tile([P, 1, PASSES, P, PACK], BF16, name="xm_first", align_bytes=64)
+        g_codes = [keep.tile([P, HALF + N], U32, name=f"g_codes{g}", align_bytes=64) for g in range(PASSES)]
+        g_scales = [keep.tile([P, HALF + N], U8, name=f"g_scales{g}", align_bytes=64) for g in range(PASSES)]
+        for g in range(PASSES):
+            nc.vector.memset(g_codes[g][:, 0:HALF], 0)
+            nc.vector.memset(g_scales[g][:, 0:HALF].bitcast(U32), 0)
 
         for u in range(TILES):
             g, t = divmod(u, PACK)
@@ -136,7 +138,7 @@ def tile_attend_gnce_w_clip_kernel(tc, xT, wT, y, wt, xn, xm, offs, out):
         nc.vector.reciprocal(inv_sq[:], rel_sq[:])
         rel_len = keep.tile([P, TILES], F32, name="rel_len", tag="column")
         nc.scalar.activation(rel_len[:], inv_sq[:].rearrange("p g t -> p (g t)"), ACT.Abs_reciprocal_sqrt)
-        ratio = keep.tile([P, TILES], F32, name="ratio")
+        ratio = keep.tile([P, TILES], F32, name="ratio", tag="after_factor", align_bytes=64)
 
         def residual(u):
             g, t = divmod(u, PACK)
@@ -150,12 +152,7 @@ def tile_attend_gnce_w_clip_kernel(tc, xT, wT, y, wt, xn, xm, offs, out):
 
         def square_on_scalar(u):
             g, t = divmod(u, PACK)
-            if u == TILES - 1:
-                dst = xm_first[:].rearrange("p j g d t -> p (j g) (d t)")[:, :, 0 : N // PASSES]
-                src = q[g][:, t, :].rearrange("p (a b) -> p a b", a=PASSES)
-            else:
-                dst, src = squares_s[u % 2][:], q[g][:, t, :]
-            nc.scalar.activation(dst, src, ACT.Square, scale=rel_len[:, u : u + 1], accum_out=sum_sq[:, u : u + 1])
+            nc.scalar.activation(squares_s[u % 2][:], q[g][:, t, :], ACT.Square, scale=rel_len[:, u : u + 1], accum_out=sum_sq[:, u : u + 1])
 
         def row_ratio(g):
             cols = slice(g * PACK, (g + 1) * PACK)
@@ -166,20 +163,21 @@ def tile_attend_gnce_w_clip_kernel(tc, xT, wT, y, wt, xn, xm, offs, out):
                 factor[g][:], ratio[:, g * PACK : (g + 1) * PACK], 1.0, weight[:, g, :], ALU.min, ALU.mult
             )
 
-        def gradient(g, width):
+        def slots(h):
+            return slice(h * HALF, (h + 1) * HALF)
+
+        def gradient(dst, g, h):
             nc.vector.tensor_tensor(
-                g_bf[g][:, 0:width, :].rearrange("p (c i) t -> p c t i", i=RUN),
-                q[g][:, :, 0:width].rearrange("p t (c i) -> p c t i", i=RUN),
-                factor[g][:].unsqueeze(1).unsqueeze(3).to_broadcast([P, width // RUN, PACK, RUN]),
+                dst[:].rearrange("p (c i) t -> p c t i", i=RUN),
+                q[g][:, :, slots(h)].rearrange("p t (c i) -> p c t i", i=RUN),
+                factor[g][:].unsqueeze(1).unsqueeze(3).to_broadcast([P, HALF // RUN, PACK, RUN]),
                 ALU.mult,
             )
-            if width < N:
-                for t in range(PACK):
-                    nc.scalar.activation(g_bf[g][:, width:N, t], q[g][:, t, width:N], ACT.Copy, scale=factor[g][:, t : t + 1])
 
-        def quantize_g(g):
+        def quantize_g(src, g, h):
+            cols = slots(h + 1)
             nc.vector.quantize_mx(
-                out=g_codes[g][:].bitcast(E5M2), scales=g_scales[g][:], in_=g_bf[g][:].rearrange("p n t -> p (n t)")
+                out=g_codes[g][:, cols].bitcast(E5M2), scales=g_scales[g][:, cols], in_=src[:].rearrange("p n t -> p (n t)")
             )
 
         residual(0)
@@ -198,56 +196,83 @@ def tile_attend_gnce_w_clip_kernel(tc, xT, wT, y, wt, xn, xm, offs, out):
             if u % PACK == PACK - 1:
                 row_ratio(u // PACK)
 
-        xm_codes = keep.tile([P, D // P, PASSES, P], U32, name="xm_codes", align_bytes=64)
-        xm_scales = keep.tile([P, D // P, PASSES, P], U8, name="xm_scales", align_bytes=64)
-        dense = [keep.tile([P, N], F32, name=f"dense{j}") for j in range(D // P)]
+        xm_codes = [keep.tile([P, PASSES, P], U32, name=f"xm_codes{j}", align_bytes=64) for j in range(D // P)]
+        xm_scales = [keep.tile([P, PASSES, P], U8, name=f"xm_scales{j}", align_bytes=64) for j in range(D // P)]
 
-        def group_xm(copy, dst, g, j0, j1):
-            copy(
-                out=dst[:, :, g, :, :].rearrange("p j (c i) t -> p j c t i", i=RUN),
-                in_=xm_raw[g][:, :, j0 * P : j1 * P].rearrange("p t (j c i) -> p j c t i", j=j1 - j0, i=RUN),
+        def group_xm(j, tag):
+            dst = keep.tile([P, PASSES, P, PACK], BF16, name=f"xm_bf{j}", tag=tag, align_bytes=64)
+            nc.scalar.copy(
+                out=dst[:].rearrange("p g (c i) t -> p g c t i", i=RUN),
+                in_=xm_raw[j // 2][:, :, :, (j % 2) * P : (j % 2 + 1) * P].rearrange("p g t (c i) -> p g c t i", i=RUN),
             )
+            return dst
 
-        def quantize_xm(src, j0, j1):
+        def quantize_xm(src, j):
             nc.vector.quantize_mx(
-                out=xm_codes[:, j0:j1, :, :].rearrange("p j g d -> p (j g d)").bitcast(E4M3),
-                scales=xm_scales[:, j0:j1, :, :].rearrange("p j g d -> p (j g d)"),
-                in_=src[:].rearrange("p j g d t -> p (j g d t)"),
+                out=xm_codes[j][:].rearrange("p g d -> p (g d)").bitcast(E4M3),
+                scales=xm_scales[j][:].rearrange("p g d -> p (g d)"),
+                in_=src[:].rearrange("p g d t -> p (g d t)"),
             )
 
-        def product(j):
-            dw = psum.tile([P, N], F32, name=f"bank{j}")
+        def product(j, bank, first):
+            dw = psum.tile([P, N], F32, name=f"bank{bank}")
+            cols = slice(first, first + N)
             for g in range(PASSES):
                 nc.tensor.matmul_mx(
-                    out=dw[:], lhsT=xm_codes[:, j, g, :].bitcast(E4M3), lhsT_scale=xm_scales[:, j, g, :],
-                    rhs=g_codes[g][:].bitcast(E5M2), rhs_scale=g_scales[g][:], start=(g == 0), stop=(g == PASSES - 1),
+                    out=dw[:], lhsT=xm_codes[j][:, g, :].bitcast(E4M3), lhsT_scale=xm_scales[j][:, g, :],
+                    rhs=g_codes[g][:, cols].bitcast(E5M2), rhs_scale=g_scales[g][:, cols], start=(g == 0), stop=(g == PASSES - 1),
                 )
-            nc.scalar.copy(out=dense[j][:], in_=dw[:])
+            return dw
 
-        def place(j):
-            nc.vector.tensor_copy(out=wide[j][:].indirect(offsets[:]), in_=dense[j][:])
+        def empty(dw, first, name):
+            dense = keep.tile([P, N - first], F32, name=name, align_bytes=64)
+            nc.scalar.copy(out=dense[:], in_=dw[:, first:N])
+            return dense
+
+        def place(j, dense, first_slot):
+            count = dense.shape[1]
+            nc.vector.tensor_copy(out=wide[j][:].indirect(offsets[:, first_slot // 16 : (first_slot + count) // 16]), in_=dense[:])
+
+        def store(j):
             nc.sync.dma_start(out=out[j * P : (j + 1) * P, :], in_=wide[j][:])
 
+        g_early = [keep.tile([P, HALF, PACK], BF16, name=f"g_early{g}", align_bytes=64) for g in range(PASSES)]
         row_factor(0)
-        gradient(0, N)
-        for g in range(PASSES):
-            group_xm(nc.scalar.copy, xm_first[:], g, 0, 1)
+        gradient(g_early[0], 0, 0)
         row_factor(1)
-        quantize_g(0)
-        gradient(1, N - ON_SCALAR)
-        quantize_xm(xm_first, 0, 1)
-        quantize_g(1)
-        product(0)
-        xm_second = keep.tile([P, 1, PASSES, P, PACK], BF16, name="xm_second", tag="q1", align_bytes=64)
-        for g in range(PASSES):
-            group_xm(nc.scalar.copy, xm_second[:], g, 1, 2)
-        xm_rest = keep.tile([P, 2, PASSES, P, PACK], BF16, name="xm_rest", tag="g_bf1", align_bytes=64)
-        group_xm(nc.scalar.copy, xm_rest[:, 1:2], 0, 3, 4)
-        group_xm(nc.vector.tensor_copy, xm_rest[:, 0:1], 0, 2, 3)
-        group_xm(nc.vector.tensor_copy, xm_rest[:], 1, 2, 4)
-        quantize_xm(xm_second, 1, 2)
-        quantize_xm(xm_rest, 2, 4)
-        place(0)
-        for j in range(1, D // P):
-            product(j)
-            place(j)
+        quantize_g(g_early[0], 0, 0)
+        gradient(g_early[1], 1, 0)
+        xm0 = group_xm(0, "after_ratio")
+        xm1 = group_xm(1, "after_factor")
+        quantize_xm(xm0, 0)
+        quantize_g(g_early[1], 1, 0)
+        early0 = empty(product(0, 0, 0), HALF, "early0")
+        quantize_xm(xm1, 1)
+        g_late0 = keep.tile([P, HALF, PACK], BF16, name="g_late0", tag="g_early1", align_bytes=64)
+        gradient(g_late0, 0, 1)
+        place(0, early0, 0)
+
+        g_rows = keep.tile([P, PACK, HALF], BF16, name="g_rows", tag="after_ratio", align_bytes=64)
+        g_late1 = keep.tile([P, HALF, PACK], BF16, name="g_late1", align_bytes=64)
+        for t in range(PACK):
+            nc.scalar.activation(g_rows[:, t, :], q[1][:, t, slots(1)], ACT.Copy, scale=factor[1][:, t : t + 1])
+        nc.scalar.copy(
+            out=g_late1[:].rearrange("p (c i) t -> p c t i", i=RUN), in_=g_rows[:].rearrange("p t (c i) -> p c t i", i=RUN)
+        )
+        quantize_g(g_late0, 0, 1)
+        quantize_g(g_late1, 1, 1)
+        early1 = empty(product(1, 1, 0), HALF, "early1")
+        place(1, early1, 0)
+        late0 = empty(product(0, 2, HALF), HALF, "late0")
+        late1 = empty(product(1, 3, HALF), HALF, "late1")
+        xm2 = group_xm(2, "after_ratio")
+        xm3 = group_xm(3, "early1")
+        place(0, late0, HALF)
+        store(0)
+        quantize_xm(xm2, 2)
+        place(1, late1, HALF)
+        store(1)
+        quantize_xm(xm3, 3)
+        for j in (2, 3):
+            place(j, empty(product(j, 2 + j, HALF), 0, f"dense{j}"), 0)
+            store(j)

@@ -187,8 +187,8 @@ def tile_attend_gnce_w_clip_kernel(tc, xT, wT, y, wt, xn, xm, offs, out):
             square_on_vector(u)
         for u in range(ON_VECTOR + 2, TILES):
             residual(u)
-        for g in range(PASSES):
-            late = keep.tile([P, T], F32, name=f"wide{2 + g}", tag=f"y_raw{g}")
+        for j, tag in ((2, "stage"), (3, "x_hi")):
+            late = keep.tile([P, T], F32, name=f"wide{j}", tag=tag, align_bytes=64)
             nc.gpsimd.memset(late[:], 0.0)
             wide.append(late)
         for u in range(ON_VECTOR, TILES):
@@ -247,9 +247,10 @@ def tile_attend_gnce_w_clip_kernel(tc, xT, wT, y, wt, xn, xm, offs, out):
         quantize_xm(xm0, 0)
         quantize_g(g_early[1], 1, 0)
         early0 = empty(product(0, 0, 0), HALF, "early0")
-        quantize_xm(xm1, 1)
         g_late0 = keep.tile([P, HALF, PACK], BF16, name="g_late0", tag="g_early1", align_bytes=64)
         gradient(g_late0, 0, 1)
+        quantize_xm(xm1, 1)
+        quantize_g(g_late0, 0, 1)
         place(0, early0, 0)
 
         g_rows = keep.tile([P, PACK, HALF], BF16, name="g_rows", tag="after_ratio", align_bytes=64)
@@ -259,7 +260,6 @@ def tile_attend_gnce_w_clip_kernel(tc, xT, wT, y, wt, xn, xm, offs, out):
         nc.scalar.copy(
             out=g_late1[:].rearrange("p (c i) t -> p c t i", i=RUN), in_=g_rows[:].rearrange("p t (c i) -> p c t i", i=RUN)
         )
-        quantize_g(g_late0, 0, 1)
         quantize_g(g_late1, 1, 1)
         early1 = empty(product(1, 1, 0), HALF, "early1")
         place(1, early1, 0)

@@ -21,7 +21,7 @@ PACK = 4
 PASS = P * PACK
 PASSES = R // PASS
 RUN = 4
-ON_VECTOR = 3
+ON_VECTOR = 4
 HALF = N // 2
 TINY = 2.0**-60
 
@@ -39,7 +39,8 @@ def tile_attend_gnce_w_clip_kernel(tc, xT, wT, y, wt, xn, xm, offs, out):
         y_rows = y[0].rearrange("(g p t) n -> g p t n", p=P, t=PACK)
         xm_rows = xm[0].rearrange("(g p t) d -> g p t d", p=P, t=PACK)
 
-        x_raw = [keep.tile([P, PACK, PASS], F32, name=f"x_raw{g}") for g in range(PASSES)]
+        x_raw = keep.tile([P, PACK, PASS], F32, name="x_raw")
+        x_part = [keep.tile([P, PACK, PASS // 2], F32, name=f"x_part{h}") for h in range(2)]
         w_raw = [keep.tile([P, T], F32, name=f"w_raw{j}") for j in range(PACK)]
         y_raw = [keep.tile([P, PACK, N], F32, name=f"y_raw{g}") for g in range(PASSES)]
         xm_raw = [keep.tile([P, PASSES, PACK, D // 2], F32, name=f"xm_raw{h}") for h in range(2)]
@@ -50,8 +51,9 @@ def tile_attend_gnce_w_clip_kernel(tc, xT, wT, y, wt, xn, xm, offs, out):
             nc.sync.dma_start(out=w_raw[j][:], in_=wT_planes[:, j, :])
             if j == 0:
                 nc.sync.dma_start(offsets[:], offs)
-        for g in range(PASSES):
-            nc.sync.dma_start(out=x_raw[g][:], in_=xT_planes[:, :, g * PASS : (g + 1) * PASS])
+        nc.sync.dma_start(out=x_raw[:], in_=xT_planes[:, :, 0:PASS])
+        for h in range(2):
+            nc.sync.dma_start(out=x_part[h][:], in_=xT_planes[:, :, PASS + h * PASS // 2 : PASS + (h + 1) * PASS // 2])
         nc.sync.dma_start(out=sq_len[:], in_=xn[0].rearrange("(g p t) o -> p g (t o)", p=P, t=PACK))
         nc.sync.dma_start(out=weight[:], in_=wt[0].rearrange("(g p t) o -> p g (t o)", p=P, t=PACK))
         for g in range(PASSES):
@@ -79,41 +81,53 @@ def tile_attend_gnce_w_clip_kernel(tc, xT, wT, y, wt, xn, xm, offs, out):
         w_bf = keep.tile([P, N, PACK], BF16, name="w_bf", tag="stage", align_bytes=64)
         w_codes = keep.tile([P, N], U32, name="w_codes", align_bytes=64)
         w_scales = keep.tile([P, N], U8, name="w_scales", align_bytes=64)
-        for j in range(PACK):
+        for j in range(PACK - 1):
             nc.vector.tensor_copy(out=w_bf[:, :, j], in_=w_raw[j][:].indirect(offsets[:]))
-        nc.vector.quantize_mx(out=w_codes[:].bitcast(E4M3), scales=w_scales[:], in_=w_bf[:].rearrange("p n j -> p (n j)"))
+        for h in range(2):
+            nc.vector.tensor_copy(
+                out=w_bf[:, h * HALF : (h + 1) * HALF, PACK - 1],
+                in_=w_raw[PACK - 1][:].indirect(offsets[:, h * HALF // 16 : (h + 1) * HALF // 16]),
+            )
+        for h in range(2):
+            cols = slice(h * HALF, (h + 1) * HALF)
+            nc.vector.quantize_mx(
+                out=w_codes[:, cols].bitcast(E4M3), scales=w_scales[:, cols], in_=w_bf[:, cols, :].rearrange("p n j -> p (n j)")
+            )
 
         x_codes = [keep.tile([P, PASS], U32, name=f"x_codes{g}", align_bytes=64) for g in range(PASSES)]
         x_scales = [keep.tile([P, PASS], U8, name=f"x_scales{g}", align_bytes=64) for g in range(PASSES)]
 
-        def group_x(copy, dst, g, t0, t1):
+        def group_x(copy, dst, src, t0, t1):
             copy(
-                out=dst[:].rearrange("p t m j -> p m j t"),
-                in_=x_raw[g][:].rearrange("p j (m t) -> p m j t", t=PACK)[:, :, :, t0:t1],
+                out=dst.rearrange("p t m j -> p m j t"),
+                in_=src[:].rearrange("p j (m t) -> p m j t", t=PACK)[:, :, :, t0:t1],
             )
 
         def quantize_x(src, g, t0, t1):
             cols = slice(t0 * P, t1 * P)
             nc.vector.quantize_mx(
                 out=x_codes[g][:, cols].bitcast(E4M3), scales=x_scales[g][:, cols],
-                in_=src[:].rearrange("p t m j -> p (t m j)"),
+                in_=src.rearrange("p t m j -> p (t m j)"),
             )
 
         x_lo = keep.tile([P, 2, P, PACK], BF16, name="x_lo", tag="stage", align_bytes=64)
         x_hi = keep.tile([P, 2, P, PACK], BF16, name="x_hi", align_bytes=64)
-        group_x(nc.vector.tensor_copy, x_lo, 0, 0, 2)
-        group_x(nc.scalar.copy, x_hi, 0, 2, 4)
-        quantize_x(x_lo, 0, 0, 2)
-        quantize_x(x_hi, 0, 2, 4)
+        group_x(nc.vector.tensor_copy, x_lo[:], x_raw, 0, 2)
+        group_x(nc.scalar.copy, x_hi[:], x_raw, 2, 4)
+        quantize_x(x_lo[:, 0:1], 0, 0, 1)
+        quantize_x(x_lo[:, 1:2], 0, 1, 2)
         x_lo2 = keep.tile([P, 2, P, PACK], BF16, name="x_lo2", tag="stage", align_bytes=64)
-        group_x(nc.vector.tensor_copy, x_lo2, 1, 0, 2)
+        group_x(nc.vector.tensor_copy, x_lo2[:, :, 0 : P // 2, :], x_part[0], 0, 2)
+        quantize_x(x_hi[:], 0, 2, 4)
         x_hi2 = keep.tile([P, 2, P, PACK], BF16, name="x_hi2", tag="x_hi", align_bytes=64)
-        group_x(nc.vector.tensor_copy, x_hi2, 1, 2, 4)
-        quantize_x(x_lo2, 1, 0, 2)
-        quantize_x(x_hi2, 1, 2, 4)
+        group_x(nc.vector.tensor_copy, x_hi2[:, :, 0 : P // 2, :], x_part[0], 2, 4)
+        group_x(nc.vector.tensor_copy, x_lo2[:, :, P // 2 : P, :], x_part[1], 0, 2)
+        group_x(nc.vector.tensor_copy, x_hi2[:, :, P // 2 : P, :], x_part[1], 2, 4)
+        quantize_x(x_lo2[:], 1, 0, 2)
+        quantize_x(x_hi2[:], 1, 2, 4)
 
         TILES = PASSES * PACK
-        prob = [keep.tile([P, N], F32, name=f"prob{u}") for u in range(TILES)]
+        prob = [keep.tile([P, PACK, N], F32, name=f"prob{g}") for g in range(PASSES)]
         q = [keep.tile([P, PACK, N], F32, name=f"q{g}", align_bytes=64) for g in range(PASSES)]
         squares_v = [keep.tile([P, N], BF16, name=f"squares_v{h}") for h in range(2)]
         squares_s = [keep.tile([P, N], BF16, name=f"squares_s{h}") for h in range(2)]
@@ -133,16 +147,17 @@ def tile_attend_gnce_w_clip_kernel(tc, xT, wT, y, wt, xn, xm, offs, out):
                 out=a[:], lhsT=x_codes[g][:, cols].bitcast(E4M3), lhsT_scale=x_scales[g][:, cols],
                 rhs=w_codes[:].bitcast(E4M3), rhs_scale=w_scales[:], start=True, stop=True,
             )
-            nc.scalar.activation(prob[u][:], a[:], ACT.Sigmoid, bias=zero[:])
+            nc.scalar.activation(prob[g][:, t, :], a[:], ACT.Sigmoid, bias=zero[:])
 
         nc.vector.reciprocal(inv_sq[:], rel_sq[:])
         rel_len = keep.tile([P, TILES], F32, name="rel_len", tag="column")
         nc.scalar.activation(rel_len[:], inv_sq[:].rearrange("p g t -> p (g t)"), ACT.Abs_reciprocal_sqrt)
         ratio = keep.tile([P, TILES], F32, name="ratio", tag="after_factor", align_bytes=64)
 
-        def residual(u):
+        def residual(u, count):
             g, t = divmod(u, PACK)
-            nc.vector.tensor_tensor(q[g][:, t, :], prob[u][:], y_raw[g][:, t, :], ALU.subtract)
+            rows = slice(t, t + count)
+            nc.vector.tensor_tensor(q[g][:, rows, :], prob[g][:, rows, :], y_raw[g][:, rows, :], ALU.subtract)
 
         def square_on_vector(u):
             g, t = divmod(u, PACK)
@@ -180,21 +195,24 @@ def tile_attend_gnce_w_clip_kernel(tc, xT, wT, y, wt, xn, xm, offs, out):
                 out=g_codes[g][:, cols].bitcast(E5M2), scales=g_scales[g][:, cols], in_=src[:].rearrange("p n t -> p (n t)")
             )
 
-        residual(0)
-        residual(1)
-        for u in range(ON_VECTOR):
-            residual(u + 2)
-            square_on_vector(u)
-        for u in range(ON_VECTOR + 2, TILES):
-            residual(u)
+        residual(0, 2)
+        residual(2, 2)
+        square_on_vector(0)
+        residual(4, 2)
+        square_on_vector(1)
+        square_on_vector(2)
+        residual(6, 1)
+        square_on_vector(3)
+        residual(7, 1)
         for j, tag in ((2, "stage"), (3, "x_hi")):
             late = keep.tile([P, T], F32, name=f"wide{j}", tag=tag, align_bytes=64)
             nc.gpsimd.memset(late[:], 0.0)
             wide.append(late)
-        for u in range(ON_VECTOR, TILES):
+        for u in range(ON_VECTOR, TILES - 1):
             square_on_scalar(u)
-            if u % PACK == PACK - 1:
-                row_ratio(u // PACK)
+        row_ratio(0)
+        square_on_scalar(TILES - 1)
+        row_ratio(1)
 
         xm_codes = [keep.tile([P, PASSES, P], U32, name=f"xm_codes{j}", align_bytes=64) for j in range(D // P)]
         xm_scales = [keep.tile([P, PASSES, P], U8, name=f"xm_scales{j}", align_bytes=64) for j in range(D // P)]

@@ -23,6 +23,7 @@ PASSES = R // PASS
 RUN = 4
 ON_VECTOR = 4
 HALF = N // 2
+WINDOWS = 3
 TINY = 2.0**-60
 
 
@@ -54,28 +55,28 @@ def tile_attend_gnce_w_clip_kernel(tc, xT, wT, y, wt, xn, xm, offs, out):
         nc.sync.dma_start(out=x_raw[:], in_=xT_planes[:, :, 0:PASS])
         for h in range(2):
             nc.sync.dma_start(out=x_part[h][:], in_=xT_planes[:, :, PASS + h * PASS // 2 : PASS + (h + 1) * PASS // 2])
-        nc.sync.dma_start(out=sq_len[:], in_=xn[0].rearrange("(g p t) o -> p g (t o)", p=P, t=PACK))
-        nc.sync.dma_start(out=weight[:], in_=wt[0].rearrange("(g p t) o -> p g (t o)", p=P, t=PACK))
         for g in range(PASSES):
             for h in range(2):
                 nc.sync.dma_start(out=y_raw[g][:, 2 * h : 2 * h + 2, :], in_=y_rows[g][:, 2 * h : 2 * h + 2, :])
+                if g == 0 and h == 0:
+                    nc.sync.dma_start(out=sq_len[:], in_=xn[0].rearrange("(g p t) o -> p g (t o)", p=P, t=PACK))
+        nc.sync.dma_start(out=weight[:], in_=wt[0].rearrange("(g p t) o -> p g (t o)", p=P, t=PACK))
         for h in range(2):
             for g in range(PASSES):
                 nc.sync.dma_start(out=xm_raw[h][:, g], in_=xm_rows[g][:, :, h * D // 2 : (h + 1) * D // 2])
 
         zero = keep.tile([P, 1], F32, name="zero", tag="column")
         tiny = keep.tile([P, 1], F32, name="tiny")
-        nc.gpsimd.memset(zero[:], 0.0)
-        nc.gpsimd.memset(tiny[:], TINY)
+        nc.vector.memset(zero[:], 0.0)
+        nc.vector.memset(tiny[:], TINY)
         warm = keep.tile([P, 1], F32, name="warm")
         nc.scalar.activation(warm[:], tiny[:], ACT.Sigmoid)
 
-        wide = [keep.tile([P, T], F32, name=f"wide{j}") for j in range(2)]
-        for j in range(2):
+        wide = [keep.tile([P, T], F32, name=f"wide{j}") for j in range(WINDOWS)]
+        for j in range(WINDOWS):
             nc.vector.memset(wide[j][:], 0.0)
 
         rel_sq = keep.tile([P, PASSES, PACK], F32, name="rel_sq")
-        nc.gpsimd.tensor_scalar(rel_sq[:], sq_len[:], 1.0 / (CLIP * CLIP), TINY, ALU.mult, ALU.add)
         inv_sq = keep.tile([P, PASSES, PACK], F32, name="inv_sq")
 
         w_bf = keep.tile([P, N, PACK], BF16, name="w_bf", tag="stage", align_bytes=64)
@@ -149,9 +150,7 @@ def tile_attend_gnce_w_clip_kernel(tc, xT, wT, y, wt, xn, xm, offs, out):
             )
             nc.scalar.activation(prob[g][:, t, :], a[:], ACT.Sigmoid, bias=zero[:])
 
-        nc.vector.reciprocal(inv_sq[:], rel_sq[:])
         rel_len = keep.tile([P, TILES], F32, name="rel_len", tag="column")
-        nc.scalar.activation(rel_len[:], inv_sq[:].rearrange("p g t -> p (g t)"), ACT.Abs_reciprocal_sqrt)
         ratio = keep.tile([P, TILES], F32, name="ratio", tag="after_factor", align_bytes=64)
 
         def residual(u, count):
@@ -196,7 +195,10 @@ def tile_attend_gnce_w_clip_kernel(tc, xT, wT, y, wt, xn, xm, offs, out):
             )
 
         residual(0, 2)
+        nc.vector.tensor_scalar(rel_sq[:], sq_len[:], 1.0 / (CLIP * CLIP), TINY, ALU.mult, ALU.add)
         residual(2, 2)
+        nc.vector.reciprocal(inv_sq[:], rel_sq[:])
+        nc.scalar.activation(rel_len[:], inv_sq[:].rearrange("p g t -> p (g t)"), ACT.Abs_reciprocal_sqrt)
         square_on_vector(0)
         residual(4, 2)
         square_on_vector(1)
@@ -204,10 +206,6 @@ def tile_attend_gnce_w_clip_kernel(tc, xT, wT, y, wt, xn, xm, offs, out):
         residual(6, 1)
         square_on_vector(3)
         residual(7, 1)
-        for j, tag in ((2, "stage"), (3, "x_hi")):
-            late = keep.tile([P, T], F32, name=f"wide{j}", tag=tag, align_bytes=64)
-            nc.gpsimd.memset(late[:], 0.0)
-            wide.append(late)
         for u in range(ON_VECTOR, TILES - 1):
             square_on_scalar(u)
         row_ratio(0)
@@ -249,10 +247,10 @@ def tile_attend_gnce_w_clip_kernel(tc, xT, wT, y, wt, xn, xm, offs, out):
 
         def place(j, dense, first_slot):
             count = dense.shape[1]
-            nc.vector.tensor_copy(out=wide[j][:].indirect(offsets[:, first_slot // 16 : (first_slot + count) // 16]), in_=dense[:])
+            nc.vector.tensor_copy(out=wide[j % WINDOWS][:].indirect(offsets[:, first_slot // 16 : (first_slot + count) // 16]), in_=dense[:])
 
         def store(j):
-            nc.sync.dma_start(out=out[j * P : (j + 1) * P, :], in_=wide[j][:])
+            nc.sync.dma_start(out=out[j * P : (j + 1) * P, :], in_=wide[j % WINDOWS][:])
 
         g_early = [keep.tile([P, HALF, PACK], BF16, name=f"g_early{g}", align_bytes=64) for g in range(PASSES)]
         row_factor(0)

@@ -21,9 +21,10 @@ PACK = 4
 PASS = P * PACK
 PASSES = R // PASS
 RUN = 4
-ON_VECTOR = 4
+ON_VECTOR = 3
 HALF = N // 2
 WINDOWS = 3
+AHEAD = 64
 TINY = 2.0**-60
 
 
@@ -180,18 +181,18 @@ def tile_attend_gnce_w_clip_kernel(tc, xT, wT, y, wt, xn, xm, offs, out):
         def slots(h):
             return slice(h * HALF, (h + 1) * HALF)
 
-        def gradient(dst, g, h):
+        def gradient(dst, g, h, first=0, count=HALF):
             nc.vector.tensor_tensor(
-                dst[:].rearrange("p (c i) t -> p c t i", i=RUN),
-                q[g][:, :, slots(h)].rearrange("p t (c i) -> p c t i", i=RUN),
-                factor[g][:].unsqueeze(1).unsqueeze(3).to_broadcast([P, HALF // RUN, PACK, RUN]),
+                dst[:, first : first + count, :].rearrange("p (c i) t -> p c t i", i=RUN),
+                q[g][:, :, h * HALF + first : h * HALF + first + count].rearrange("p t (c i) -> p c t i", i=RUN),
+                factor[g][:].unsqueeze(1).unsqueeze(3).to_broadcast([P, count // RUN, PACK, RUN]),
                 ALU.mult,
             )
 
         def quantize_g(src, g, h):
             cols = slots(h + 1)
             nc.vector.quantize_mx(
-                out=g_codes[g][:, cols].bitcast(E5M2), scales=g_scales[g][:, cols], in_=src[:].rearrange("p n t -> p (n t)")
+                out=g_codes[g][:, cols].bitcast(E5M2), scales=g_scales[g][:, cols], in_=src.rearrange("p n t -> p (n t)")
             )
 
         residual(0, 2)
@@ -203,13 +204,11 @@ def tile_attend_gnce_w_clip_kernel(tc, xT, wT, y, wt, xn, xm, offs, out):
         residual(4, 2)
         square_on_vector(1)
         square_on_vector(2)
-        residual(6, 1)
-        square_on_vector(3)
-        residual(7, 1)
-        for u in range(ON_VECTOR, TILES - 1):
+        residual(6, 2)
+        for u in range(ON_VECTOR, TILES):
             square_on_scalar(u)
-        row_ratio(0)
-        square_on_scalar(TILES - 1)
+            if u == PACK:
+                row_ratio(0)
         row_ratio(1)
 
         xm_codes = [keep.tile([P, PASSES, P], U32, name=f"xm_codes{j}", align_bytes=64) for j in range(D // P)]
@@ -252,19 +251,30 @@ def tile_attend_gnce_w_clip_kernel(tc, xT, wT, y, wt, xn, xm, offs, out):
         def store(j):
             nc.sync.dma_start(out=out[j * P : (j + 1) * P, :], in_=wide[j % WINDOWS][:])
 
-        g_early = [keep.tile([P, HALF, PACK], BF16, name=f"g_early{g}", align_bytes=64) for g in range(PASSES)]
+        g_first = keep.tile([P, HALF, PACK], BF16, name="g_first", align_bytes=64)
+        g_shared = keep.tile([P, AHEAD + HALF, PACK], BF16, name="g_shared", align_bytes=64)
+        g_early = [g_first[:], g_shared[:, AHEAD : AHEAD + HALF, :]]
+        g_late0 = g_shared[:, 0:HALF, :]
         row_factor(0)
         gradient(g_early[0], 0, 0)
+        gradient(g_late0, 0, 1, 0, AHEAD)
         row_factor(1)
         quantize_g(g_early[0], 0, 0)
-        gradient(g_early[1], 1, 0)
-        xm0 = group_xm(0, "after_ratio")
+        xm0 = keep.tile([P, PASSES, P, PACK], BF16, name="xm_bf0", tag="after_ratio", align_bytes=64)
+        for g in range(PASSES):
+            nc.scalar.copy(
+                out=xm0[:, g].rearrange("p (c i) t -> p c t i", i=RUN),
+                in_=xm_raw[0][:, g, :, 0:P].rearrange("p t (c i) -> p c t i", i=RUN),
+            )
         xm1 = group_xm(1, "after_factor")
-        quantize_xm(xm0, 0)
+        for g in range(PASSES):
+            gradient(g_early[1], 1, 0, g * HALF // 2, HALF // 2)
+            nc.vector.quantize_mx(
+                out=xm_codes[0][:, g, :].bitcast(E4M3), scales=xm_scales[0][:, g, :], in_=xm0[:, g].rearrange("p d t -> p (d t)")
+            )
         quantize_g(g_early[1], 1, 0)
         early0 = empty(product(0, 0, 0), HALF, "early0")
-        g_late0 = keep.tile([P, HALF, PACK], BF16, name="g_late0", tag="g_early1", align_bytes=64)
-        gradient(g_late0, 0, 1)
+        gradient(g_late0, 0, 1, AHEAD, HALF - AHEAD)
         quantize_xm(xm1, 1)
         quantize_g(g_late0, 0, 1)
         place(0, early0, 0)
@@ -276,7 +286,7 @@ def tile_attend_gnce_w_clip_kernel(tc, xT, wT, y, wt, xn, xm, offs, out):
         nc.scalar.copy(
             out=g_late1[:].rearrange("p (c i) t -> p c t i", i=RUN), in_=g_rows[:].rearrange("p t (c i) -> p c t i", i=RUN)
         )
-        quantize_g(g_late1, 1, 1)
+        quantize_g(g_late1[:], 1, 1)
         early1 = empty(product(1, 1, 0), HALF, "early1")
         place(1, early1, 0)
         late0 = empty(product(0, 2, HALF), HALF, "late0")

@@ -25,6 +25,7 @@ ON_VECTOR = 3
 HALF = N // 2
 WINDOWS = 3
 AHEAD = 64
+X_FIRST = 320
 TINY = 2.0**-60
 
 
@@ -42,7 +43,7 @@ def tile_attend_gnce_w_clip_kernel(tc, xT, wT, y, wt, xn, xm, offs, out):
         xm_rows = xm[0].rearrange("(g p t) d -> g p t d", p=P, t=PACK)
 
         x_raw = keep.tile([P, PACK, PASS], F32, name="x_raw")
-        x_part = [keep.tile([P, PACK, PASS // 2], F32, name=f"x_part{h}") for h in range(2)]
+        x_part = [keep.tile([P, PACK, rows], F32, name=f"x_part{h}") for h, rows in enumerate((X_FIRST, PASS - X_FIRST))]
         w_raw = [keep.tile([P, T], F32, name=f"w_raw{j}") for j in range(PACK)]
         y_raw = [keep.tile([P, PACK, N], F32, name=f"y_raw{g}") for g in range(PASSES)]
         xm_raw = [keep.tile([P, PASSES, PACK, D // 2], F32, name=f"xm_raw{h}") for h in range(2)]
@@ -54,8 +55,8 @@ def tile_attend_gnce_w_clip_kernel(tc, xT, wT, y, wt, xn, xm, offs, out):
             if j == 0:
                 nc.sync.dma_start(offsets[:], offs)
         nc.sync.dma_start(out=x_raw[:], in_=xT_planes[:, :, 0:PASS])
-        for h in range(2):
-            nc.sync.dma_start(out=x_part[h][:], in_=xT_planes[:, :, PASS + h * PASS // 2 : PASS + (h + 1) * PASS // 2])
+        nc.sync.dma_start(out=x_part[0][:], in_=xT_planes[:, :, PASS : PASS + X_FIRST])
+        nc.sync.dma_start(out=x_part[1][:], in_=xT_planes[:, :, PASS + X_FIRST : R])
         for g in range(PASSES):
             for h in range(2):
                 nc.sync.dma_start(out=y_raw[g][:, 2 * h : 2 * h + 2, :], in_=y_rows[g][:, 2 * h : 2 * h + 2, :])
@@ -119,13 +120,14 @@ def tile_attend_gnce_w_clip_kernel(tc, xT, wT, y, wt, xn, xm, offs, out):
         quantize_x(x_lo[:, 0:1], 0, 0, 1)
         quantize_x(x_lo[:, 1:2], 0, 1, 2)
         x_lo2 = keep.tile([P, 2, P, PACK], BF16, name="x_lo2", tag="stage", align_bytes=64)
-        group_x(nc.vector.tensor_copy, x_lo2[:, :, 0 : P // 2, :], x_part[0], 0, 2)
+        group_x(nc.vector.tensor_copy, x_lo2[:, :, 0 : X_FIRST // PACK, :], x_part[0], 0, 2)
         quantize_x(x_hi[:], 0, 2, 4)
         x_hi2 = keep.tile([P, 2, P, PACK], BF16, name="x_hi2", tag="x_hi", align_bytes=64)
-        group_x(nc.vector.tensor_copy, x_hi2[:, :, 0 : P // 2, :], x_part[0], 2, 4)
-        group_x(nc.vector.tensor_copy, x_lo2[:, :, P // 2 : P, :], x_part[1], 0, 2)
-        group_x(nc.vector.tensor_copy, x_hi2[:, :, P // 2 : P, :], x_part[1], 2, 4)
-        quantize_x(x_lo2[:], 1, 0, 2)
+        group_x(nc.vector.tensor_copy, x_hi2[:, :, 0 : X_FIRST // PACK, :], x_part[0], 2, 4)
+        group_x(nc.vector.tensor_copy, x_lo2[:, :, X_FIRST // PACK : P, :], x_part[1], 0, 2)
+        group_x(nc.vector.tensor_copy, x_hi2[:, :, X_FIRST // PACK : P, :], x_part[1], 2, 4)
+        quantize_x(x_lo2[:, 0:1], 1, 0, 1)
+        quantize_x(x_lo2[:, 1:2], 1, 1, 2)
         quantize_x(x_hi2[:], 1, 2, 4)
 
         TILES = PASSES * PACK
@@ -203,12 +205,18 @@ def tile_attend_gnce_w_clip_kernel(tc, xT, wT, y, wt, xn, xm, offs, out):
         square_on_vector(0)
         residual(4, 2)
         square_on_vector(1)
-        square_on_vector(2)
+        nc.vector.scalar_tensor_tensor(
+            squares_v[0][:, 0:HALF], q[0][:, 3, 0:HALF], rel_sq[:, 0, 3:4], q[0][:, 3, 0:HALF], ALU.mult, ALU.mult, accum_out=sum_sq[:, 3:4]
+        )
         residual(6, 2)
-        for u in range(ON_VECTOR, TILES):
+        rest_sq = keep.tile([P, 1], F32, name="rest_sq")
+        nc.scalar.activation(squares_s[1][:, 0:HALF], q[0][:, 3, HALF:N], ACT.Square, accum_out=rest_sq[:])
+        square_on_scalar(2)
+        square_on_scalar(4)
+        nc.scalar.activation(ratio[:, 0:3], sum_sq[:, 0:3], ACT.Abs_reciprocal_sqrt, bias=tiny[:])
+        nc.scalar.activation(ratio[:, 3:4], rest_sq[:], ACT.Abs_reciprocal_sqrt, scale=rel_sq[:, 0, 3:4], bias=sum_sq[:, 3:4])
+        for u in range(PACK + 1, TILES):
             square_on_scalar(u)
-            if u == PACK:
-                row_ratio(0)
         row_ratio(1)
 
         xm_codes = [keep.tile([P, PASSES, P], U32, name=f"xm_codes{j}", align_bytes=64) for j in range(D // P)]

@@ -44,7 +44,7 @@ def tile_attend_gnce_w_clip_kernel(tc, xT, wT, y, wt, xn, xm, offs, out):
 
         x_raw = keep.tile([P, PACK, PASS], F32, name="x_raw")
         x_part = [keep.tile([P, PACK, rows], F32, name=f"x_part{h}") for h, rows in enumerate((X_FIRST, PASS - X_FIRST))]
-        w_raw = [keep.tile([P, T], F32, name=f"w_raw{j}") for j in range(PACK)]
+        w_raw = [keep.tile([P, T], F32, name=f"w_raw{j}", tag=f"w_raw{j}") for j in range(PACK)]
         y_raw = [keep.tile([P, PACK, N], F32, name=f"y_raw{g}") for g in range(PASSES)]
         xm_raw = [keep.tile([P, PASSES, PACK, D // 2], F32, name=f"xm_raw{h}") for h in range(2)]
         weight = keep.tile([P, PASSES, PACK], F32, name="weight")
@@ -91,6 +91,8 @@ def tile_attend_gnce_w_clip_kernel(tc, xT, wT, y, wt, xn, xm, offs, out):
                 out=w_bf[:, h * HALF : (h + 1) * HALF, PACK - 1],
                 in_=w_raw[PACK - 1][:].indirect(offsets[:, h * HALF // 16 : (h + 1) * HALF // 16]),
             )
+        wide.append(keep.tile([P, T], F32, name="wide3", tag="w_raw0"))
+        nc.gpsimd.memset(wide[WINDOWS][:], 0.0)
         for h in range(2):
             cols = slice(h * HALF, (h + 1) * HALF)
             nc.vector.quantize_mx(
@@ -137,11 +139,8 @@ def tile_attend_gnce_w_clip_kernel(tc, xT, wT, y, wt, xn, xm, offs, out):
         squares_s = [keep.tile([P, N], BF16, name=f"squares_s{h}") for h in range(2)]
         sum_sq = keep.tile([P, TILES], F32, name="sum_sq", tag="after_ratio", align_bytes=64)
         factor = [keep.tile([P, PACK], F32, name=f"factor{g}") for g in range(PASSES)]
-        g_codes = [keep.tile([P, HALF + N], U32, name=f"g_codes{g}", align_bytes=64) for g in range(PASSES)]
-        g_scales = [keep.tile([P, HALF + N], U8, name=f"g_scales{g}", align_bytes=64) for g in range(PASSES)]
-        for g in range(PASSES):
-            nc.vector.memset(g_codes[g][:, 0:HALF], 0)
-            nc.vector.memset(g_scales[g][:, 0:HALF].bitcast(U32), 0)
+        g_codes = [keep.tile([P, N], U32, name=f"g_codes{g}", align_bytes=64) for g in range(PASSES)]
+        g_scales = [keep.tile([P, N], U8, name=f"g_scales{g}", align_bytes=64) for g in range(PASSES)]
 
         for u in range(TILES):
             g, t = divmod(u, PACK)
@@ -192,7 +191,7 @@ def tile_attend_gnce_w_clip_kernel(tc, xT, wT, y, wt, xn, xm, offs, out):
             )
 
         def quantize_g(src, g, h):
-            cols = slots(h + 1)
+            cols = slots(h)
             nc.vector.quantize_mx(
                 out=g_codes[g][:, cols].bitcast(E5M2), scales=g_scales[g][:, cols], in_=src.rearrange("p n t -> p (n t)")
             )
@@ -237,9 +236,9 @@ def tile_attend_gnce_w_clip_kernel(tc, xT, wT, y, wt, xn, xm, offs, out):
                 in_=src[:].rearrange("p g d t -> p (g d t)"),
             )
 
-        def product(j, bank, first):
-            dw = psum.tile([P, N], F32, name=f"bank{bank}")
-            cols = slice(first, first + N)
+        def product(j, bank, first, count):
+            dw = psum.tile([P, count], F32, name=f"bank{bank}")
+            cols = slice(first, first + count)
             for g in range(PASSES):
                 nc.tensor.matmul_mx(
                     out=dw[:], lhsT=xm_codes[j][:, g, :].bitcast(E4M3), lhsT_scale=xm_scales[j][:, g, :],
@@ -247,22 +246,28 @@ def tile_attend_gnce_w_clip_kernel(tc, xT, wT, y, wt, xn, xm, offs, out):
                 )
             return dw
 
-        def empty(dw, first, name):
-            dense = keep.tile([P, N - first], F32, name=name, align_bytes=64)
-            nc.scalar.copy(out=dense[:], in_=dw[:, first:N])
+        def empty(copy, dw, name):
+            dense = keep.tile([P, dw.shape[1]], F32, name=name, align_bytes=64)
+            copy(out=dense[:], in_=dw[:])
             return dense
 
-        def place(j, dense, first_slot):
-            count = dense.shape[1]
-            nc.vector.tensor_copy(out=wide[j % WINDOWS][:].indirect(offsets[:, first_slot // 16 : (first_slot + count) // 16]), in_=dense[:])
+        def places(j, h):
+            return wide[j][:].indirect(offsets[:, h * HALF // 16 : (h + 1) * HALF // 16])
+
+        def place_on_vector(j, h, dense):
+            nc.vector.tensor_copy(out=places(j, h), in_=dense)
+
+        def place_on_scalar(j, h, dense):
+            nc.scalar.activation(places(j, h), dense, ACT.Copy)
 
         def store(j):
-            nc.sync.dma_start(out=out[j * P : (j + 1) * P, :], in_=wide[j % WINDOWS][:])
+            nc.sync.dma_start(out=out[j * P : (j + 1) * P, :], in_=wide[j][:])
 
         g_first = keep.tile([P, HALF, PACK], BF16, name="g_first", align_bytes=64)
         g_shared = keep.tile([P, AHEAD + HALF, PACK], BF16, name="g_shared", align_bytes=64)
         g_early = [g_first[:], g_shared[:, AHEAD : AHEAD + HALF, :]]
         g_late0 = g_shared[:, 0:HALF, :]
+        g_late1 = keep.tile([P, HALF, PACK], BF16, name="g_late1", tag="g_first", align_bytes=64)
         row_factor(0)
         gradient(g_early[0], 0, 0)
         gradient(g_late0, 0, 1, 0, AHEAD)
@@ -281,32 +286,30 @@ def tile_attend_gnce_w_clip_kernel(tc, xT, wT, y, wt, xn, xm, offs, out):
                 out=xm_codes[0][:, g, :].bitcast(E4M3), scales=xm_scales[0][:, g, :], in_=xm0[:, g].rearrange("p d t -> p (d t)")
             )
         quantize_g(g_early[1], 1, 0)
-        early0 = empty(product(0, 0, 0), HALF, "early0")
+        early0 = empty(nc.scalar.copy, product(0, 0, 0, HALF), "early0")
+        place_on_scalar(0, 0, early0[:])
         gradient(g_late0, 0, 1, AHEAD, HALF - AHEAD)
         quantize_xm(xm1, 1)
         quantize_g(g_late0, 0, 1)
-        place(0, early0, 0)
-
-        g_rows = keep.tile([P, PACK, HALF], BF16, name="g_rows", tag="after_ratio", align_bytes=64)
-        g_late1 = keep.tile([P, HALF, PACK], BF16, name="g_late1", align_bytes=64)
-        for t in range(PACK):
-            nc.scalar.activation(g_rows[:, t, :], q[1][:, t, slots(1)], ACT.Copy, scale=factor[1][:, t : t + 1])
-        nc.scalar.copy(
-            out=g_late1[:].rearrange("p (c i) t -> p c t i", i=RUN), in_=g_rows[:].rearrange("p t (c i) -> p c t i", i=RUN)
-        )
-        quantize_g(g_late1[:], 1, 1)
-        early1 = empty(product(1, 1, 0), HALF, "early1")
-        place(1, early1, 0)
-        late0 = empty(product(0, 2, HALF), HALF, "late0")
-        late1 = empty(product(1, 3, HALF), HALF, "late1")
+        gradient(g_late1[:], 1, 1)
+        early1 = empty(nc.scalar.copy, product(1, 1, 0, HALF), "early1")
+        place_on_scalar(1, 0, early1[:])
         xm2 = group_xm(2, "after_ratio")
-        xm3 = group_xm(3, "early1")
-        place(0, late0, HALF)
-        store(0)
+        quantize_g(g_late1[:], 1, 1)
         quantize_xm(xm2, 2)
-        place(1, late1, HALF)
+        late0 = empty(nc.vector.tensor_copy, product(0, 2, HALF, HALF), "late0")
+        place_on_vector(0, 1, late0[:])
+        store(0)
+        xm3 = group_xm(3, "early1")
+        late1 = empty(nc.scalar.copy, product(1, 3, HALF, HALF), "late1")
+        place_on_scalar(1, 1, late1[:])
         store(1)
+        dense2 = empty(nc.vector.tensor_copy, product(2, 4, 0, N), "dense2")
         quantize_xm(xm3, 3)
-        for j in (2, 3):
-            place(j, empty(product(j, 2 + j, HALF), 0, f"dense{j}"), 0)
-            store(j)
+        for h in range(2):
+            place_on_vector(2, h, dense2[:, slots(h)])
+        store(2)
+        dense3 = empty(nc.scalar.copy, product(3, 5, 0, N), "dense3")
+        for h in range(2):
+            place_on_scalar(3, h, dense3[:, slots(h)])
+        store(3)

@@ -221,13 +221,14 @@ def tile_attend_gnce_w_clip_kernel(tc, xT, wT, y, wt, xn, xm, offs, out):
         xm_codes = [keep.tile([P, PASSES, P], U32, name=f"xm_codes{j}", align_bytes=64) for j in range(D // P)]
         xm_scales = [keep.tile([P, PASSES, P], U8, name=f"xm_scales{j}", align_bytes=64) for j in range(D // P)]
 
-        def group_xm(j, tag):
-            dst = keep.tile([P, PASSES, P, PACK], BF16, name=f"xm_bf{j}", tag=tag, align_bytes=64)
-            nc.scalar.copy(
-                out=dst[:].rearrange("p g (c i) t -> p g c t i", i=RUN),
-                in_=xm_raw[j // 2][:, :, :, (j % 2) * P : (j % 2 + 1) * P].rearrange("p g t (c i) -> p g c t i", i=RUN),
+        def xm_tile(j, tag):
+            return keep.tile([P, PASSES, P, PACK], BF16, name=f"xm_bf{j}", tag=tag, align_bytes=64)
+
+        def group_xm(copy, dst, j, g):
+            copy(
+                out=dst[:, g].rearrange("p (c i) t -> p c t i", i=RUN),
+                in_=xm_raw[j // 2][:, g, :, (j % 2) * P : (j % 2 + 1) * P].rearrange("p t (c i) -> p c t i", i=RUN),
             )
-            return dst
 
         def quantize_xm(src, j):
             nc.vector.quantize_mx(
@@ -244,11 +245,11 @@ def tile_attend_gnce_w_clip_kernel(tc, xT, wT, y, wt, xn, xm, offs, out):
                     out=dw[:], lhsT=xm_codes[j][:, g, :].bitcast(E4M3), lhsT_scale=xm_scales[j][:, g, :],
                     rhs=g_codes[g][:, cols].bitcast(E5M2), rhs_scale=g_scales[g][:, cols], start=(g == 0), stop=(g == PASSES - 1),
                 )
-            return dw
+            return dw[:]
 
         def empty(copy, dw, name):
             dense = keep.tile([P, dw.shape[1]], F32, name=name, align_bytes=64)
-            copy(out=dense[:], in_=dw[:])
+            copy(out=dense[:], in_=dw)
             return dense
 
         def places(j, h):
@@ -263,53 +264,50 @@ def tile_attend_gnce_w_clip_kernel(tc, xT, wT, y, wt, xn, xm, offs, out):
         def store(j):
             nc.sync.dma_start(out=out[j * P : (j + 1) * P, :], in_=wide[j][:])
 
-        g_first = keep.tile([P, HALF, PACK], BF16, name="g_first", align_bytes=64)
-        g_shared = keep.tile([P, AHEAD + HALF, PACK], BF16, name="g_shared", align_bytes=64)
-        g_early = [g_first[:], g_shared[:, AHEAD : AHEAD + HALF, :]]
-        g_late0 = g_shared[:, 0:HALF, :]
-        g_late1 = keep.tile([P, HALF, PACK], BF16, name="g_late1", tag="g_first", align_bytes=64)
+        g_bf = [[keep.tile([P, HALF, PACK], BF16, name=f"g_bf{g}{h}", align_bytes=64) for h in range(2)] for g in range(PASSES)]
+        xm0 = xm_tile(0, "xm_bf0")
+        for g in range(PASSES):
+            group_xm(nc.vector.tensor_copy, xm0, 0, g)
         row_factor(0)
-        gradient(g_early[0], 0, 0)
-        gradient(g_late0, 0, 1, 0, AHEAD)
+        quantize_xm(xm0, 0)
+        gradient(g_bf[0][0][:], 0, 0)
+        gradient(g_bf[0][1][:], 0, 1, 0, AHEAD)
         row_factor(1)
-        quantize_g(g_early[0], 0, 0)
-        xm0 = keep.tile([P, PASSES, P, PACK], BF16, name="xm_bf0", tag="after_ratio", align_bytes=64)
+        quantize_g(g_bf[0][0][:], 0, 0)
+        xm1 = xm_tile(1, "after_ratio")
+        xm2 = xm_tile(2, "after_factor")
+        xm3 = xm_tile(3, "xm_bf3")
         for g in range(PASSES):
-            nc.scalar.copy(
-                out=xm0[:, g].rearrange("p (c i) t -> p c t i", i=RUN),
-                in_=xm_raw[0][:, g, :, 0:P].rearrange("p t (c i) -> p c t i", i=RUN),
-            )
-        xm1 = group_xm(1, "after_factor")
+            group_xm(nc.scalar.copy, xm1, 1, g)
         for g in range(PASSES):
-            gradient(g_early[1], 1, 0, g * HALF // 2, HALF // 2)
-            nc.vector.quantize_mx(
-                out=xm_codes[0][:, g, :].bitcast(E4M3), scales=xm_scales[0][:, g, :], in_=xm0[:, g].rearrange("p d t -> p (d t)")
-            )
-        quantize_g(g_early[1], 1, 0)
+            group_xm(nc.scalar.copy, xm2, 2, g)
+        gradient(g_bf[1][0][:], 1, 0)
+        gradient(g_bf[1][1][:], 1, 1, 0, AHEAD)
+        quantize_g(g_bf[1][0][:], 1, 0)
         early0 = empty(nc.scalar.copy, product(0, 0, 0, HALF), "early0")
         place_on_scalar(0, 0, early0[:])
-        gradient(g_late0, 0, 1, AHEAD, HALF - AHEAD)
-        quantize_xm(xm1, 1)
-        quantize_g(g_late0, 0, 1)
-        gradient(g_late1[:], 1, 1)
-        early1 = empty(nc.scalar.copy, product(1, 1, 0, HALF), "early1")
-        place_on_scalar(1, 0, early1[:])
-        xm2 = group_xm(2, "after_ratio")
-        quantize_g(g_late1[:], 1, 1)
-        quantize_xm(xm2, 2)
-        late0 = empty(nc.vector.tensor_copy, product(0, 2, HALF, HALF), "late0")
-        place_on_vector(0, 1, late0[:])
+        gradient(g_bf[0][1][:], 0, 1, AHEAD, HALF - AHEAD)
+        gradient(g_bf[1][1][:], 1, 1, AHEAD, HALF - AHEAD)
+        quantize_g(g_bf[0][1][:], 0, 1)
+        quantize_g(g_bf[1][1][:], 1, 1)
+        late0 = empty(nc.scalar.copy, product(0, 1, HALF, HALF), "late0")
+        place_on_scalar(0, 1, late0[:])
         store(0)
-        xm3 = group_xm(3, "early1")
-        late1 = empty(nc.scalar.copy, product(1, 3, HALF, HALF), "late1")
-        place_on_scalar(1, 1, late1[:])
-        store(1)
-        dense2 = empty(nc.vector.tensor_copy, product(2, 4, 0, N), "dense2")
+        quantize_xm(xm1, 1)
+        sums1 = product(1, 2, 0, N)
+        group_xm(nc.scalar.copy, xm3, 3, 0)
+        group_xm(nc.vector.tensor_copy, xm3, 3, 1)
+        quantize_xm(xm2, 2)
         quantize_xm(xm3, 3)
+        dense1 = empty(nc.vector.tensor_copy, sums1, "dense1")
+        dense2 = empty(nc.scalar.copy, product(2, 3, 0, N), "dense2")
+        dense3 = empty(nc.scalar.copy, product(3, 4, 0, N), "dense3")
         for h in range(2):
-            place_on_vector(2, h, dense2[:, slots(h)])
-        store(2)
-        dense3 = empty(nc.scalar.copy, product(3, 5, 0, N), "dense3")
+            place_on_vector(1, h, dense1[:, slots(h)])
+        store(1)
         for h in range(2):
             place_on_scalar(3, h, dense3[:, slots(h)])
         store(3)
+        for h in range(2):
+            place_on_vector(2, h, dense2[:, slots(h)])
+        store(2)

@@ -26,6 +26,7 @@ HALF = N // 2
 WINDOWS = 3
 AHEAD = 64
 X_FIRST = 320
+ON_SCALAR = 96
 TINY = 2.0**-60
 
 
@@ -255,8 +256,8 @@ def tile_attend_gnce_w_clip_kernel(tc, xT, wT, y, wt, xn, xm, offs, out):
         def places(j, h):
             return wide[j][:].indirect(offsets[:, h * HALF // 16 : (h + 1) * HALF // 16])
 
-        def place_on_vector(j, h, dense):
-            nc.vector.tensor_copy(out=places(j, h), in_=dense)
+        def place_on_vector(j, dense):
+            nc.vector.tensor_copy(out=wide[j][:].indirect(offsets[:]), in_=dense)
 
         def place_on_scalar(j, h, dense):
             nc.scalar.activation(places(j, h), dense, ACT.Copy)
@@ -275,39 +276,47 @@ def tile_attend_gnce_w_clip_kernel(tc, xT, wT, y, wt, xn, xm, offs, out):
         row_factor(1)
         quantize_g(g_bf[0][0][:], 0, 0)
         xm1 = xm_tile(1, "after_ratio")
-        xm2 = xm_tile(2, "after_factor")
         xm3 = xm_tile(3, "xm_bf3")
         for g in range(PASSES):
             group_xm(nc.scalar.copy, xm1, 1, g)
+        rest = HALF - ON_SCALAR
+        g_rows = keep.tile([P, PACK, ON_SCALAR], BF16, name="g_rows", tag="after_factor", align_bytes=64)
+        for t in range(PACK):
+            nc.scalar.activation(g_rows[:, t, :], q[0][:, t, HALF + rest : N], ACT.Copy, scale=factor[0][:, t : t + 1])
+        nc.scalar.copy(
+            out=g_bf[0][1][:, rest:HALF, :].rearrange("p (c i) t -> p c t i", i=RUN),
+            in_=g_rows[:].rearrange("p t (c i) -> p c t i", i=RUN),
+        )
+        xm2 = xm_tile(2, "after_factor")
         for g in range(PASSES):
             group_xm(nc.scalar.copy, xm2, 2, g)
         gradient(g_bf[1][0][:], 1, 0)
-        gradient(g_bf[1][1][:], 1, 1, 0, AHEAD)
+        quantize_xm(xm1, 1)
         quantize_g(g_bf[1][0][:], 1, 0)
         early0 = empty(nc.scalar.copy, product(0, 0, 0, HALF), "early0")
         place_on_scalar(0, 0, early0[:])
-        gradient(g_bf[0][1][:], 0, 1, AHEAD, HALF - AHEAD)
-        gradient(g_bf[1][1][:], 1, 1, AHEAD, HALF - AHEAD)
+        sums1 = [product(1, 1, 0, HALF)]
+        gradient(g_bf[0][1][:], 0, 1, AHEAD, rest - AHEAD)
+        gradient(g_bf[1][1][:], 1, 1)
         quantize_g(g_bf[0][1][:], 0, 1)
         quantize_g(g_bf[1][1][:], 1, 1)
-        late0 = empty(nc.scalar.copy, product(0, 1, HALF, HALF), "late0")
+        late0 = empty(nc.scalar.copy, product(0, 2, HALF, HALF), "late0")
         place_on_scalar(0, 1, late0[:])
         store(0)
-        quantize_xm(xm1, 1)
-        sums1 = product(1, 2, 0, N)
-        group_xm(nc.scalar.copy, xm3, 3, 0)
-        group_xm(nc.vector.tensor_copy, xm3, 3, 1)
+        sums1.append(product(1, 3, HALF, HALF))
+        for g in range(PASSES):
+            group_xm(nc.vector.tensor_copy, xm3, 3, g)
         quantize_xm(xm2, 2)
         quantize_xm(xm3, 3)
-        dense1 = empty(nc.vector.tensor_copy, sums1, "dense1")
-        dense2 = empty(nc.scalar.copy, product(2, 3, 0, N), "dense2")
-        dense3 = empty(nc.scalar.copy, product(3, 4, 0, N), "dense3")
+        dense1 = keep.tile([P, N], F32, name="dense1", align_bytes=64)
         for h in range(2):
-            place_on_vector(1, h, dense1[:, slots(h)])
+            nc.vector.tensor_copy(out=dense1[:, slots(h)], in_=sums1[h])
+        place_on_vector(1, dense1[:])
         store(1)
+        dense2 = empty(nc.scalar.copy, product(2, 4, 0, N), "dense2")
         for h in range(2):
-            place_on_scalar(3, h, dense3[:, slots(h)])
-        store(3)
-        for h in range(2):
-            place_on_vector(2, h, dense2[:, slots(h)])
+            place_on_scalar(2, h, dense2[:, slots(h)])
         store(2)
+        dense3 = empty(nc.vector.tensor_copy, product(3, 5, 0, N), "dense1")
+        place_on_vector(3, dense3[:])
+        store(3)

@@ -24,9 +24,8 @@ RUN = 4
 ON_VECTOR = 3
 HALF = N // 2
 WINDOWS = 3
-AHEAD = 64
 X_FIRST = 320
-ON_SCALAR = 96
+ON_SCALAR = 128
 TINY = 2.0**-60
 
 
@@ -266,13 +265,11 @@ def tile_attend_gnce_w_clip_kernel(tc, xT, wT, y, wt, xn, xm, offs, out):
             nc.sync.dma_start(out=out[j * P : (j + 1) * P, :], in_=wide[j][:])
 
         g_bf = [[keep.tile([P, HALF, PACK], BF16, name=f"g_bf{g}{h}", align_bytes=64) for h in range(2)] for g in range(PASSES)]
+        row_factor(0)
+        gradient(g_bf[0][0][:], 0, 0)
         xm0 = xm_tile(0, "xm_bf0")
         for g in range(PASSES):
             group_xm(nc.vector.tensor_copy, xm0, 0, g)
-        row_factor(0)
-        quantize_xm(xm0, 0)
-        gradient(g_bf[0][0][:], 0, 0)
-        gradient(g_bf[0][1][:], 0, 1, 0, AHEAD)
         row_factor(1)
         quantize_g(g_bf[0][0][:], 0, 0)
         xm1 = xm_tile(1, "after_ratio")
@@ -291,12 +288,13 @@ def tile_attend_gnce_w_clip_kernel(tc, xT, wT, y, wt, xn, xm, offs, out):
         for g in range(PASSES):
             group_xm(nc.scalar.copy, xm2, 2, g)
         gradient(g_bf[1][0][:], 1, 0)
-        quantize_xm(xm1, 1)
+        quantize_xm(xm0, 0)
         quantize_g(g_bf[1][0][:], 1, 0)
         early0 = empty(nc.scalar.copy, product(0, 0, 0, HALF), "early0")
         place_on_scalar(0, 0, early0[:])
+        gradient(g_bf[0][1][:], 0, 1, 0, rest)
+        quantize_xm(xm1, 1)
         sums1 = [product(1, 1, 0, HALF)]
-        gradient(g_bf[0][1][:], 0, 1, AHEAD, rest - AHEAD)
         gradient(g_bf[1][1][:], 1, 1)
         quantize_g(g_bf[0][1][:], 0, 1)
         quantize_g(g_bf[1][1][:], 1, 1)

@@ -25,7 +25,7 @@ ON_VECTOR = 3
 HALF = N // 2
 WINDOWS = 3
 X_FIRST = 320
-ON_SCALAR = 128
+ON_SCALAR = 160
 TINY = 2.0**-60
 
 
@@ -46,7 +46,9 @@ def tile_attend_gnce_w_clip_kernel(tc, xT, wT, y, wt, xn, xm, offs, out):
         x_part = [keep.tile([P, PACK, rows], F32, name=f"x_part{h}") for h, rows in enumerate((X_FIRST, PASS - X_FIRST))]
         w_raw = [keep.tile([P, T], F32, name=f"w_raw{j}", tag=f"w_raw{j}") for j in range(PACK)]
         y_raw = [keep.tile([P, PACK, N], F32, name=f"y_raw{g}") for g in range(PASSES)]
-        xm_raw = [keep.tile([P, PASSES, PACK, D // 2], F32, name=f"xm_raw{h}") for h in range(2)]
+        xm_front = [keep.tile([P, PACK, D // 2], F32, name=f"xm_front{g}") for g in range(PASSES)]
+        xm_back = keep.tile([P, PASSES, PACK, D // 2], F32, name="xm_back")
+        xm_raw = [[xm_front[g][:] for g in range(PASSES)], [xm_back[:, g] for g in range(PASSES)]]
         weight = keep.tile([P, PASSES, PACK], F32, name="weight")
         sq_len = keep.tile([P, PASSES, PACK], F32, name="sq_len")
 
@@ -62,10 +64,11 @@ def tile_attend_gnce_w_clip_kernel(tc, xT, wT, y, wt, xn, xm, offs, out):
                 nc.sync.dma_start(out=y_raw[g][:, 2 * h : 2 * h + 2, :], in_=y_rows[g][:, 2 * h : 2 * h + 2, :])
                 if g == 0 and h == 0:
                     nc.sync.dma_start(out=sq_len[:], in_=xn[0].rearrange("(g p t) o -> p g (t o)", p=P, t=PACK))
-        nc.sync.dma_start(out=weight[:], in_=wt[0].rearrange("(g p t) o -> p g (t o)", p=P, t=PACK))
         for h in range(2):
             for g in range(PASSES):
-                nc.sync.dma_start(out=xm_raw[h][:, g], in_=xm_rows[g][:, :, h * D // 2 : (h + 1) * D // 2])
+                nc.sync.dma_start(out=xm_raw[h][g], in_=xm_rows[g][:, :, h * D // 2 : (h + 1) * D // 2])
+            if h == 0:
+                nc.sync.dma_start(out=weight[:], in_=wt[0].rearrange("(g p t) o -> p g (t o)", p=P, t=PACK))
 
         zero = keep.tile([P, 1], F32, name="zero", tag="column")
         tiny = keep.tile([P, 1], F32, name="tiny")
@@ -138,7 +141,7 @@ def tile_attend_gnce_w_clip_kernel(tc, xT, wT, y, wt, xn, xm, offs, out):
         squares_v = [keep.tile([P, N], BF16, name=f"squares_v{h}") for h in range(2)]
         squares_s = [keep.tile([P, N], BF16, name=f"squares_s{h}") for h in range(2)]
         sum_sq = keep.tile([P, TILES], F32, name="sum_sq", tag="after_ratio", align_bytes=64)
-        factor = [keep.tile([P, PACK], F32, name=f"factor{g}") for g in range(PASSES)]
+        factor = [keep.tile([P, PACK], F32, name=f"factor{g}", tag=("xm_front0", "factor1")[g]) for g in range(PASSES)]
         g_codes = [keep.tile([P, N], U32, name=f"g_codes{g}", align_bytes=64) for g in range(PASSES)]
         g_scales = [keep.tile([P, N], U8, name=f"g_scales{g}", align_bytes=64) for g in range(PASSES)]
 
@@ -204,17 +207,11 @@ def tile_attend_gnce_w_clip_kernel(tc, xT, wT, y, wt, xn, xm, offs, out):
         square_on_vector(0)
         residual(4, 2)
         square_on_vector(1)
-        nc.vector.scalar_tensor_tensor(
-            squares_v[0][:, 0:HALF], q[0][:, 3, 0:HALF], rel_sq[:, 0, 3:4], q[0][:, 3, 0:HALF], ALU.mult, ALU.mult, accum_out=sum_sq[:, 3:4]
-        )
         residual(6, 2)
-        rest_sq = keep.tile([P, 1], F32, name="rest_sq")
-        nc.scalar.activation(squares_s[1][:, 0:HALF], q[0][:, 3, HALF:N], ACT.Square, accum_out=rest_sq[:])
-        square_on_scalar(2)
-        square_on_scalar(4)
-        nc.scalar.activation(ratio[:, 0:3], sum_sq[:, 0:3], ACT.Abs_reciprocal_sqrt, bias=tiny[:])
-        nc.scalar.activation(ratio[:, 3:4], rest_sq[:], ACT.Abs_reciprocal_sqrt, scale=rel_sq[:, 0, 3:4], bias=sum_sq[:, 3:4])
-        for u in range(PACK + 1, TILES):
+        for u in range(2, PACK):
+            square_on_scalar(u)
+        row_ratio(0)
+        for u in range(PACK, TILES):
             square_on_scalar(u)
         row_ratio(1)
 
@@ -227,7 +224,7 @@ def tile_attend_gnce_w_clip_kernel(tc, xT, wT, y, wt, xn, xm, offs, out):
         def group_xm(copy, dst, j, g):
             copy(
                 out=dst[:, g].rearrange("p (c i) t -> p c t i", i=RUN),
-                in_=xm_raw[j // 2][:, g, :, (j % 2) * P : (j % 2 + 1) * P].rearrange("p t (c i) -> p c t i", i=RUN),
+                in_=xm_raw[j // 2][g][:, :, (j % 2) * P : (j % 2 + 1) * P].rearrange("p t (c i) -> p c t i", i=RUN),
             )
 
         def quantize_xm(src, j):
@@ -265,46 +262,47 @@ def tile_attend_gnce_w_clip_kernel(tc, xT, wT, y, wt, xn, xm, offs, out):
             nc.sync.dma_start(out=out[j * P : (j + 1) * P, :], in_=wide[j][:])
 
         g_bf = [[keep.tile([P, HALF, PACK], BF16, name=f"g_bf{g}{h}", align_bytes=64) for h in range(2)] for g in range(PASSES)]
-        row_factor(0)
-        gradient(g_bf[0][0][:], 0, 0)
         xm0 = xm_tile(0, "xm_bf0")
-        for g in range(PASSES):
-            group_xm(nc.vector.tensor_copy, xm0, 0, g)
+        xm1 = xm_tile(1, "xm_bf1")
+        group_xm(nc.vector.tensor_copy, xm0, 0, 0)
+        group_xm(nc.vector.tensor_copy, xm1, 1, 0)
+        row_factor(0)
+        group_xm(nc.vector.tensor_copy, xm0, 0, 1)
+        gradient(g_bf[0][0][:], 0, 0)
+        quantize_xm(xm0, 0)
         row_factor(1)
-        quantize_g(g_bf[0][0][:], 0, 0)
-        xm1 = xm_tile(1, "after_ratio")
         xm3 = xm_tile(3, "xm_bf3")
-        for g in range(PASSES):
-            group_xm(nc.scalar.copy, xm1, 1, g)
         rest = HALF - ON_SCALAR
-        g_rows = keep.tile([P, PACK, ON_SCALAR], BF16, name="g_rows", tag="after_factor", align_bytes=64)
+        g_rows = keep.tile([P, PACK, ON_SCALAR], BF16, name="g_rows", tag="after_ratio", align_bytes=64)
         for t in range(PACK):
             nc.scalar.activation(g_rows[:, t, :], q[0][:, t, HALF + rest : N], ACT.Copy, scale=factor[0][:, t : t + 1])
         nc.scalar.copy(
             out=g_bf[0][1][:, rest:HALF, :].rearrange("p (c i) t -> p c t i", i=RUN),
             in_=g_rows[:].rearrange("p t (c i) -> p c t i", i=RUN),
         )
-        xm2 = xm_tile(2, "after_factor")
+        xm2 = xm_tile(2, "after_ratio")
         for g in range(PASSES):
             group_xm(nc.scalar.copy, xm2, 2, g)
         gradient(g_bf[1][0][:], 1, 0)
-        quantize_xm(xm0, 0)
+        quantize_g(g_bf[0][0][:], 0, 0)
         quantize_g(g_bf[1][0][:], 1, 0)
         early0 = empty(nc.scalar.copy, product(0, 0, 0, HALF), "early0")
         place_on_scalar(0, 0, early0[:])
         gradient(g_bf[0][1][:], 0, 1, 0, rest)
-        quantize_xm(xm1, 1)
-        sums1 = [product(1, 1, 0, HALF)]
         gradient(g_bf[1][1][:], 1, 1)
         quantize_g(g_bf[0][1][:], 0, 1)
         quantize_g(g_bf[1][1][:], 1, 1)
         late0 = empty(nc.scalar.copy, product(0, 2, HALF, HALF), "late0")
         place_on_scalar(0, 1, late0[:])
         store(0)
-        sums1.append(product(1, 3, HALF, HALF))
-        for g in range(PASSES):
-            group_xm(nc.vector.tensor_copy, xm3, 3, g)
+        group_xm(nc.vector.tensor_copy, xm1, 1, 1)
+        quantize_xm(xm1, 1)
         quantize_xm(xm2, 2)
+        sums1 = [product(1, 1 + 2 * h, h * HALF, HALF) for h in range(2)]
+        nc.vector.tensor_copy(
+            out=xm3[:].rearrange("p g (c i) t -> p g c t i", i=RUN),
+            in_=xm_back[:, :, :, P : 2 * P].rearrange("p g t (c i) -> p g c t i", i=RUN),
+        )
         quantize_xm(xm3, 3)
         dense1 = keep.tile([P, N], F32, name="dense1", align_bytes=64)
         for h in range(2):

@@ -292,7 +292,7 @@ def tile_attend_gnce_w_clip_kernel(tc, xT, wT, y, wt, xn, xm, offs, out):
         gradient(g_bf[1][1][:], 1, 1)
         quantize_g(g_bf[0][1][:], 0, 1)
         quantize_g(g_bf[1][1][:], 1, 1)
-        late0 = empty(nc.scalar.copy, product(0, 2, HALF, HALF), "late0")
+        late0 = empty(nc.vector.tensor_copy, product(0, 2, HALF, HALF), "late0")
         place_on_scalar(0, 1, late0[:])
         store(0)
         group_xm(nc.vector.tensor_copy, xm1, 1, 1)

@@ -20,12 +20,13 @@ P = 128
 PACK = 4
 PASS = P * PACK
 PASSES = R // PASS
-RUN = 4
-ON_VECTOR = 3
+TILES = PASSES * PACK
+BLOCKS = D // P
 HALF = N // 2
-WINDOWS = 3
+BAND = 16
+RUN = 4
 X_FIRST = 320
-ON_SCALAR = 160
+ON_SCALAR = 128
 TINY = 2.0**-60
 
 
@@ -35,7 +36,7 @@ def tile_attend_gnce_w_clip_kernel(tc, xT, wT, y, wt, xn, xm, offs, out):
         keep = ctx.enter_context(tc.tile_pool(name="keep", bufs=1))
         psum = ctx.enter_context(tc.psum_pool(name="psum", bufs=1))
 
-        offsets = keep.tile([P, N // 16], U16, name="offsets")
+        offsets = keep.tile([P, N // BAND], U16, name="offsets")
 
         xT_planes = xT[0].rearrange("(p j) r -> p j r", j=PACK)
         wT_planes = wT.rearrange("(p j) c -> p j c", j=PACK)
@@ -70,19 +71,25 @@ def tile_attend_gnce_w_clip_kernel(tc, xT, wT, y, wt, xn, xm, offs, out):
             if h == 0:
                 nc.sync.dma_start(out=weight[:], in_=wt[0].rearrange("(g p t) o -> p g (t o)", p=P, t=PACK))
 
-        zero = keep.tile([P, 1], F32, name="zero", tag="column")
+        zero = keep.tile([P, 1], F32, name="zero", tag="after_sigmoids")
         tiny = keep.tile([P, 1], F32, name="tiny")
         nc.vector.memset(zero[:], 0.0)
         nc.vector.memset(tiny[:], TINY)
         warm = keep.tile([P, 1], F32, name="warm")
         nc.scalar.activation(warm[:], tiny[:], ACT.Sigmoid)
 
-        wide = [keep.tile([P, T], F32, name=f"wide{j}") for j in range(WINDOWS)]
-        for j in range(WINDOWS):
-            nc.vector.memset(wide[j][:], 0.0)
+        window = [keep.tile([P, T], F32, name=f"window{j}") for j in range(BLOCKS - 1)]
+        for j in range(BLOCKS - 1):
+            nc.vector.memset(window[j][:], 0.0)
 
         rel_sq = keep.tile([P, PASSES, PACK], F32, name="rel_sq")
         inv_sq = keep.tile([P, PASSES, PACK], F32, name="inv_sq")
+
+        def slots(h):
+            return slice(h * HALF, (h + 1) * HALF)
+
+        def offsets_of(h):
+            return offsets[:, h * HALF // BAND : (h + 1) * HALF // BAND]
 
         w_bf = keep.tile([P, N, PACK], BF16, name="w_bf", tag="stage", align_bytes=64)
         w_codes = keep.tile([P, N], U32, name="w_codes", align_bytes=64)
@@ -90,16 +97,12 @@ def tile_attend_gnce_w_clip_kernel(tc, xT, wT, y, wt, xn, xm, offs, out):
         for j in range(PACK - 1):
             nc.vector.tensor_copy(out=w_bf[:, :, j], in_=w_raw[j][:].indirect(offsets[:]))
         for h in range(2):
-            nc.vector.tensor_copy(
-                out=w_bf[:, h * HALF : (h + 1) * HALF, PACK - 1],
-                in_=w_raw[PACK - 1][:].indirect(offsets[:, h * HALF // 16 : (h + 1) * HALF // 16]),
-            )
-        wide.append(keep.tile([P, T], F32, name="wide3", tag="w_raw0"))
-        nc.gpsimd.memset(wide[WINDOWS][:], 0.0)
+            nc.vector.tensor_copy(out=w_bf[:, slots(h), PACK - 1], in_=w_raw[PACK - 1][:].indirect(offsets_of(h)))
+        window.append(keep.tile([P, T], F32, name=f"window{BLOCKS - 1}", tag="w_raw0"))
+        nc.gpsimd.memset(window[BLOCKS - 1][:], 0.0)
         for h in range(2):
-            cols = slice(h * HALF, (h + 1) * HALF)
             nc.vector.quantize_mx(
-                out=w_codes[:, cols].bitcast(E4M3), scales=w_scales[:, cols], in_=w_bf[:, cols, :].rearrange("p n j -> p (n j)")
+                out=w_codes[:, slots(h)].bitcast(E4M3), scales=w_scales[:, slots(h)], in_=w_bf[:, slots(h), :].rearrange("p n j -> p (n j)")
             )
 
         x_codes = [keep.tile([P, PASS], U32, name=f"x_codes{g}", align_bytes=64) for g in range(PASSES)]
@@ -118,6 +121,7 @@ def tile_attend_gnce_w_clip_kernel(tc, xT, wT, y, wt, xn, xm, offs, out):
                 in_=src.rearrange("p t m j -> p (t m j)"),
             )
 
+        split = X_FIRST // PACK
         x_lo = keep.tile([P, 2, P, PACK], BF16, name="x_lo", tag="stage", align_bytes=64)
         x_hi = keep.tile([P, 2, P, PACK], BF16, name="x_hi", align_bytes=64)
         group_x(nc.vector.tensor_copy, x_lo[:], x_raw, 0, 2)
@@ -125,42 +129,41 @@ def tile_attend_gnce_w_clip_kernel(tc, xT, wT, y, wt, xn, xm, offs, out):
         quantize_x(x_lo[:, 0:1], 0, 0, 1)
         quantize_x(x_lo[:, 1:2], 0, 1, 2)
         x_lo2 = keep.tile([P, 2, P, PACK], BF16, name="x_lo2", tag="stage", align_bytes=64)
-        group_x(nc.vector.tensor_copy, x_lo2[:, :, 0 : X_FIRST // PACK, :], x_part[0], 0, 2)
+        group_x(nc.vector.tensor_copy, x_lo2[:, :, 0:split, :], x_part[0], 0, 2)
         quantize_x(x_hi[:], 0, 2, 4)
         x_hi2 = keep.tile([P, 2, P, PACK], BF16, name="x_hi2", tag="x_hi", align_bytes=64)
-        group_x(nc.vector.tensor_copy, x_hi2[:, :, 0 : X_FIRST // PACK, :], x_part[0], 2, 4)
-        group_x(nc.vector.tensor_copy, x_lo2[:, :, X_FIRST // PACK : P, :], x_part[1], 0, 2)
-        group_x(nc.vector.tensor_copy, x_hi2[:, :, X_FIRST // PACK : P, :], x_part[1], 2, 4)
+        group_x(nc.vector.tensor_copy, x_hi2[:, :, 0:split, :], x_part[0], 2, 4)
+        group_x(nc.vector.tensor_copy, x_lo2[:, :, split:P, :], x_part[1], 0, 2)
+        group_x(nc.vector.tensor_copy, x_hi2[:, :, split:P, :], x_part[1], 2, 4)
         quantize_x(x_lo2[:, 0:1], 1, 0, 1)
         quantize_x(x_lo2[:, 1:2], 1, 1, 2)
         quantize_x(x_hi2[:], 1, 2, 4)
 
-        TILES = PASSES * PACK
         prob = [keep.tile([P, PACK, N], F32, name=f"prob{g}") for g in range(PASSES)]
         q = [keep.tile([P, PACK, N], F32, name=f"q{g}", align_bytes=64) for g in range(PASSES)]
         squares_v = [keep.tile([P, N], BF16, name=f"squares_v{h}") for h in range(2)]
         squares_s = [keep.tile([P, N], BF16, name=f"squares_s{h}") for h in range(2)]
-        sum_sq = keep.tile([P, TILES], F32, name="sum_sq", tag="after_ratio", align_bytes=64)
+        sum_sq = keep.tile([P, TILES], F32, name="sum_sq", tag="after_ratios", align_bytes=64)
         factor = [keep.tile([P, PACK], F32, name=f"factor{g}", tag=("xm_front0", "factor1")[g]) for g in range(PASSES)]
         g_codes = [keep.tile([P, N], U32, name=f"g_codes{g}", align_bytes=64) for g in range(PASSES)]
         g_scales = [keep.tile([P, N], U8, name=f"g_scales{g}", align_bytes=64) for g in range(PASSES)]
 
         for u in range(TILES):
             g, t = divmod(u, PACK)
-            a = psum.tile([P, N], F32, name=f"bank{u}")
+            scores = psum.tile([P, N], F32, name=f"bank{u}")
             cols = slice(t * P, (t + 1) * P)
             nc.tensor.matmul_mx(
-                out=a[:], lhsT=x_codes[g][:, cols].bitcast(E4M3), lhsT_scale=x_scales[g][:, cols],
+                out=scores[:], lhsT=x_codes[g][:, cols].bitcast(E4M3), lhsT_scale=x_scales[g][:, cols],
                 rhs=w_codes[:].bitcast(E4M3), rhs_scale=w_scales[:], start=True, stop=True,
             )
-            nc.scalar.activation(prob[g][:, t, :], a[:], ACT.Sigmoid, bias=zero[:])
+            nc.scalar.activation(prob[g][:, t, :], scores[:], ACT.Sigmoid, bias=zero[:])
 
-        rel_len = keep.tile([P, TILES], F32, name="rel_len", tag="column")
-        ratio = keep.tile([P, TILES], F32, name="ratio", tag="after_factor", align_bytes=64)
+        rel_len = keep.tile([P, TILES], F32, name="rel_len", tag="after_sigmoids")
+        ratio = keep.tile([P, TILES], F32, name="ratio", align_bytes=64)
 
-        def residual(u, count):
+        def residual_pair(u):
             g, t = divmod(u, PACK)
-            rows = slice(t, t + count)
+            rows = slice(t, t + 2)
             nc.vector.tensor_tensor(q[g][:, rows, :], prob[g][:, rows, :], y_raw[g][:, rows, :], ALU.subtract)
 
         def square_on_vector(u):
@@ -182,32 +185,15 @@ def tile_attend_gnce_w_clip_kernel(tc, xT, wT, y, wt, xn, xm, offs, out):
                 factor[g][:], ratio[:, g * PACK : (g + 1) * PACK], 1.0, weight[:, g, :], ALU.min, ALU.mult
             )
 
-        def slots(h):
-            return slice(h * HALF, (h + 1) * HALF)
-
-        def gradient(dst, g, h, first=0, count=HALF):
-            nc.vector.tensor_tensor(
-                dst[:, first : first + count, :].rearrange("p (c i) t -> p c t i", i=RUN),
-                q[g][:, :, h * HALF + first : h * HALF + first + count].rearrange("p t (c i) -> p c t i", i=RUN),
-                factor[g][:].unsqueeze(1).unsqueeze(3).to_broadcast([P, count // RUN, PACK, RUN]),
-                ALU.mult,
-            )
-
-        def quantize_g(src, g, h):
-            cols = slots(h)
-            nc.vector.quantize_mx(
-                out=g_codes[g][:, cols].bitcast(E5M2), scales=g_scales[g][:, cols], in_=src.rearrange("p n t -> p (n t)")
-            )
-
-        residual(0, 2)
+        residual_pair(0)
         nc.vector.tensor_scalar(rel_sq[:], sq_len[:], 1.0 / (CLIP * CLIP), TINY, ALU.mult, ALU.add)
-        residual(2, 2)
+        residual_pair(2)
         nc.vector.reciprocal(inv_sq[:], rel_sq[:])
         nc.scalar.activation(rel_len[:], inv_sq[:].rearrange("p g t -> p (g t)"), ACT.Abs_reciprocal_sqrt)
         square_on_vector(0)
-        residual(4, 2)
+        residual_pair(4)
         square_on_vector(1)
-        residual(6, 2)
+        residual_pair(6)
         for u in range(2, PACK):
             square_on_scalar(u)
         row_ratio(0)
@@ -215,8 +201,8 @@ def tile_attend_gnce_w_clip_kernel(tc, xT, wT, y, wt, xn, xm, offs, out):
             square_on_scalar(u)
         row_ratio(1)
 
-        xm_codes = [keep.tile([P, PASSES, P], U32, name=f"xm_codes{j}", align_bytes=64) for j in range(D // P)]
-        xm_scales = [keep.tile([P, PASSES, P], U8, name=f"xm_scales{j}", align_bytes=64) for j in range(D // P)]
+        xm_codes = [keep.tile([P, PASSES, P], U32, name=f"xm_codes{j}", align_bytes=64) for j in range(BLOCKS)]
+        xm_scales = [keep.tile([P, PASSES, P], U8, name=f"xm_scales{j}", align_bytes=64) for j in range(BLOCKS)]
 
         def xm_tile(j, tag):
             return keep.tile([P, PASSES, P, PACK], BF16, name=f"xm_bf{j}", tag=tag, align_bytes=64)
@@ -234,71 +220,85 @@ def tile_attend_gnce_w_clip_kernel(tc, xT, wT, y, wt, xn, xm, offs, out):
                 in_=src[:].rearrange("p g d t -> p (g d t)"),
             )
 
+        g_bf = [[keep.tile([P, HALF, PACK], BF16, name=f"g_bf{g}{h}", align_bytes=64) for h in range(2)] for g in range(PASSES)]
+
+        def gradient(g, h, count=HALF):
+            nc.vector.tensor_tensor(
+                g_bf[g][h][:, 0:count, :].rearrange("p (c i) t -> p c t i", i=RUN),
+                q[g][:, :, h * HALF : h * HALF + count].rearrange("p t (c i) -> p c t i", i=RUN),
+                factor[g][:].unsqueeze(1).unsqueeze(3).to_broadcast([P, count // RUN, PACK, RUN]),
+                ALU.mult,
+            )
+
+        def quantize_g(g, h):
+            nc.vector.quantize_mx(
+                out=g_codes[g][:, slots(h)].bitcast(E5M2), scales=g_scales[g][:, slots(h)], in_=g_bf[g][h][:].rearrange("p n t -> p (n t)")
+            )
+
         def product(j, bank, first, count):
-            dw = psum.tile([P, count], F32, name=f"bank{bank}")
+            sums = psum.tile([P, count], F32, name=f"bank{bank}")
             cols = slice(first, first + count)
             for g in range(PASSES):
                 nc.tensor.matmul_mx(
-                    out=dw[:], lhsT=xm_codes[j][:, g, :].bitcast(E4M3), lhsT_scale=xm_scales[j][:, g, :],
+                    out=sums[:], lhsT=xm_codes[j][:, g, :].bitcast(E4M3), lhsT_scale=xm_scales[j][:, g, :],
                     rhs=g_codes[g][:, cols].bitcast(E5M2), rhs_scale=g_scales[g][:, cols], start=(g == 0), stop=(g == PASSES - 1),
                 )
-            return dw[:]
+            return sums[:]
 
-        def empty(copy, dw, name):
-            dense = keep.tile([P, dw.shape[1]], F32, name=name, align_bytes=64)
-            copy(out=dense[:], in_=dw)
+        def to_sbuf(copy, sums, tag):
+            dense = keep.tile([P, sums.shape[1]], F32, name=tag, align_bytes=64)
+            copy(out=dense[:], in_=sums)
             return dense
 
-        def places(j, h):
-            return wide[j][:].indirect(offsets[:, h * HALF // 16 : (h + 1) * HALF // 16])
+        def scatter_on_vector(j, dense):
+            nc.vector.tensor_copy(out=window[j][:].indirect(offsets[:]), in_=dense)
 
-        def place_on_vector(j, dense):
-            nc.vector.tensor_copy(out=wide[j][:].indirect(offsets[:]), in_=dense)
-
-        def place_on_scalar(j, h, dense):
-            nc.scalar.activation(places(j, h), dense, ACT.Copy)
+        def scatter_half_on_scalar(j, h, dense):
+            nc.scalar.activation(window[j][:].indirect(offsets_of(h)), dense, ACT.Copy)
 
         def store(j):
-            nc.sync.dma_start(out=out[j * P : (j + 1) * P, :], in_=wide[j][:])
+            nc.sync.dma_start(out=out[j * P : (j + 1) * P, :], in_=window[j][:])
 
-        g_bf = [[keep.tile([P, HALF, PACK], BF16, name=f"g_bf{g}{h}", align_bytes=64) for h in range(2)] for g in range(PASSES)]
         xm0 = xm_tile(0, "xm_bf0")
         xm1 = xm_tile(1, "xm_bf1")
         group_xm(nc.vector.tensor_copy, xm0, 0, 0)
         group_xm(nc.vector.tensor_copy, xm1, 1, 0)
         row_factor(0)
         group_xm(nc.vector.tensor_copy, xm0, 0, 1)
-        gradient(g_bf[0][0][:], 0, 0)
+        gradient(0, 0)
         quantize_xm(xm0, 0)
         row_factor(1)
+
         xm3 = xm_tile(3, "xm_bf3")
-        rest = HALF - ON_SCALAR
-        g_rows = keep.tile([P, PACK, ON_SCALAR], BF16, name="g_rows", tag="after_ratio", align_bytes=64)
+        on_vector = HALF - ON_SCALAR
+        g_rows = keep.tile([P, PACK, ON_SCALAR], BF16, name="g_rows", tag="after_ratios", align_bytes=64)
         for t in range(PACK):
-            nc.scalar.activation(g_rows[:, t, :], q[0][:, t, HALF + rest : N], ACT.Copy, scale=factor[0][:, t : t + 1])
+            nc.scalar.activation(g_rows[:, t, :], q[0][:, t, HALF + on_vector : N], ACT.Copy, scale=factor[0][:, t : t + 1])
         nc.scalar.copy(
-            out=g_bf[0][1][:, rest:HALF, :].rearrange("p (c i) t -> p c t i", i=RUN),
+            out=g_bf[0][1][:, on_vector:HALF, :].rearrange("p (c i) t -> p c t i", i=RUN),
             in_=g_rows[:].rearrange("p t (c i) -> p c t i", i=RUN),
         )
-        xm2 = xm_tile(2, "after_ratio")
+        xm2 = xm_tile(2, "after_ratios")
         for g in range(PASSES):
             group_xm(nc.scalar.copy, xm2, 2, g)
-        gradient(g_bf[1][0][:], 1, 0)
-        quantize_g(g_bf[0][0][:], 0, 0)
-        quantize_g(g_bf[1][0][:], 1, 0)
-        early0 = empty(nc.scalar.copy, product(0, 0, 0, HALF), "early0")
-        place_on_scalar(0, 0, early0[:])
-        gradient(g_bf[0][1][:], 0, 1, 0, rest)
-        gradient(g_bf[1][1][:], 1, 1)
-        quantize_g(g_bf[0][1][:], 0, 1)
-        quantize_g(g_bf[1][1][:], 1, 1)
-        late0 = empty(nc.vector.tensor_copy, product(0, 2, HALF, HALF), "late0")
-        place_on_scalar(0, 1, late0[:])
+
+        gradient(1, 0)
+        quantize_g(0, 0)
+        quantize_g(1, 0)
+        early0 = to_sbuf(nc.scalar.copy, product(0, 0, 0, HALF), "early0")
+        scatter_half_on_scalar(0, 0, early0[:])
+        gradient(0, 1, on_vector)
+        gradient(1, 1)
+        quantize_g(0, 1)
+        quantize_g(1, 1)
+        late0 = to_sbuf(nc.vector.tensor_copy, product(0, 2, HALF, HALF), "late0")
+        scatter_half_on_scalar(0, 1, late0[:])
         store(0)
+
         group_xm(nc.vector.tensor_copy, xm1, 1, 1)
         quantize_xm(xm1, 1)
         quantize_xm(xm2, 2)
-        sums1 = [product(1, 1 + 2 * h, h * HALF, HALF) for h in range(2)]
+        sums1 = [product(1, bank, h * HALF, HALF) for h, bank in enumerate((1, 3))]
         nc.vector.tensor_copy(
             out=xm3[:].rearrange("p g (c i) t -> p g c t i", i=RUN),
             in_=xm_back[:, :, :, P : 2 * P].rearrange("p g t (c i) -> p g c t i", i=RUN),
@@ -307,12 +307,14 @@ def tile_attend_gnce_w_clip_kernel(tc, xT, wT, y, wt, xn, xm, offs, out):
         dense1 = keep.tile([P, N], F32, name="dense1", align_bytes=64)
         for h in range(2):
             nc.vector.tensor_copy(out=dense1[:, slots(h)], in_=sums1[h])
-        place_on_vector(1, dense1[:])
+        scatter_on_vector(1, dense1[:])
         store(1)
-        dense2 = empty(nc.scalar.copy, product(2, 4, 0, N), "dense2")
+
+        dense2 = to_sbuf(nc.scalar.copy, product(2, 2, 0, N), "dense2")
         for h in range(2):
-            place_on_scalar(2, h, dense2[:, slots(h)])
+            scatter_half_on_scalar(2, h, dense2[:, slots(h)])
         store(2)
-        dense3 = empty(nc.vector.tensor_copy, product(3, 5, 0, N), "dense1")
-        place_on_vector(3, dense3[:])
+
+        dense3 = to_sbuf(nc.vector.tensor_copy, product(3, 5, 0, N), "dense1")
+        scatter_on_vector(3, dense3[:])
         store(3)

@@ -72,7 +72,7 @@ def tile_attend_gnce_w_clip_kernel(tc, xT, wT, y, wt, xn, xm, offs, out):
                 nc.sync.dma_start(out=weight[:], in_=wt[0].rearrange("(g p t) o -> p g (t o)", p=P, t=PACK))
 
         zero = keep.tile([P, 1], F32, name="zero", tag="after_sigmoids")
-        tiny = keep.tile([P, 1], F32, name="tiny")
+        tiny = keep.tile([P, 1], F32, name="tiny", align_bytes=64)
         nc.vector.memset(zero[:], 0.0)
         nc.vector.memset(tiny[:], TINY)
         warm = keep.tile([P, 1], F32, name="warm")
@@ -91,7 +91,7 @@ def tile_attend_gnce_w_clip_kernel(tc, xT, wT, y, wt, xn, xm, offs, out):
         def offsets_of(h):
             return offsets[:, h * HALF // BAND : (h + 1) * HALF // BAND]
 
-        w_bf = keep.tile([P, N, PACK], BF16, name="w_bf", tag="stage", align_bytes=64)
+        w_bf = keep.tile([P, N, PACK], BF16, name="w_bf", align_bytes=64)
         w_codes = keep.tile([P, N], U32, name="w_codes", align_bytes=64)
         w_scales = keep.tile([P, N], U8, name="w_scales", align_bytes=64)
         for j in range(PACK - 1):
@@ -122,22 +122,19 @@ def tile_attend_gnce_w_clip_kernel(tc, xT, wT, y, wt, xn, xm, offs, out):
             )
 
         split = X_FIRST // PACK
-        x_lo = keep.tile([P, 2, P, PACK], BF16, name="x_lo", tag="stage", align_bytes=64)
+        x_lo = keep.tile([P, 2, P, PACK], BF16, name="x_lo", align_bytes=64)
         x_hi = keep.tile([P, 2, P, PACK], BF16, name="x_hi", align_bytes=64)
         group_x(nc.vector.tensor_copy, x_lo[:], x_raw, 0, 2)
         group_x(nc.scalar.copy, x_hi[:], x_raw, 2, 4)
         quantize_x(x_lo[:, 0:1], 0, 0, 1)
         quantize_x(x_lo[:, 1:2], 0, 1, 2)
-        x_lo2 = keep.tile([P, 2, P, PACK], BF16, name="x_lo2", tag="stage", align_bytes=64)
-        group_x(nc.vector.tensor_copy, x_lo2[:, :, 0:split, :], x_part[0], 0, 2)
+        x_second = keep.tile([P, PACK, P, PACK], BF16, name="x_second", align_bytes=64)
+        group_x(nc.vector.tensor_copy, x_second[:, :, 0:split, :], x_part[0], 0, PACK)
         quantize_x(x_hi[:], 0, 2, 4)
-        x_hi2 = keep.tile([P, 2, P, PACK], BF16, name="x_hi2", tag="x_hi", align_bytes=64)
-        group_x(nc.vector.tensor_copy, x_hi2[:, :, 0:split, :], x_part[0], 2, 4)
-        group_x(nc.vector.tensor_copy, x_lo2[:, :, split:P, :], x_part[1], 0, 2)
-        group_x(nc.vector.tensor_copy, x_hi2[:, :, split:P, :], x_part[1], 2, 4)
-        quantize_x(x_lo2[:, 0:1], 1, 0, 1)
-        quantize_x(x_lo2[:, 1:2], 1, 1, 2)
-        quantize_x(x_hi2[:], 1, 2, 4)
+        group_x(nc.vector.tensor_copy, x_second[:, :, split:P, :], x_part[1], 0, PACK)
+        quantize_x(x_second[:, 0:1], 1, 0, 1)
+        quantize_x(x_second[:, 1:2], 1, 1, 2)
+        quantize_x(x_second[:, 2:4], 1, 2, 4)
 
         prob = [keep.tile([P, PACK, N], F32, name=f"prob{g}") for g in range(PASSES)]
         q = [keep.tile([P, PACK, N], F32, name=f"q{g}", align_bytes=64) for g in range(PASSES)]
@@ -274,13 +271,13 @@ def tile_attend_gnce_w_clip_kernel(tc, xT, wT, y, wt, xn, xm, offs, out):
         g_rows = keep.tile([P, PACK, ON_SCALAR], BF16, name="g_rows", tag="after_ratios", align_bytes=64)
         for t in range(PACK):
             nc.scalar.activation(g_rows[:, t, :], q[0][:, t, HALF + on_vector : N], ACT.Copy, scale=factor[0][:, t : t + 1])
+        xm2 = xm_tile(2, "tiny")
+        group_xm(nc.scalar.copy, xm2, 2, 0)
         nc.scalar.copy(
             out=g_bf[0][1][:, on_vector:HALF, :].rearrange("p (c i) t -> p c t i", i=RUN),
             in_=g_rows[:].rearrange("p t (c i) -> p c t i", i=RUN),
         )
-        xm2 = xm_tile(2, "after_ratios")
-        for g in range(PASSES):
-            group_xm(nc.scalar.copy, xm2, 2, g)
+        group_xm(nc.scalar.copy, xm2, 2, 1)
 
         gradient(1, 0)
         quantize_g(0, 0)

@@ -254,7 +254,7 @@ def tile_attend_gnce_w_clip_kernel(tc, xT, wT, y, wt, xn, xm, offs, out):
             nc.scalar.activation(window[j][:].indirect(offsets_of(h)), dense, ACT.Copy)
 
         def store(j):
-            nc.sync.dma_start(out=out[j * P : (j + 1) * P, :], in_=window[j][:])
+            (nc.sync, nc.scalar)[j % 2].dma_start(out=out[j * P : (j + 1) * P, :], in_=window[j][:])
 
         xm0 = xm_tile(0, "xm_bf0")
         xm1 = xm_tile(1, "xm_bf1")
@@ -289,7 +289,7 @@ def tile_attend_gnce_w_clip_kernel(tc, xT, wT, y, wt, xn, xm, offs, out):
         quantize_g(0, 1)
         quantize_g(1, 1)
         late0 = to_sbuf(nc.vector.tensor_copy, product(0, 2, HALF, HALF), "late0")
-        scatter_half_on_scalar(0, 1, late0[:])
+        nc.vector.tensor_copy(out=window[0][:].indirect(offsets_of(1)), in_=late0[:])
         store(0)
 
         group_xm(nc.vector.tensor_copy, xm1, 1, 1)
@@ -301,17 +301,16 @@ def tile_attend_gnce_w_clip_kernel(tc, xT, wT, y, wt, xn, xm, offs, out):
             in_=xm_back[:, :, :, P : 2 * P].rearrange("p g t (c i) -> p g c t i", i=RUN),
         )
         quantize_xm(xm3, 3)
-        dense1 = keep.tile([P, N], F32, name="dense1", align_bytes=64)
         for h in range(2):
-            nc.vector.tensor_copy(out=dense1[:, slots(h)], in_=sums1[h])
-        scatter_on_vector(1, dense1[:])
+            half1 = to_sbuf(nc.scalar.copy, sums1[h], f"half1{h}")
+            scatter_half_on_scalar(1, h, half1[:])
         store(1)
 
-        dense2 = to_sbuf(nc.scalar.copy, product(2, 2, 0, N), "dense2")
-        for h in range(2):
-            scatter_half_on_scalar(2, h, dense2[:, slots(h)])
+        dense2 = to_sbuf(nc.vector.tensor_copy, product(2, 2, 0, N), "dense2")
+        dense3 = to_sbuf(nc.vector.tensor_copy, product(3, 5, 0, N), "late0")
+        scatter_on_vector(2, dense2[:])
         store(2)
 
-        dense3 = to_sbuf(nc.vector.tensor_copy, product(3, 5, 0, N), "dense1")
-        scatter_on_vector(3, dense3[:])
+        for h in range(2):
+            scatter_half_on_scalar(3, h, dense3[:, slots(h)])
         store(3)

@@ -26,7 +26,7 @@ HALF = N // 2
 BAND = 16
 RUN = 4
 X_FIRST = 320
-ON_SCALAR = 128
+ON_SCALAR = 160
 TINY = 2.0**-60
 
 
@@ -50,7 +50,7 @@ def tile_attend_gnce_w_clip_kernel(tc, xT, wT, y, wt, xn, xm, offs, out):
         xm_front = [keep.tile([P, PACK, D // 2], F32, name=f"xm_front{g}") for g in range(PASSES)]
         xm_back = keep.tile([P, PASSES, PACK, D // 2], F32, name="xm_back")
         xm_raw = [[xm_front[g][:] for g in range(PASSES)], [xm_back[:, g] for g in range(PASSES)]]
-        weight = keep.tile([P, PASSES, PACK], F32, name="weight")
+        weight = keep.tile([P, PASSES, PACK], F32, name="weight", align_bytes=64)
         sq_len = keep.tile([P, PASSES, PACK], F32, name="sq_len")
 
         for j in range(PACK):
@@ -142,7 +142,6 @@ def tile_attend_gnce_w_clip_kernel(tc, xT, wT, y, wt, xn, xm, offs, out):
         squares_s = [keep.tile([P, N], BF16, name=f"squares_s{h}") for h in range(2)]
         sum_sq = keep.tile([P, TILES], F32, name="sum_sq", tag="after_ratios", align_bytes=64)
         factor = [keep.tile([P, PACK], F32, name=f"factor{g}", tag=("xm_front0", "factor1")[g]) for g in range(PASSES)]
-        g_codes = [keep.tile([P, N], U32, name=f"g_codes{g}", align_bytes=64) for g in range(PASSES)]
         g_scales = [keep.tile([P, N], U8, name=f"g_scales{g}", align_bytes=64) for g in range(PASSES)]
 
         for u in range(TILES):
@@ -156,7 +155,7 @@ def tile_attend_gnce_w_clip_kernel(tc, xT, wT, y, wt, xn, xm, offs, out):
             nc.scalar.activation(prob[g][:, t, :], scores[:], ACT.Sigmoid, bias=zero[:])
 
         rel_len = keep.tile([P, TILES], F32, name="rel_len", tag="after_sigmoids")
-        ratio = keep.tile([P, TILES], F32, name="ratio", align_bytes=64)
+        ratio = [keep.tile([P, PACK], F32, name=f"ratio{g}", align_bytes=64) for g in range(PASSES)]
 
         def residual_pair(u):
             g, t = divmod(u, PACK)
@@ -175,11 +174,11 @@ def tile_attend_gnce_w_clip_kernel(tc, xT, wT, y, wt, xn, xm, offs, out):
 
         def row_ratio(g):
             cols = slice(g * PACK, (g + 1) * PACK)
-            nc.scalar.activation(ratio[:, cols], sum_sq[:, cols], ACT.Abs_reciprocal_sqrt, bias=tiny[:])
+            nc.scalar.activation(ratio[g][:], sum_sq[:, cols], ACT.Abs_reciprocal_sqrt, bias=tiny[:])
 
         def row_factor(g):
             nc.vector.scalar_tensor_tensor(
-                factor[g][:], ratio[:, g * PACK : (g + 1) * PACK], 1.0, weight[:, g, :], ALU.min, ALU.mult
+                factor[g][:], ratio[g][:], 1.0, weight[:, g, :], ALU.min, ALU.mult
             )
 
         residual_pair(0)
@@ -217,7 +216,10 @@ def tile_attend_gnce_w_clip_kernel(tc, xT, wT, y, wt, xn, xm, offs, out):
                 in_=src[:].rearrange("p g d t -> p (g d t)"),
             )
 
-        g_bf = [[keep.tile([P, HALF, PACK], BF16, name=f"g_bf{g}{h}", align_bytes=64) for h in range(2)] for g in range(PASSES)]
+        def g_tile(g, h, tag):
+            return keep.tile([P, HALF, PACK], BF16, name=f"g_bf{g}{h}", tag=tag, align_bytes=64)
+
+        g_bf = [[g_tile(0, 0, "g_bf00")], [g_tile(1, h, f"g_bf1{h}") for h in range(2)]]
 
         def gradient(g, h, count=HALF):
             nc.vector.tensor_tensor(
@@ -232,13 +234,13 @@ def tile_attend_gnce_w_clip_kernel(tc, xT, wT, y, wt, xn, xm, offs, out):
                 out=g_codes[g][:, slots(h)].bitcast(E5M2), scales=g_scales[g][:, slots(h)], in_=g_bf[g][h][:].rearrange("p n t -> p (n t)")
             )
 
-        def product(j, bank, first, count):
+        def product(j, bank, first, count, passes=(1, 0)):
             sums = psum.tile([P, count], F32, name=f"bank{bank}")
             cols = slice(first, first + count)
-            for g in range(PASSES):
+            for g in passes:
                 nc.tensor.matmul_mx(
                     out=sums[:], lhsT=xm_codes[j][:, g, :].bitcast(E4M3), lhsT_scale=xm_scales[j][:, g, :],
-                    rhs=g_codes[g][:, cols].bitcast(E5M2), rhs_scale=g_scales[g][:, cols], start=(g == 0), stop=(g == PASSES - 1),
+                    rhs=g_codes[g][:, cols].bitcast(E5M2), rhs_scale=g_scales[g][:, cols], start=(g == passes[0]), stop=(g == passes[-1]),
                 )
             return sums[:]
 
@@ -265,6 +267,8 @@ def tile_attend_gnce_w_clip_kernel(tc, xT, wT, y, wt, xn, xm, offs, out):
         gradient(0, 0)
         quantize_xm(xm0, 0)
         row_factor(1)
+        g_bf[0].append(g_tile(0, 1, "ratio1"))
+        g_codes = [keep.tile([P, N], U32, name=f"g_codes{g}", tag=("weight", "g_codes1")[g], align_bytes=64) for g in range(PASSES)]
 
         xm3 = xm_tile(3, "xm_bf3")
         on_vector = HALF - ON_SCALAR
@@ -282,13 +286,13 @@ def tile_attend_gnce_w_clip_kernel(tc, xT, wT, y, wt, xn, xm, offs, out):
         gradient(1, 0)
         quantize_g(0, 0)
         quantize_g(1, 0)
-        early0 = to_sbuf(nc.scalar.copy, product(0, 0, 0, HALF), "early0")
+        early0 = to_sbuf(nc.scalar.copy, product(0, 0, 0, HALF, (0, 1)), "early0")
         scatter_half_on_scalar(0, 0, early0[:])
         gradient(0, 1, on_vector)
         gradient(1, 1)
         quantize_g(0, 1)
         quantize_g(1, 1)
-        late0 = to_sbuf(nc.vector.tensor_copy, product(0, 2, HALF, HALF), "late0")
+        late0 = to_sbuf(nc.vector.tensor_copy, product(0, 2, HALF, HALF, (0, 1)), "late0")
         nc.vector.tensor_copy(out=window[0][:].indirect(offsets_of(1)), in_=late0[:])
         store(0)
 
@@ -296,10 +300,8 @@ def tile_attend_gnce_w_clip_kernel(tc, xT, wT, y, wt, xn, xm, offs, out):
         quantize_xm(xm1, 1)
         quantize_xm(xm2, 2)
         sums1 = [product(1, bank, h * HALF, HALF) for h, bank in enumerate((1, 3))]
-        nc.vector.tensor_copy(
-            out=xm3[:].rearrange("p g (c i) t -> p g c t i", i=RUN),
-            in_=xm_back[:, :, :, P : 2 * P].rearrange("p g t (c i) -> p g c t i", i=RUN),
-        )
+        for g in range(PASSES):
+            group_xm(nc.vector.tensor_copy, xm3, 3, g)
         quantize_xm(xm3, 3)
         for h in range(2):
             half1 = to_sbuf(nc.scalar.copy, sums1[h], f"half1{h}")

@@ -25,7 +25,7 @@ BLOCKS = D // P
 HALF = N // 2
 BAND = 16
 RUN = 4
-X_FIRST = 320
+X_FIRST = 384
 ON_SCALAR = 160
 TINY = 2.0**-60
 
@@ -78,9 +78,10 @@ def tile_attend_gnce_w_clip_kernel(tc, xT, wT, y, wt, xn, xm, offs, out):
         warm = keep.tile([P, 1], F32, name="warm")
         nc.scalar.activation(warm[:], tiny[:], ACT.Sigmoid)
 
-        window = [keep.tile([P, T], F32, name=f"window{j}") for j in range(BLOCKS - 1)]
+        window = [keep.tile([P, T], F32, name=f"window{j}") for j in range(BLOCKS)]
         for j in range(BLOCKS - 1):
             nc.vector.memset(window[j][:], 0.0)
+        nc.gpsimd.memset(window[BLOCKS - 1][:], 0.0)
 
         rel_sq = keep.tile([P, PASSES, PACK], F32, name="rel_sq")
         inv_sq = keep.tile([P, PASSES, PACK], F32, name="inv_sq")
@@ -98,8 +99,6 @@ def tile_attend_gnce_w_clip_kernel(tc, xT, wT, y, wt, xn, xm, offs, out):
             nc.vector.tensor_copy(out=w_bf[:, :, j], in_=w_raw[j][:].indirect(offsets[:]))
         for h in range(2):
             nc.vector.tensor_copy(out=w_bf[:, slots(h), PACK - 1], in_=w_raw[PACK - 1][:].indirect(offsets_of(h)))
-        window.append(keep.tile([P, T], F32, name=f"window{BLOCKS - 1}", tag="w_raw0"))
-        nc.gpsimd.memset(window[BLOCKS - 1][:], 0.0)
         for h in range(2):
             nc.vector.quantize_mx(
                 out=w_codes[:, slots(h)].bitcast(E4M3), scales=w_scales[:, slots(h)], in_=w_bf[:, slots(h), :].rearrange("p n j -> p (n j)")

@@ -26,7 +26,6 @@ HALF = N // 2
 BAND = 16
 RUN = 4
 X_FIRST = 384
-ON_SCALAR = 160
 TINY = 2.0**-60
 
 
@@ -48,8 +47,8 @@ def tile_attend_gnce_w_clip_kernel(tc, xT, wT, y, wt, xn, xm, offs, out):
         w_raw = [keep.tile([P, T], F32, name=f"w_raw{j}", tag=f"w_raw{j}") for j in range(PACK)]
         y_raw = [keep.tile([P, PACK, N], F32, name=f"y_raw{g}") for g in range(PASSES)]
         xm_front = [keep.tile([P, PACK, D // 2], F32, name=f"xm_front{g}") for g in range(PASSES)]
-        xm_back = keep.tile([P, PASSES, PACK, D // 2], F32, name="xm_back")
-        xm_raw = [[xm_front[g][:] for g in range(PASSES)], [xm_back[:, g] for g in range(PASSES)]]
+        xm_back = [keep.tile([P, PACK, D // 2], F32, name=f"xm_back{g}", align_bytes=64) for g in range(PASSES)]
+        xm_raw = [[xm_front[g][:] for g in range(PASSES)], [xm_back[g][:] for g in range(PASSES)]]
         weight = keep.tile([P, PASSES, PACK], F32, name="weight", align_bytes=64)
         sq_len = keep.tile([P, PASSES, PACK], F32, name="sq_len")
 
@@ -140,7 +139,9 @@ def tile_attend_gnce_w_clip_kernel(tc, xT, wT, y, wt, xn, xm, offs, out):
         squares_v = [keep.tile([P, N], BF16, name=f"squares_v{h}") for h in range(2)]
         squares_s = [keep.tile([P, N], BF16, name=f"squares_s{h}") for h in range(2)]
         sum_sq = keep.tile([P, TILES], F32, name="sum_sq", tag="after_ratios", align_bytes=64)
-        factor = [keep.tile([P, PACK], F32, name=f"factor{g}", tag=("xm_front0", "factor1")[g]) for g in range(PASSES)]
+        factor0 = keep.tile([P, PACK], F32, name="factor0", tag="xm_front0")
+        factor1 = [keep.tile([P, PACK], F32, name=f"factor1{h}", align_bytes=64) for h in range(2)]
+        factor = [[factor0, factor0], factor1]
         g_scales = [keep.tile([P, N], U8, name=f"g_scales{g}", align_bytes=64) for g in range(PASSES)]
 
         for u in range(TILES):
@@ -175,10 +176,8 @@ def tile_attend_gnce_w_clip_kernel(tc, xT, wT, y, wt, xn, xm, offs, out):
             cols = slice(g * PACK, (g + 1) * PACK)
             nc.scalar.activation(ratio[g][:], sum_sq[:, cols], ACT.Abs_reciprocal_sqrt, bias=tiny[:])
 
-        def row_factor(g):
-            nc.vector.scalar_tensor_tensor(
-                factor[g][:], ratio[g][:], 1.0, weight[:, g, :], ALU.min, ALU.mult
-            )
+        def row_factor(dst, g):
+            nc.vector.scalar_tensor_tensor(dst[:], ratio[g][:], 1.0, weight[:, g, :], ALU.min, ALU.mult)
 
         residual_pair(0)
         nc.vector.tensor_scalar(rel_sq[:], sq_len[:], 1.0 / (CLIP * CLIP), TINY, ALU.mult, ALU.add)
@@ -218,13 +217,13 @@ def tile_attend_gnce_w_clip_kernel(tc, xT, wT, y, wt, xn, xm, offs, out):
         def g_tile(g, h, tag):
             return keep.tile([P, HALF, PACK], BF16, name=f"g_bf{g}{h}", tag=tag, align_bytes=64)
 
-        g_bf = [[g_tile(0, 0, "g_bf00")], [g_tile(1, h, f"g_bf1{h}") for h in range(2)]]
+        g_bf = [[g_tile(g, 0, f"g_bf{g}0")] for g in range(PASSES)]
 
-        def gradient(g, h, count=HALF):
+        def gradient(g, h):
             nc.vector.tensor_tensor(
-                g_bf[g][h][:, 0:count, :].rearrange("p (c i) t -> p c t i", i=RUN),
-                q[g][:, :, h * HALF : h * HALF + count].rearrange("p t (c i) -> p c t i", i=RUN),
-                factor[g][:].unsqueeze(1).unsqueeze(3).to_broadcast([P, count // RUN, PACK, RUN]),
+                g_bf[g][h][:].rearrange("p (c i) t -> p c t i", i=RUN),
+                q[g][:, :, slots(h)].rearrange("p t (c i) -> p c t i", i=RUN),
+                factor[g][h][:].unsqueeze(1).unsqueeze(3).to_broadcast([P, HALF // RUN, PACK, RUN]),
                 ALU.mult,
             )
 
@@ -233,85 +232,86 @@ def tile_attend_gnce_w_clip_kernel(tc, xT, wT, y, wt, xn, xm, offs, out):
                 out=g_codes[g][:, slots(h)].bitcast(E5M2), scales=g_scales[g][:, slots(h)], in_=g_bf[g][h][:].rearrange("p n t -> p (n t)")
             )
 
-        def product(j, bank, first, count, passes=(1, 0)):
-            sums = psum.tile([P, count], F32, name=f"bank{bank}")
-            cols = slice(first, first + count)
+        def product(j, h, passes=(1, 0)):
+            sums = psum.tile([P, HALF], F32, name=f"bank{2 * j + h}")
             for g in passes:
                 nc.tensor.matmul_mx(
                     out=sums[:], lhsT=xm_codes[j][:, g, :].bitcast(E4M3), lhsT_scale=xm_scales[j][:, g, :],
-                    rhs=g_codes[g][:, cols].bitcast(E5M2), rhs_scale=g_scales[g][:, cols], start=(g == passes[0]), stop=(g == passes[-1]),
+                    rhs=g_codes[g][:, slots(h)].bitcast(E5M2), rhs_scale=g_scales[g][:, slots(h)], start=(g == passes[0]), stop=(g == passes[-1]),
                 )
             return sums[:]
 
-        def to_sbuf(copy, sums, tag):
-            dense = keep.tile([P, sums.shape[1]], F32, name=tag, align_bytes=64)
-            copy(out=dense[:], in_=sums)
-            return dense
+        def to_sbuf(copy, j, h, passes=(1, 0)):
+            dense = keep.tile([P, HALF], F32, name=f"dense{j}{h}", align_bytes=64)
+            copy(out=dense[:], in_=product(j, h, passes))
+            return dense[:]
 
-        def scatter_on_vector(j, dense):
-            nc.vector.tensor_copy(out=window[j][:].indirect(offsets[:]), in_=dense)
+        def scatter_early(j, dense):
+            nc.scalar.activation(window[j][:].indirect(offsets_of(0)), dense, ACT.Copy)
 
-        def scatter_half_on_scalar(j, h, dense):
-            nc.scalar.activation(window[j][:].indirect(offsets_of(h)), dense, ACT.Copy)
+        def scatter_late(j, dense):
+            nc.vector.tensor_copy(out=window[j][:].indirect(offsets_of(1)), in_=dense)
+            nc.sync.dma_start(out=out[j * P : (j + 1) * P, :], in_=window[j][:])
 
-        def store(j):
-            (nc.sync, nc.scalar)[j % 2].dma_start(out=out[j * P : (j + 1) * P, :], in_=window[j][:])
+        def group_xm_on_gpsimd(dst, j, g):
+            nc.gpsimd.tensor_scalar(
+                dst[:, g].rearrange("p (c i) t -> p c t i", i=RUN),
+                xm_raw[j // 2][g][:, :, (j % 2) * P : (j % 2 + 1) * P].rearrange("p t (c i) -> p c t i", i=RUN),
+                1.0, 0.0, ALU.mult, ALU.add,
+            )
 
-        xm0 = xm_tile(0, "xm_bf0")
-        xm1 = xm_tile(1, "xm_bf1")
-        group_xm(nc.vector.tensor_copy, xm0, 0, 0)
-        group_xm(nc.vector.tensor_copy, xm1, 1, 0)
-        row_factor(0)
-        group_xm(nc.vector.tensor_copy, xm0, 0, 1)
+        xm_bf = [xm_tile(j, f"xm_bf{j}") for j in range(2)]
+        group_xm(nc.vector.tensor_copy, xm_bf[0], 0, 0)
+        group_xm(nc.vector.tensor_copy, xm_bf[1], 1, 0)
+        row_factor(factor0, 0)
+        group_xm(nc.vector.tensor_copy, xm_bf[0], 0, 1)
         gradient(0, 0)
-        quantize_xm(xm0, 0)
-        row_factor(1)
-        g_bf[0].append(g_tile(0, 1, "ratio1"))
-        g_codes = [keep.tile([P, N], U32, name=f"g_codes{g}", tag=("weight", "g_codes1")[g], align_bytes=64) for g in range(PASSES)]
+        quantize_xm(xm_bf[0], 0)
+        group_xm(nc.vector.tensor_copy, xm_bf[1], 1, 1)
+        quantize_xm(xm_bf[1], 1)
+        row_factor(factor1[0], 1)
+        g_codes = [keep.tile([P, N], U32, name=f"g_codes{g}", tag=("tiny", "g_codes1")[g], align_bytes=64) for g in range(PASSES)]
+        quantize_g(0, 0)
+        gradient(1, 0)
+        row_factor(factor1[1], 1)
+        quantize_g(1, 0)
+        g_bf[0].append(g_tile(0, 1, "g_bf01"))
+        g_bf[1].append(g_tile(1, 1, "factor10"))
 
-        xm3 = xm_tile(3, "xm_bf3")
-        on_vector = HALF - ON_SCALAR
-        g_rows = keep.tile([P, PACK, ON_SCALAR], BF16, name="g_rows", tag="after_ratios", align_bytes=64)
+        g_rows = keep.tile([P, PACK, HALF], BF16, name="g_rows", tag="after_ratios", align_bytes=64)
         for t in range(PACK):
-            nc.scalar.activation(g_rows[:, t, :], q[0][:, t, HALF + on_vector : N], ACT.Copy, scale=factor[0][:, t : t + 1])
-        xm2 = xm_tile(2, "tiny")
-        group_xm(nc.scalar.copy, xm2, 2, 0)
+            nc.scalar.activation(g_rows[:, t, :], q[0][:, t, slots(1)], ACT.Copy, scale=factor0[:, t : t + 1])
         nc.scalar.copy(
-            out=g_bf[0][1][:, on_vector:HALF, :].rearrange("p (c i) t -> p c t i", i=RUN),
+            out=g_bf[0][1][:].rearrange("p (c i) t -> p c t i", i=RUN),
             in_=g_rows[:].rearrange("p t (c i) -> p c t i", i=RUN),
         )
-        group_xm(nc.scalar.copy, xm2, 2, 1)
 
-        gradient(1, 0)
-        quantize_g(0, 0)
-        quantize_g(1, 0)
-        early0 = to_sbuf(nc.scalar.copy, product(0, 0, 0, HALF, (0, 1)), "early0")
-        scatter_half_on_scalar(0, 0, early0[:])
-        gradient(0, 1, on_vector)
+        early0 = to_sbuf(nc.scalar.copy, 0, 0, (0, 1))
+        early1 = to_sbuf(nc.scalar.copy, 1, 0, (0, 1))
+        scatter_early(0, early0)
+        scatter_early(1, early1)
         gradient(1, 1)
         quantize_g(0, 1)
         quantize_g(1, 1)
-        late0 = to_sbuf(nc.vector.tensor_copy, product(0, 2, HALF, HALF, (0, 1)), "late0")
-        nc.vector.tensor_copy(out=window[0][:].indirect(offsets_of(1)), in_=late0[:])
-        store(0)
-
-        group_xm(nc.vector.tensor_copy, xm1, 1, 1)
-        quantize_xm(xm1, 1)
-        quantize_xm(xm2, 2)
-        sums1 = [product(1, bank, h * HALF, HALF) for h, bank in enumerate((1, 3))]
+        xm_bf.append(xm_tile(2, "g_bf01"))
+        group_xm(nc.vector.tensor_copy, xm_bf[2], 2, 0)
+        group_xm(nc.vector.tensor_copy, xm_bf[2], 2, 1)
+        late0 = to_sbuf(nc.vector.tensor_copy, 0, 1, (0, 1))
+        quantize_xm(xm_bf[2], 2)
+        scatter_late(0, late0)
+        xm_bf.append(xm_tile(3, "g_bf01"))
         for g in range(PASSES):
-            group_xm(nc.vector.tensor_copy, xm3, 3, g)
-        quantize_xm(xm3, 3)
-        for h in range(2):
-            half1 = to_sbuf(nc.scalar.copy, sums1[h], f"half1{h}")
-            scatter_half_on_scalar(1, h, half1[:])
-        store(1)
-
-        dense2 = to_sbuf(nc.vector.tensor_copy, product(2, 2, 0, N), "dense2")
-        dense3 = to_sbuf(nc.vector.tensor_copy, product(3, 5, 0, N), "late0")
-        scatter_on_vector(2, dense2[:])
-        store(2)
-
-        for h in range(2):
-            scatter_half_on_scalar(3, h, dense3[:, slots(h)])
-        store(3)
+            group_xm_on_gpsimd(xm_bf[3], 3, g)
+        quantize_xm(xm_bf[3], 3)
+        held = keep.tile([P, 2, HALF], F32, name="held", tag="xm_back1", align_bytes=64)
+        late1, early2 = held[:, 0, :], held[:, 1, :]
+        nc.scalar.copy(out=late1, in_=product(1, 1))
+        nc.scalar.copy(out=early2, in_=product(2, 0))
+        scatter_early(2, early2)
+        scatter_late(1, late1)
+        late2 = to_sbuf(nc.vector.tensor_copy, 2, 1)
+        late3 = to_sbuf(nc.vector.tensor_copy, 3, 1)
+        scatter_late(2, late2)
+        early3 = to_sbuf(nc.scalar.copy, 3, 0)
+        scatter_early(3, early3)
+        scatter_late(3, late3)

@@ -52,10 +52,9 @@ def tile_attend_gnce_w_clip_kernel(tc, xT, wT, y, wt, xn, xm, offs, out):
         weight = keep.tile([P, PASSES, PACK], F32, name="weight", align_bytes=64)
         sq_len = keep.tile([P, PASSES, PACK], F32, name="sq_len")
 
+        nc.sync.dma_start(offsets[:], offs)
         for j in range(PACK):
             nc.sync.dma_start(out=w_raw[j][:], in_=wT_planes[:, j, :])
-            if j == 0:
-                nc.sync.dma_start(offsets[:], offs)
         nc.sync.dma_start(out=x_raw[:], in_=xT_planes[:, :, 0:PASS])
         nc.sync.dma_start(out=x_part[0][:], in_=xT_planes[:, :, PASS : PASS + X_FIRST])
         nc.sync.dma_start(out=x_part[1][:], in_=xT_planes[:, :, PASS + X_FIRST : R])
@@ -77,10 +76,9 @@ def tile_attend_gnce_w_clip_kernel(tc, xT, wT, y, wt, xn, xm, offs, out):
         warm = keep.tile([P, 1], F32, name="warm")
         nc.scalar.activation(warm[:], tiny[:], ACT.Sigmoid)
 
-        window = [keep.tile([P, T], F32, name=f"window{j}") for j in range(BLOCKS)]
-        for j in range(BLOCKS - 1):
+        window = [keep.tile([P, T], F32, name=f"window{j}") for j in range(2)]
+        for j in range(2):
             nc.vector.memset(window[j][:], 0.0)
-        nc.gpsimd.memset(window[BLOCKS - 1][:], 0.0)
 
         rel_sq = keep.tile([P, PASSES, PACK], F32, name="rel_sq")
         inv_sq = keep.tile([P, PASSES, PACK], F32, name="inv_sq")
@@ -98,6 +96,9 @@ def tile_attend_gnce_w_clip_kernel(tc, xT, wT, y, wt, xn, xm, offs, out):
             nc.vector.tensor_copy(out=w_bf[:, :, j], in_=w_raw[j][:].indirect(offsets[:]))
         for h in range(2):
             nc.vector.tensor_copy(out=w_bf[:, slots(h), PACK - 1], in_=w_raw[PACK - 1][:].indirect(offsets_of(h)))
+        for j in range(2):
+            window.append(keep.tile([P, T], F32, name=f"window{2 + j}", tag=f"w_raw{j}"))
+            nc.gpsimd.memset(window[2 + j][:], 0.0)
         for h in range(2):
             nc.vector.quantize_mx(
                 out=w_codes[:, slots(h)].bitcast(E4M3), scales=w_scales[:, slots(h)], in_=w_bf[:, slots(h), :].rearrange("p n j -> p (n j)")

@@ -46,13 +46,15 @@ def tile_attend_gnce_w_clip_kernel(tc, xT, wT, y, wt, xn, xm, offs, out):
         x_part = [keep.tile([P, PACK, rows], F32, name=f"x_part{h}") for h, rows in enumerate((X_FIRST, PASS - X_FIRST))]
         w_raw = [keep.tile([P, T], F32, name=f"w_raw{j}", tag=f"w_raw{j}") for j in range(PACK)]
         y_raw = [keep.tile([P, PACK, N], F32, name=f"y_raw{g}") for g in range(PASSES)]
-        xm_front = [keep.tile([P, PACK, D // 2], F32, name=f"xm_front{g}") for g in range(PASSES)]
+        xm_front = [keep.tile([P, PACK, D // 2], F32, name=f"xm_front{g}", align_bytes=64) for g in range(PASSES)]
         xm_back = [keep.tile([P, PACK, D // 2], F32, name=f"xm_back{g}", align_bytes=64) for g in range(PASSES)]
         xm_raw = [[xm_front[g][:] for g in range(PASSES)], [xm_back[g][:] for g in range(PASSES)]]
         weight = keep.tile([P, PASSES, PACK], F32, name="weight", align_bytes=64)
         sq_len = keep.tile([P, PASSES, PACK], F32, name="sq_len")
 
         nc.sync.dma_start(offsets[:], offs)
+        nc.sync.dma_start(out=sq_len[:], in_=xn[0].rearrange("(g p t) o -> p g (t o)", p=P, t=PACK))
+        nc.sync.dma_start(out=weight[:], in_=wt[0].rearrange("(g p t) o -> p g (t o)", p=P, t=PACK))
         for j in range(PACK):
             nc.sync.dma_start(out=w_raw[j][:], in_=wT_planes[:, j, :])
         nc.sync.dma_start(out=x_raw[:], in_=xT_planes[:, :, 0:PASS])
@@ -61,13 +63,9 @@ def tile_attend_gnce_w_clip_kernel(tc, xT, wT, y, wt, xn, xm, offs, out):
         for g in range(PASSES):
             for h in range(2):
                 nc.sync.dma_start(out=y_raw[g][:, 2 * h : 2 * h + 2, :], in_=y_rows[g][:, 2 * h : 2 * h + 2, :])
-                if g == 0 and h == 0:
-                    nc.sync.dma_start(out=sq_len[:], in_=xn[0].rearrange("(g p t) o -> p g (t o)", p=P, t=PACK))
         for h in range(2):
             for g in range(PASSES):
                 nc.sync.dma_start(out=xm_raw[h][g], in_=xm_rows[g][:, :, h * D // 2 : (h + 1) * D // 2])
-            if h == 0:
-                nc.sync.dma_start(out=weight[:], in_=wt[0].rearrange("(g p t) o -> p g (t o)", p=P, t=PACK))
 
         zero = keep.tile([P, 1], F32, name="zero", tag="after_sigmoids")
         tiny = keep.tile([P, 1], F32, name="tiny", align_bytes=64)
@@ -140,8 +138,8 @@ def tile_attend_gnce_w_clip_kernel(tc, xT, wT, y, wt, xn, xm, offs, out):
         squares_v = [keep.tile([P, N], BF16, name=f"squares_v{h}") for h in range(2)]
         squares_s = [keep.tile([P, N], BF16, name=f"squares_s{h}") for h in range(2)]
         sum_sq = keep.tile([P, TILES], F32, name="sum_sq", tag="after_ratios", align_bytes=64)
-        factor0 = keep.tile([P, PACK], F32, name="factor0", tag="xm_front0")
-        factor1 = [keep.tile([P, PACK], F32, name=f"factor1{h}", align_bytes=64) for h in range(2)]
+        factor0 = keep.tile([P, PACK], F32, name="factor0", tag="xm_front0", align_bytes=64)
+        factor1 = [keep.tile([P, PACK], F32, name=f"factor1{h}", tag=("xm_front1", "factor11")[h], align_bytes=64) for h in range(2)]
         factor = [[factor0, factor0], factor1]
         g_scales = [keep.tile([P, N], U8, name=f"g_scales{g}", align_bytes=64) for g in range(PASSES)]
 
@@ -277,7 +275,7 @@ def tile_attend_gnce_w_clip_kernel(tc, xT, wT, y, wt, xn, xm, offs, out):
         row_factor(factor1[1], 1)
         quantize_g(1, 0)
         g_bf[0].append(g_tile(0, 1, "g_bf01"))
-        g_bf[1].append(g_tile(1, 1, "factor10"))
+        g_bf[1].append(g_tile(1, 1, "xm_front1"))
 
         g_rows = keep.tile([P, PACK, HALF], BF16, name="g_rows", tag="after_ratios", align_bytes=64)
         for t in range(PACK):

@@ -1,6 +1,7 @@
 from contextlib import ExitStack
 
 import concourse.mybir as mybir
+from concourse.masks import make_identity
 
 N, T, D, R = 512, 2048, 512, 1024
 CLIP = 277.0
@@ -53,10 +54,13 @@ def tile_attend_gnce_w_clip_kernel(tc, xT, wT, y, wt, xn, xm, offs, out):
         sq_len = keep.tile([P, PASSES, PACK], F32, name="sq_len")
 
         nc.sync.dma_start(offsets[:], offs)
-        nc.sync.dma_start(out=sq_len[:], in_=xn[0].rearrange("(g p t) o -> p g (t o)", p=P, t=PACK))
-        nc.sync.dma_start(out=weight[:], in_=wt[0].rearrange("(g p t) o -> p g (t o)", p=P, t=PACK))
+        row_wise = keep.tile([P, PASS], F32, name="row_wise")
+        nc.vector.memset(row_wise[:], 0.0)
         for j in range(PACK):
             nc.sync.dma_start(out=w_raw[j][:], in_=wT_planes[:, j, :])
+            if j == 0:
+                nc.sync.dma_start(out=row_wise[0:PASSES, :], in_=xn[0].rearrange("(g r) o -> g (r o)", g=PASSES))
+                nc.sync.dma_start(out=row_wise[PASSES : 2 * PASSES, :], in_=wt[0].rearrange("(g r) o -> g (r o)", g=PASSES))
         nc.sync.dma_start(out=x_raw[:], in_=xT_planes[:, :, 0:PASS])
         nc.sync.dma_start(out=x_part[0][:], in_=xT_planes[:, :, PASS : PASS + X_FIRST])
         nc.sync.dma_start(out=x_part[1][:], in_=xT_planes[:, :, PASS + X_FIRST : R])
@@ -66,6 +70,14 @@ def tile_attend_gnce_w_clip_kernel(tc, xT, wT, y, wt, xn, xm, offs, out):
         for h in range(2):
             for g in range(PASSES):
                 nc.sync.dma_start(out=xm_raw[h][g], in_=xm_rows[g][:, :, h * D // 2 : (h + 1) * D // 2])
+
+        identity = keep.tile([P, P], F32, name="identity")
+        make_identity(nc, identity[:])
+        turned = psum.tile([P, PACK, P], F32, name=f"bank{TILES - 1}")
+        for t in range(PACK):
+            nc.tensor.transpose(turned[:, t, :], row_wise[:].rearrange("p (m t) -> p t m", t=PACK)[:, t, :], identity[:])
+        nc.scalar.copy(out=sq_len[:], in_=turned[:, :, 0:PASSES].rearrange("p t g -> p g t"))
+        nc.scalar.copy(out=weight[:], in_=turned[:, :, PASSES : 2 * PASSES].rearrange("p t g -> p g t"))
 
         zero = keep.tile([P, 1], F32, name="zero", tag="after_sigmoids")
         tiny = keep.tile([P, 1], F32, name="tiny", align_bytes=64)

from contextlib import ExitStack

import concourse.mybir as mybir
from concourse.masks import make_identity

N, T, D, R = 512, 2048, 512, 1024
CLIP = 277.0
FLOPS = 2 * 2 * R * D * N

F32 = mybir.dt.float32
BF16 = mybir.dt.bfloat16
U32 = mybir.dt.uint32
U16 = mybir.dt.uint16
U8 = mybir.dt.uint8
E4M3 = mybir.dt.float8_e4m3fn_x4
E5M2 = mybir.dt.float8_e5m2_x4
ALU = mybir.AluOpType
ACT = mybir.ActivationFunctionType

P = 128
PACK = 4
PASS = P * PACK
PASSES = R // PASS
TILES = PASSES * PACK
BLOCKS = D // P
HALF = N // 2
BAND = 16
RUN = 4
X_FIRST = 384
TINY = 2.0**-60


def tile_attend_gnce_w_clip_kernel(tc, xT, wT, y, wt, xn, xm, offs, out):
    nc = tc.nc
    with ExitStack() as ctx:
        keep = ctx.enter_context(tc.tile_pool(name="keep", bufs=1))
        psum = ctx.enter_context(tc.psum_pool(name="psum", bufs=1))

        offsets = keep.tile([P, N // BAND], U16, name="offsets")

        xT_planes = xT[0].rearrange("(p j) r -> p j r", j=PACK)
        wT_planes = wT.rearrange("(p j) c -> p j c", j=PACK)
        y_rows = y[0].rearrange("(g p t) n -> g p t n", p=P, t=PACK)
        xm_rows = xm[0].rearrange("(g p t) d -> g p t d", p=P, t=PACK)

        x_raw = keep.tile([P, PACK, PASS], F32, name="x_raw")
        x_part = [keep.tile([P, PACK, rows], F32, name=f"x_part{h}") for h, rows in enumerate((X_FIRST, PASS - X_FIRST))]
        w_raw = [keep.tile([P, T], F32, name=f"w_raw{j}", tag=f"w_raw{j}") for j in range(PACK)]
        y_raw = [keep.tile([P, PACK, N], F32, name=f"y_raw{g}") for g in range(PASSES)]
        xm_front = [keep.tile([P, PACK, D // 2], F32, name=f"xm_front{g}", align_bytes=64) for g in range(PASSES)]
        xm_back = [keep.tile([P, PACK, D // 2], F32, name=f"xm_back{g}", align_bytes=64) for g in range(PASSES)]
        xm_raw = [[xm_front[g][:] for g in range(PASSES)], [xm_back[g][:] for g in range(PASSES)]]
        weight = keep.tile([P, PASSES, PACK], F32, name="weight", align_bytes=64)
        sq_len = keep.tile([P, PASSES, PACK], F32, name="sq_len")

        nc.sync.dma_start(offsets[:], offs)
        row_wise = keep.tile([P, PASS], F32, name="row_wise")
        nc.vector.memset(row_wise[:], 0.0)
        for j in range(PACK):
            nc.sync.dma_start(out=w_raw[j][:], in_=wT_planes[:, j, :])
            if j == 0:
                nc.sync.dma_start(out=row_wise[0:PASSES, :], in_=xn[0].rearrange("(g r) o -> g (r o)", g=PASSES))
                nc.sync.dma_start(out=row_wise[PASSES : 2 * PASSES, :], in_=wt[0].rearrange("(g r) o -> g (r o)", g=PASSES))
        nc.sync.dma_start(out=x_raw[:], in_=xT_planes[:, :, 0:PASS])
        nc.sync.dma_start(out=x_part[0][:], in_=xT_planes[:, :, PASS : PASS + X_FIRST])
        nc.sync.dma_start(out=x_part[1][:], in_=xT_planes[:, :, PASS + X_FIRST : R])
        for g in range(PASSES):
            for h in range(2):
                nc.sync.dma_start(out=y_raw[g][:, 2 * h : 2 * h + 2, :], in_=y_rows[g][:, 2 * h : 2 * h + 2, :])
        for h in range(2):
            for g in range(PASSES):
                nc.sync.dma_start(out=xm_raw[h][g], in_=xm_rows[g][:, :, h * D // 2 : (h + 1) * D // 2])

        identity = keep.tile([P, P], F32, name="identity")
        make_identity(nc, identity[:])
        turned = psum.tile([P, PACK, P], F32, name=f"bank{TILES - 1}")
        for t in range(PACK):
            nc.tensor.transpose(turned[:, t, :], row_wise[:].rearrange("p (m t) -> p t m", t=PACK)[:, t, :], identity[:])
        nc.scalar.copy(out=sq_len[:], in_=turned[:, :, 0:PASSES].rearrange("p t g -> p g t"))
        nc.scalar.copy(out=weight[:], in_=turned[:, :, PASSES : 2 * PASSES].rearrange("p t g -> p g t"))

        zero = keep.tile([P, 1], F32, name="zero", tag="after_sigmoids")
        tiny = keep.tile([P, 1], F32, name="tiny", align_bytes=64)
        nc.vector.memset(zero[:], 0.0)
        nc.vector.memset(tiny[:], TINY)
        warm = keep.tile([P, 1], F32, name="warm")
        nc.scalar.activation(warm[:], tiny[:], ACT.Sigmoid)

        window = [keep.tile([P, T], F32, name=f"window{j}") for j in range(2)]
        for j in range(2):
            nc.vector.memset(window[j][:], 0.0)

        rel_sq = keep.tile([P, PASSES, PACK], F32, name="rel_sq")
        inv_sq = keep.tile([P, PASSES, PACK], F32, name="inv_sq")

        def slots(h):
            return slice(h * HALF, (h + 1) * HALF)

        def offsets_of(h):
            return offsets[:, h * HALF // BAND : (h + 1) * HALF // BAND]

        w_bf = keep.tile([P, N, PACK], BF16, name="w_bf", align_bytes=64)
        w_codes = keep.tile([P, N], U32, name="w_codes", align_bytes=64)
        w_scales = keep.tile([P, N], U8, name="w_scales", align_bytes=64)
        for j in range(PACK - 1):
            nc.vector.tensor_copy(out=w_bf[:, :, j], in_=w_raw[j][:].indirect(offsets[:]))
        for h in range(2):
            nc.vector.tensor_copy(out=w_bf[:, slots(h), PACK - 1], in_=w_raw[PACK - 1][:].indirect(offsets_of(h)))
        for j in range(2):
            window.append(keep.tile([P, T], F32, name=f"window{2 + j}", tag=f"w_raw{j}"))
            nc.gpsimd.memset(window[2 + j][:], 0.0)
        for h in range(2):
            nc.vector.quantize_mx(
                out=w_codes[:, slots(h)].bitcast(E4M3), scales=w_scales[:, slots(h)], in_=w_bf[:, slots(h), :].rearrange("p n j -> p (n j)")
            )

        x_codes = [keep.tile([P, PASS], U32, name=f"x_codes{g}", align_bytes=64) for g in range(PASSES)]
        x_scales = [keep.tile([P, PASS], U8, name=f"x_scales{g}", align_bytes=64) for g in range(PASSES)]

        def group_x(copy, dst, src, t0, t1):
            copy(
                out=dst.rearrange("p t m j -> p m j t"),
                in_=src[:].rearrange("p j (m t) -> p m j t", t=PACK)[:, :, :, t0:t1],
            )

        def quantize_x(src, g, t0, t1):
            cols = slice(t0 * P, t1 * P)
            nc.vector.quantize_mx(
                out=x_codes[g][:, cols].bitcast(E4M3), scales=x_scales[g][:, cols],
                in_=src.rearrange("p t m j -> p (t m j)"),
            )

        split = X_FIRST // PACK
        x_lo = keep.tile([P, 2, P, PACK], BF16, name="x_lo", align_bytes=64)
        x_hi = keep.tile([P, 2, P, PACK], BF16, name="x_hi", align_bytes=64)
        group_x(nc.vector.tensor_copy, x_lo[:], x_raw, 0, 2)
        group_x(nc.scalar.copy, x_hi[:], x_raw, 2, 4)
        quantize_x(x_lo[:, 0:1], 0, 0, 1)
        quantize_x(x_lo[:, 1:2], 0, 1, 2)
        x_second = keep.tile([P, PACK, P, PACK], BF16, name="x_second", align_bytes=64)
        group_x(nc.vector.tensor_copy, x_second[:, :, 0:split, :], x_part[0], 0, PACK)
        quantize_x(x_hi[:], 0, 2, 4)
        group_x(nc.vector.tensor_copy, x_second[:, :, split:P, :], x_part[1], 0, PACK)
        quantize_x(x_second[:, 0:1], 1, 0, 1)
        quantize_x(x_second[:, 1:2], 1, 1, 2)
        quantize_x(x_second[:, 2:4], 1, 2, 4)

        prob = [keep.tile([P, PACK, N], F32, name=f"prob{g}") for g in range(PASSES)]
        q = [keep.tile([P, PACK, N], F32, name=f"q{g}", align_bytes=64) for g in range(PASSES)]
        squares_v = [keep.tile([P, N], BF16, name=f"squares_v{h}") for h in range(2)]
        squares_s = [keep.tile([P, N], BF16, name=f"squares_s{h}") for h in range(2)]
        sum_sq = keep.tile([P, TILES], F32, name="sum_sq", tag="after_ratios", align_bytes=64)
        factor0 = keep.tile([P, PACK], F32, name="factor0", tag="xm_front0", align_bytes=64)
        factor1 = [keep.tile([P, PACK], F32, name=f"factor1{h}", tag=("xm_front1", "factor11")[h], align_bytes=64) for h in range(2)]
        factor = [[factor0, factor0], factor1]
        g_scales = [keep.tile([P, N], U8, name=f"g_scales{g}", align_bytes=64) for g in range(PASSES)]

        for u in range(TILES):
            g, t = divmod(u, PACK)
            scores = psum.tile([P, N], F32, name=f"bank{u}")
            cols = slice(t * P, (t + 1) * P)
            nc.tensor.matmul_mx(
                out=scores[:], lhsT=x_codes[g][:, cols].bitcast(E4M3), lhsT_scale=x_scales[g][:, cols],
                rhs=w_codes[:].bitcast(E4M3), rhs_scale=w_scales[:], start=True, stop=True,
            )
            nc.scalar.activation(prob[g][:, t, :], scores[:], ACT.Sigmoid, bias=zero[:])

        rel_len = keep.tile([P, TILES], F32, name="rel_len", tag="after_sigmoids")
        ratio = [keep.tile([P, PACK], F32, name=f"ratio{g}", align_bytes=64) for g in range(PASSES)]

        def residual_pair(u):
            g, t = divmod(u, PACK)
            rows = slice(t, t + 2)
            nc.vector.tensor_tensor(q[g][:, rows, :], prob[g][:, rows, :], y_raw[g][:, rows, :], ALU.subtract)

        def square_on_vector(u):
            g, t = divmod(u, PACK)
            nc.vector.scalar_tensor_tensor(
                squares_v[u % 2][:], q[g][:, t, :], rel_sq[:, g, t : t + 1], q[g][:, t, :], ALU.mult, ALU.mult, accum_out=sum_sq[:, u : u + 1]
            )

        def square_on_scalar(u):
            g, t = divmod(u, PACK)
            nc.scalar.activation(squares_s[u % 2][:], q[g][:, t, :], ACT.Square, scale=rel_len[:, u : u + 1], accum_out=sum_sq[:, u : u + 1])

        def row_ratio(g):
            cols = slice(g * PACK, (g + 1) * PACK)
            nc.scalar.activation(ratio[g][:], sum_sq[:, cols], ACT.Abs_reciprocal_sqrt, bias=tiny[:])

        def row_factor(dst, g):
            nc.vector.scalar_tensor_tensor(dst[:], ratio[g][:], 1.0, weight[:, g, :], ALU.min, ALU.mult)

        residual_pair(0)
        nc.vector.tensor_scalar(rel_sq[:], sq_len[:], 1.0 / (CLIP * CLIP), TINY, ALU.mult, ALU.add)
        residual_pair(2)
        nc.vector.reciprocal(inv_sq[:], rel_sq[:])
        nc.scalar.activation(rel_len[:], inv_sq[:].rearrange("p g t -> p (g t)"), ACT.Abs_reciprocal_sqrt)
        square_on_vector(0)
        residual_pair(4)
        square_on_vector(1)
        residual_pair(6)
        for u in range(2, PACK):
            square_on_scalar(u)
        row_ratio(0)
        for u in range(PACK, TILES):
            square_on_scalar(u)
        row_ratio(1)

        xm_codes = [keep.tile([P, PASSES, P], U32, name=f"xm_codes{j}", align_bytes=64) for j in range(BLOCKS)]
        xm_scales = [keep.tile([P, PASSES, P], U8, name=f"xm_scales{j}", align_bytes=64) for j in range(BLOCKS)]

        def xm_tile(j, tag):
            return keep.tile([P, PASSES, P, PACK], BF16, name=f"xm_bf{j}", tag=tag, align_bytes=64)

        def group_xm(copy, dst, j, g):
            copy(
                out=dst[:, g].rearrange("p (c i) t -> p c t i", i=RUN),
                in_=xm_raw[j // 2][g][:, :, (j % 2) * P : (j % 2 + 1) * P].rearrange("p t (c i) -> p c t i", i=RUN),
            )

        def quantize_xm(src, j):
            nc.vector.quantize_mx(
                out=xm_codes[j][:].rearrange("p g d -> p (g d)").bitcast(E4M3),
                scales=xm_scales[j][:].rearrange("p g d -> p (g d)"),
                in_=src[:].rearrange("p g d t -> p (g d t)"),
            )

        def g_tile(g, h, tag):
            return keep.tile([P, HALF, PACK], BF16, name=f"g_bf{g}{h}", tag=tag, align_bytes=64)

        g_bf = [[g_tile(g, 0, f"g_bf{g}0")] for g in range(PASSES)]

        def gradient(g, h):
            nc.vector.tensor_tensor(
                g_bf[g][h][:].rearrange("p (c i) t -> p c t i", i=RUN),
                q[g][:, :, slots(h)].rearrange("p t (c i) -> p c t i", i=RUN),
                factor[g][h][:].unsqueeze(1).unsqueeze(3).to_broadcast([P, HALF // RUN, PACK, RUN]),
                ALU.mult,
            )

        def quantize_g(g, h):
            nc.vector.quantize_mx(
                out=g_codes[g][:, slots(h)].bitcast(E5M2), scales=g_scales[g][:, slots(h)], in_=g_bf[g][h][:].rearrange("p n t -> p (n t)")
            )

        def product(j, h, passes=(1, 0)):
            sums = psum.tile([P, HALF], F32, name=f"bank{2 * j + h}")
            for g in passes:
                nc.tensor.matmul_mx(
                    out=sums[:], lhsT=xm_codes[j][:, g, :].bitcast(E4M3), lhsT_scale=xm_scales[j][:, g, :],
                    rhs=g_codes[g][:, slots(h)].bitcast(E5M2), rhs_scale=g_scales[g][:, slots(h)], start=(g == passes[0]), stop=(g == passes[-1]),
                )
            return sums[:]

        def to_sbuf(copy, j, h, passes=(1, 0)):
            dense = keep.tile([P, HALF], F32, name=f"dense{j}{h}", align_bytes=64)
            copy(out=dense[:], in_=product(j, h, passes))
            return dense[:]

        def scatter_early(j, dense):
            nc.scalar.activation(window[j][:].indirect(offsets_of(0)), dense, ACT.Copy)

        def scatter_late(j, dense):
            nc.vector.tensor_copy(out=window[j][:].indirect(offsets_of(1)), in_=dense)
            nc.sync.dma_start(out=out[j * P : (j + 1) * P, :], in_=window[j][:])

        def group_xm_on_gpsimd(dst, j, g):
            nc.gpsimd.tensor_scalar(
                dst[:, g].rearrange("p (c i) t -> p c t i", i=RUN),
                xm_raw[j // 2][g][:, :, (j % 2) * P : (j % 2 + 1) * P].rearrange("p t (c i) -> p c t i", i=RUN),
                1.0, 0.0, ALU.mult, ALU.add,
            )

        xm_bf = [xm_tile(j, f"xm_bf{j}") for j in range(2)]
        group_xm(nc.vector.tensor_copy, xm_bf[0], 0, 0)
        group_xm(nc.vector.tensor_copy, xm_bf[1], 1, 0)
        row_factor(factor0, 0)
        group_xm(nc.vector.tensor_copy, xm_bf[0], 0, 1)
        gradient(0, 0)
        quantize_xm(xm_bf[0], 0)
        group_xm(nc.vector.tensor_copy, xm_bf[1], 1, 1)
        quantize_xm(xm_bf[1], 1)
        row_factor(factor1[0], 1)
        g_codes = [keep.tile([P, N], U32, name=f"g_codes{g}", tag=("tiny", "g_codes1")[g], align_bytes=64) for g in range(PASSES)]
        quantize_g(0, 0)
        gradient(1, 0)
        row_factor(factor1[1], 1)
        quantize_g(1, 0)
        g_bf[0].append(g_tile(0, 1, "g_bf01"))
        g_bf[1].append(g_tile(1, 1, "xm_front1"))

        g_rows = keep.tile([P, PACK, HALF], BF16, name="g_rows", tag="after_ratios", align_bytes=64)
        for t in range(PACK):
            nc.scalar.activation(g_rows[:, t, :], q[0][:, t, slots(1)], ACT.Copy, scale=factor0[:, t : t + 1])
        nc.scalar.copy(
            out=g_bf[0][1][:].rearrange("p (c i) t -> p c t i", i=RUN),
            in_=g_rows[:].rearrange("p t (c i) -> p c t i", i=RUN),
        )

        early0 = to_sbuf(nc.scalar.copy, 0, 0, (0, 1))
        early1 = to_sbuf(nc.scalar.copy, 1, 0, (0, 1))
        scatter_early(0, early0)
        scatter_early(1, early1)
        gradient(1, 1)
        quantize_g(0, 1)
        quantize_g(1, 1)
        xm_bf.append(xm_tile(2, "g_bf01"))
        group_xm(nc.vector.tensor_copy, xm_bf[2], 2, 0)
        group_xm(nc.vector.tensor_copy, xm_bf[2], 2, 1)
        late0 = to_sbuf(nc.vector.tensor_copy, 0, 1, (0, 1))
        quantize_xm(xm_bf[2], 2)
        scatter_late(0, late0)
        xm_bf.append(xm_tile(3, "g_bf01"))
        for g in range(PASSES):
            group_xm_on_gpsimd(xm_bf[3], 3, g)
        quantize_xm(xm_bf[3], 3)
        held = keep.tile([P, 2, HALF], F32, name="held", tag="xm_back1", align_bytes=64)
        late1, early2 = held[:, 0, :], held[:, 1, :]
        nc.scalar.copy(out=late1, in_=product(1, 1))
        nc.scalar.copy(out=early2, in_=product(2, 0))
        scatter_early(2, early2)
        scatter_late(1, late1)
        late2 = to_sbuf(nc.vector.tensor_copy, 2, 1)
        late3 = to_sbuf(nc.vector.tensor_copy, 3, 1)
        scatter_late(2, late2)
        early3 = to_sbuf(nc.scalar.copy, 3, 0)
        scatter_early(3, early3)
        scatter_late(3, late3)
